import numpy as np, ml_dtypes
CORES = [9,25,41,57]
N = 4
BF = ml_dtypes.bfloat16
def gentries(a):
    return np.ascontiguousarray(a.reshape(8, 16, -1).transpose(0, 2, 1)).reshape(8, -1)
def gtable(e):
    e = np.asarray(e); return np.ascontiguousarray(e.reshape(8, -1, 16).transpose(0, 2, 1)).reshape(128, -1).astype(np.int32)
W0, B, LN, RO, SP, CAP = 3328, 256, 2048, 3, 3, 512
W = W0 + RO * B
def parts(rng):
    scale = np.array([0.5, 1, 1.5, 2, 3, 4, 6, 8])[np.argsort(rng.random((N, 8)), axis=1)][:, :, None, None]; dens = 0.1 + 0.6 * rng.random((N, 8, 1, W0))
    cnt = np.where(rng.random((N, 8, 16, W0)) < dens, np.minimum(15, 1 + (scale * rng.standard_exponential((N, 8, 16, W0))).astype(np.int64)), 0)
    hot = rng.integers(0, W0, (N, 8, 64))
    def some(n, share):
        return np.where(rng.random((N, 8, n)) < share, np.take_along_axis(hot, rng.integers(0, 64, (N, 8, n)), 2), rng.integers(0, W0, (N, 8, n)))
    ptr = some(16 * W0, 0.4).reshape(N, 8, 16, W0); suf = (np.arange(W0) * rng.random((N, 8, W0))).astype(np.int64)
    return cnt, ptr, suf, rng.integers(0, W0, (N, 8, W0)), some(LN, 0.3), rng.integers(0, 256, (N, 8, RO * SP, LN))
def levels(rng, cnt, suf, v, g):
    x = np.arange(W0); b = np.where(x <= 16, 3, np.where(x <= 32, 2, np.where(x <= 48, 1, 0)))
    cnt[:, g] = np.where((np.arange(16) >> 2)[:, None] == b, rng.integers(1, 16, (N, 16, W0)), 0)
    suf[:, g] = rng.integers(1, 17, (N, W0)) + 16 * np.maximum(2 - b, 0)
    v[:, g, :SP - 1, :B] = rng.integers(240, 256, (N, SP - 1, B)); v[:, g, SP - 1, :B] = rng.integers(0, 128, (N, B))
def clones(rng, cnt, ptr, suf, lnk, cx, v, g):
    o = 1 + np.argsort(rng.random((N, W0 - 1)), axis=1); x = o[:, :B]; b = o[:, B:2 * B]; u = o[:, 2 * B:3 * B]
    qi = np.arange(N)[:, None]; z = rng.integers(1, 16, (N, B)); ct = cnt[:, g]; pt = ptr[:, g]
    for y in (x, u):
        ct[qi, :, y] = 0; ct[qi, 0, y] = 1; pt[qi, 0, y] = y
    ct[qi, :, b] = 0; ct[qi, z, b] = 1; pt[qi, z, b] = u
    suf[qi, g, x] = b; suf[qi, g, u] = x; lnk[qi, g, u] = np.maximum(lnk[qi, g, u], 1); cx[:, g, :B] = x
    v[:, g, :, :B] = rng.integers(0, 64, (N, RO * SP, B))
    for s in (SP - 2, 2 * SP - 2): v[:, g, s, :B] = rng.integers(128, 256, (N, B))
    if (RO - 2) * SP > 2:
        v[:, g, RO * SP - 2, :B] = rng.integers(64, 128, (N, B)); v[:, g, RO * SP - 1, :B] = rng.integers(128, 256, (N, B))
def kept(rng, cnt, ptr, suf, cx, v, g):
    o = 1 + np.argsort(rng.random((N, W0 - 1)), axis=1)[:, :(SP + 1) * B]; h = o[:, :SP * B]; b = o[:, SP * B:]
    qi = np.arange(N)[:, None]; z = rng.integers(1, 16, (N, B)); ct = cnt[:, g]; pt = ptr[:, g]
    ct[qi, :, h] = 0; ct[qi, 0, h] = 1; pt[qi, 0, h] = h; suf[qi, g, h] = o[:, B:]
    ct[qi, :, b] = 0; ct[qi, z, b] = 1; cx[:, g] = o[:, np.arange(LN) % B]
    v[:, g, :SP] = rng.integers(0, 128, (N, SP, LN)); v[1::2, g, SP - 1, :B] = rng.integers(128, 256, (N // 2, B))
    v[:, g, 2 * SP - 1, :B] = rng.integers(0, 128, (N, B))
def filled(rng, cnt, ptr, suf, lnk, cx, v, g):
    o = 1 + np.argsort(rng.random((N, W0 - 1)), axis=1)[:, :(2 * SP + 1) * B]; x = o[:, :B]; y = o[:, B:]; b1 = o[:, SP * B:(SP + 1) * B]; b2 = o[:, 2 * SP * B:]
    qi = np.arange(N)[:, None]; ct = cnt[:, g]; pt = ptr[:, g]
    ct[qi, :, o] = 0; ct[qi, 0, o] = 1; pt[qi, 0, o] = o
    for b, lo in ((b1, 1), (b2, 8)):
        ct[qi, 0, b] = 0; ct[qi, rng.integers(lo, lo + 7, (N, B)), b] = 1
    suf[qi, g, x] = np.roll(x, -1, axis=1); suf[qi, g, y[:, :-B]] = y[:, B:]; lnk[qi, g, x] = np.roll(y[:, :B], -1, axis=0)
    cx[:, g] = x[:, np.arange(LN) % B]
    v[:, g, :2 * SP] = rng.integers(0, 128, (N, 2 * SP, LN)); v[:, g, SP - 1, :B] = rng.integers(128, 256, (N, B))
    q4 = np.arange(N) % 4; v[:, g, 2 * SP - 1, :B // 2] += 128 * ((q4 == 1) | (q4 == 2))[:, None]
    if RO > 2: v[:, g, 3 * SP - 1, :B // 2] = rng.integers(0, 128, (N, B // 2))
def pack(cnt, ptr, suf, lnk, cx, v):
    return {"tab": np.ascontiguousarray((16 * ptr + cnt).reshape(N, 128, W0)).astype(np.int32), "suf": suf.astype(np.int32), "lnk": lnk.astype(np.int32),
            "cx": np.stack([gtable(a) for a in cx]), "vv": v.reshape(N, 8, RO * SP * LN).astype(np.float32).astype(BF)}
def setup_inputs(rng):
    return pack(*parts(rng))
def setup_inputs_room(rng):
    cnt, ptr, suf, lnk, cx, v = parts(rng)
    cnt = np.where(np.arange(16)[:, None] == rng.integers(0, 16, (N, 8, 1, W0)), np.maximum(cnt, 1), cnt); ptr = np.maximum(ptr, 1); cx = np.maximum(cx, 1)
    v[:, :, :SP - 1] = rng.integers(0, 128, (N, 8, SP - 1, LN)); opts = (0, 1, CAP - 1, CAP, CAP + 1, LN)
    for q in range(N):
        o = rng.permutation(6)
        for g in range(6):
            m = opts[g] if q == 0 else opts[5 - g] if q == 1 else opts[int(o[g])]
            v[q, g, SP - 1] = np.where(rng.permutation(LN) < m, rng.integers(240, 256, LN), rng.integers(0, 128, LN))
    for g in (6, 7):
        levels(rng, cnt, suf, v, g)
        for q in range(N): cx[q, g, :B] = 64 + rng.permutation(W0 - 64)[:B]
    return pack(cnt, ptr, suf, lnk, cx, v)
def setup_inputs_ties(rng):
    cnt, ptr, suf, lnk, cx, v = parts(rng)
    rows = np.array([4, 1, 2, 8, 1, 0, 16, 4, 8, 8, 16]); vals = np.array([3, 1, 1, 1, 15, 0, 15, 1, 3, 7, 3]); k = rng.integers(0, 11, (N, 8, W0))
    order = np.argsort(rng.random((N, 8, W0, 16)), axis=-1)
    cnt = np.where(order < rows[k][..., None], vals[k][..., None], 0).transpose(0, 1, 3, 2)
    v = np.where(rng.random(v.shape) < 0.6, 16 * rng.integers(0, 17, v.shape), 15 * rng.integers(0, 18, v.shape)) + np.where(rng.random(v.shape) < 0.6, 0, rng.integers(-1, 2, v.shape))
    return pack(cnt, ptr, suf, lnk, cx, np.minimum(np.maximum(v, 0), 255))
def setup_inputs_alike(rng):
    cnt, ptr, suf, lnk, cx, v = parts(rng); few = rng.integers(1, W0, (N, 8, 6))
    def some(n, m):
        return np.take_along_axis(few, rng.integers(0, m, (N, 8, n)), 2)
    ptr = some(16 * W0, 6).reshape(N, 8, 16, W0); suf = np.where(rng.random((N, 8, W0)) < 0.5, some(W0, 6), suf); lnk = np.where(rng.random((N, 8, W0)) < 0.5, some(W0, 6), lnk); cx = some(LN, 4)
    levels(rng, cnt, suf, v, 3); cx[:, 3, :B] = rng.choice(np.array([70, W0 - 1]), (N, B))
    cx[:, 5] = cx[:, 5, :1]; v[:, 5] = v[:, 5, :, :1]
    filled(rng, cnt, ptr, suf, lnk, cx, v, 2); kept(rng, cnt, ptr, suf, cx, v, 6); clones(rng, cnt, ptr, suf, lnk, cx, v, 7)
    return pack(cnt, ptr, suf, lnk, cx, v)
def setup_inputs_ends(rng):
    cnt, ptr, suf, lnk, cx, v = parts(rng); e = np.array([0, 1, W0 - 1])
    ptr = np.where(rng.random(ptr.shape) < 0.3, rng.choice(e, ptr.shape), ptr); lnk = np.where(rng.random(lnk.shape) < 0.5, rng.choice(e, lnk.shape), lnk); cx = np.where(rng.random(cx.shape) < 0.5, rng.choice(e, cx.shape), cx)
    suf[:, 1::2] = np.where(rng.random((N, 4, W0)) < 0.3, np.arange(W0), rng.integers(0, W0, (N, 4, W0))); suf[:, 2] = 0; suf[:, 4] = 0; suf[:, 5] = 0
    cnt[:, 4, :, 0] = 0; cnt[:, 5, :, 0] = 15; cnt[:, 6] = 15 * (cnt[:, 6] > 0); cnt[:, 7, :, W0 - 1] = 0; cnt[:, 0, :, W0 - 1] = 15
    v = np.where(rng.random(v.shape) < 0.7, rng.choice(np.array([0, 1, 127, 128, 239, 240, 254, 255]), v.shape), v)
    return pack(cnt, ptr, suf, lnk, cx, v)
def setup_inputs_spread(rng):
    def low(*shape):
        return np.minimum((W0 * rng.random(shape) ** rng.integers(1, 5, shape[:2] + (1,) * (len(shape) - 2))).astype(np.int64), W0 - 1)
    cnt = np.where(rng.random((N, 8, 16, W0)) < rng.random((N, 8, 1, W0)) ** 2, np.minimum(np.exp2(4 * rng.random((N, 8, 16, W0)) * rng.random((N, 8, 1, W0)) ** 0.5).astype(np.int64), 15), 0)
    v = np.minimum((256 * rng.random((N, 8, RO * SP, LN)) ** 3).astype(np.int64), 255)
    return pack(cnt, low(N, 8, 16, W0), low(N, 8, W0), W0 - 1 - low(N, 8, W0), low(N, 8, LN), np.where(rng.random(v.shape) < 0.5, v, 255 - v))
def check_inputs(d):
    bad = []
    for k, hi in (("tab", 16 * W0 - 1), ("suf", W0 - 1), ("lnk", W0 - 1), ("cx", W0 - 1)):
        if np.min(d[k]) < 0 or np.max(d[k]) > hi: bad.append("range of " + k)
    v = np.asarray(d["vv"]).astype(np.float32)
    if not np.all((v >= 0) & (v <= 255) & (v == np.floor(v))): bad.append("range of vv")
    return bad
def reference(tab, suf, lnk, cx, vv):
    k = tab.astype(np.int32).reshape(N, 8, 16, W0)
    C = np.zeros((N, 8, 16, W), np.int32); S = np.zeros((N, 8, 16, W), np.int32); C[..., :W0] = k & 15; S[..., :W0] = k >> 4
    F = np.zeros((N, 8, W), np.int32); L = np.zeros((N, 8, W), np.int32); F[..., :W0] = suf; L[..., :W0] = lnk
    v = vv.astype(np.float32).astype(np.int32).reshape(N, 8, RO, SP, 1, LN)
    c = np.stack([gentries(a) for a in cx]).astype(np.int32); e = np.zeros((N, 8, 16, LN), np.int32); f = np.full((N, 8, LN), -1, np.int32)
    qi = np.arange(N)[:, None, None]; gi = np.arange(8)[None, :, None]
    for t in range(RO):
        for s in range(SP):
            cc = np.take_along_axis(C, c[:, :, None, :], 3)
            n = cc * (1 - e); P = np.add.accumulate(n, axis=2, dtype=np.int32); E = np.add.reduce((n > 0).astype(np.int32), axis=2)
            z = np.add.reduce((256 * P <= v[:, :, t, s] * (P[:, :, 15] + E)[:, :, None, :]).astype(np.int32), axis=2)
            z = np.where(c == 0, np.minimum(z, 15), z); esc = z == 16
            d, fb = c, f
            f = np.where(esc, np.where(fb < 0, d, fb), -1)
            e = np.where(esc[:, :, None, :], np.maximum(e, (cc > 0).astype(np.int32)), 0)
            c = np.where(esc, F[qi, gi, d], S[qi, gi, np.minimum(z, 15), d])
        for q in range(N):
            for g in range(8):
                j = np.nonzero(~esc[q, g, :B] & (fb[q, g, :B] >= 0))[0]
                a = j[np.unique(fb[q, g, j], return_index=True)[1]]
                w = W0 + B * t + a; to = c[q, g, a]
                cw = (C[q, g][:, to] + 1) >> 1; sw = S[q, g][:, to]
                C[q, g][:, w] = cw; S[q, g][:, w] = sw; F[q, g, w] = to; L[q, g, w] = L[q, g, to]
                C[q, g, z[q, g, a], fb[q, g, a]] = 1; S[q, g, z[q, g, a], fb[q, g, a]] = w
                b = j[np.unique(d[q, g, j], return_index=True)[1]]
                C[q, g, z[q, g, b], d[q, g, b]] = np.minimum(15, C[q, g, z[q, g, b], d[q, g, b]] + 1)
        slot = esc & (np.add.accumulate(esc.astype(np.int32), axis=2) <= CAP)
        c2 = np.array(c); e2 = np.array(e); f2 = np.array(f)
        for r in range(N):
            q = (r - 1) % N
            for g in range(8):
                a = np.nonzero(slot[q, g])[0]; b = np.nonzero(slot[r, g])[0]; m = min(len(a), len(b)); a = a[:m]; b = b[:m]
                c2[r, g, b] = L[q, g, c[q, g, a]]; e2[r, g][:, b] = e[q, g][:, a]; f2[r, g, b] = -1
        c, e, f = c2, e2, f2
    return {"yn": C.reshape(N, 128, W).astype(np.float32).astype(BF), "yc": np.stack([gtable(a) for a in c]).astype(np.float32)}

@@ -1,0 +1,605 @@
+from concourse.mybir import AluOpType as O, ActivationFunctionType as AF
+
+W0, B, LN, RO, SP, CAP = 3328, 256, 2048, 3, 3, 512
+TW = 4352
+D = 2.0 ** -14
+MAG = 1.5 * 2.0 ** 27
+NCH, CH = 4, 832
+
+
+def _sb(dtype, **shapes):
+    return {k: ("sbuf", [128] + ([n] if n > 0 else [16, -n]), dtype) for k, n in shapes.items()}
+
+
+SCRATCH = {}
+SCRATCH.update(_sb("int32", tk=W0, ti0=CH // 2, ti1=CH // 2, ip=128, im=128, pg=128, mg=128, pm=128, mm=128, io3=-16, sfi=208, lki=208, lkj=208,
+                   cxi=128, rr=256))
+SCRATCH.update(_sb("float32", TC=TW, TS=2 * TW, TL=4096, vl=384, Sg=LN, MK=640, sm=176, RS=16, RSn=16, dif=128, mrow=512, krow=128,
+                   mi=32, mL=32, Dm=32, wr0=256, wr1=256, wr2=256, zz=128, cols=16, sff=208, lhf=208, llf=208, cf=128, nz=128, c2f=128,
+                   xx=128, es=128, x2=128, o1=32, o2=32, uf=256, nu=256, u1=256, uw=256, r2=256, aC=256, aS=256,
+                   inc=128, X=128, ha=128, hb=128, hc=128, Yl=128, lnf=32, tot=8, lT0=8, lT1=8, lT2=8, vd=32, so=32, mvv=128, nmv=128))
+SCRATCH.update(_sb("bfloat16", vvr=SP * LN, G=LN, cm=LN, mk=LN + CAP, H=LN + CAP, EQ0=-256, EQ1=-256, BC=-128, yb=4096, ES=-128, Dn=-128, D15=-128,
+                   EV=-128, EW=-128, EH=-128, BO=128, PRE=128, ZT=128, NI=128, DL=128, BN=128, B15=128, cc=640, tri=-16, eb=128, cr=256, fr=512,
+                   OH=512, MS=512, Lg=512, lM0=512, lM1=512, lL0=512, lL1=512, lL2=512))
+SCRATCH.update(_sb("float16", q=LN, Y=LN, th=128, mmB=128, mm1=128, mmV=128, mv1=128, kh=64, R=512, off=128, kr=512, CG=512))
+SCRATCH.update(_sb("uint16", cu=128, cu2=128, ou=32, ofu=8, klu=32, cmu=32, lnu=32, sou=32))
+SCRATCH.update({k: ("psum", [128, n], "float32") for k, n in (("PX0", 1024), ("PX1", 1024), ("PU", 1024), ("PL0", 512), ("PL1", 512))})
+DMAS = ["d%d" % i for i in range(24)]
+REM = [a + str(t) for t in range(RO) for a in ("aT", "aM", "aL", "nT", "nM", "nL") if not (t == RO - 1 and a[1] == "M")]
+SEMAPHORES = ["sV", "sA", "sP", "sG"] + DMAS + REM
+BANKS = {"PX00", "PX01", "PX10", "PX11", "PU0", "PU1", "PL0", "PL1"}
+
+
+def rank_program(g, core, T, topo):
+    rank = T.rank_of(core)
+    if rank is None:
+        return
+    V, A, P, S = g.vector, g.scalar, g.tensor, g.sync
+    eng = {"V": V, "A": A, "P": P, "S": S, "G": g}
+    seen = {k: {} for k in eng}
+    cnt = {k: 0 for k in "VAPG"}
+    wr, rd, left = {}, {}, {}
+    ndma = [0]
+
+    def run(qn, fn, r, w, acc=False, sem=None, remote=False, n=1):
+        r, w = r.split(), w.split()
+        own = "s" + qn
+        need = {}
+
+        def want(toks, skip):
+            for s, v in toks.items():
+                if not (skip and s == own):
+                    need[s] = max(need.get(s, 0), v)
+        for k in r:
+            want(wr.get(k, {}), False)
+            if k in BANKS:
+                want(rd.get(k, {}), True)
+        for k in w:
+            want(wr.get(k, {}), acc)
+            want(rd.get(k, {}), sem is None)
+        for s in sorted(need):
+            if seen[qn].get(s, 0) < need[s]:
+                eng[qn].wait_ge(T.sem[s], need[s])
+                seen[qn][s] = need[s]
+        inst = fn()
+        if sem is None:
+            cnt[qn] += 1
+            s, v = own, cnt[qn]
+        else:
+            s, v = sem, n
+        if not remote:
+            inst.then_inc(T.sem[s], n)
+        left[s] = v
+        for k in r:
+            rd.setdefault(k, {})[s] = v
+        for k in w:
+            wr[k] = {s: v}
+            rd[k] = {}
+
+    def v_(fn, r, w): run("V", fn, r, w)
+    def a_(fn, r, w): run("A", fn, r, w)
+    def p_(fn, r, w): run("P", fn, r, w, acc=True)
+    def g_(fn, r, w): run("G", fn, r, w)
+
+    def dma(qn, out, in_, r, w):
+        s = DMAS[ndma[0]]
+        ndma[0] += 1
+        run(qn, lambda: eng[qn].dma_start(out, in_), r, w, sem=s, n=16)
+
+    def ts(out, in0, s1, op0, r, w, s2=None, op1=None):
+        if op1 is None:
+            v_(lambda: V.tensor_scalar(out, in0, s1, None, op0), r, w)
+        else:
+            v_(lambda: V.tensor_scalar(out, in0, s1, s2, op0, op1), r, w)
+
+    def tt(out, in0, in1, op, r, w):
+        v_(lambda: V.tensor_tensor(out, in0, in1, op), r, w)
+
+    def cp(out, in_, r, w):
+        v_(lambda: V.tensor_copy(out, in_), r, w)
+
+    def act(out, in_, func, r, w, bias=0.0, scale=1.0):
+        a_(lambda: A.activation(out, in_, func, bias=bias, scale=scale), r, w)
+
+    def listsum(out, fam, src, lo, hi, r, w, start=True, stop=True):
+        def f():
+            for i in range(16):
+                x = P.matmul(out, fam[:, i, :], src[:, lo + i:hi:16], start and i == 0, stop and i == 15)
+            return x
+        p_(f, r, w)
+
+    def spread(out, base, n, fam, src, lo, r, w, start=True):
+        def f():
+            for i in range(16):
+                x = P.matmul(out[:, base + i:base + n:16], fam[:, i, :], src[:, lo:lo + n // 16], start, start or i == 15)
+            return x
+        p_(f, r, w)
+
+    nxt = T.cores[(rank + 1) % len(T.cores)]
+    rid, pid, _se = topo.addr(nxt)
+    emask = topo.mask(core, nxt)
+    ne = len(topo.engines(core, nxt))
+
+    def send(dst, src, name, t, r):
+        s, rs = "n%s%d" % (name, t), "a%s%d" % (name, t)
+        run("G", lambda: g.remote_dma(dst, src, T.sem[rs], T.sem[s], pid, rid, emask), r, "", sem=s, remote=True, n=ne)
+
+    for t in range(RO):
+        for a in "TML":
+            if t < RO - 1 or a != "M":
+                wr["l%s%d" % (a, t)] = {"a%s%d" % (a, t): ne}
+                left["a%s%d" % (a, t)] = ne
+
+    def marks(t, s):
+        return not (t == RO - 1 and s == SP - 1)
+
+    def sm(k):
+        return T.sm[:, 16 * k:16 * k + 16]
+
+    def cc(k):
+        return T.cc[:, 128 * k:128 * k + 128]
+
+    def loadv(qn, t):
+        dma(qn, T.vvr[0:8, :], T.vv[:, SP * LN * t:SP * LN * (t + 1)], "", "vvr")
+
+    def vlist(t):
+        for s in range(SP):
+            def f(s=s):
+                for i in range(16):
+                    x = P.matmul(T.PU[:, 512 + 128 * s:640 + 128 * s], T.EV[0:8, i, :], T.vvr[0:8, LN * s + i:LN * (s + 1):16], i == 0, i == 15)
+                return x
+            p_(f, "EV vvr", "PU1")
+        act(T.vl[:], T.PU[:, 512:512 + 128 * SP], AF.Copy, "PU1", "vl", scale=1.0 / 256)
+
+    loadv("A", 0)
+    for k in range(NCH):
+        dma("S", T.tk[:, k * CH:(k + 1) * CH], T.tab[:, k * CH:(k + 1) * CH], "", "tk%d" % k)
+        if k == 0:
+            dma("S", T.cxi[:], T.cx[:, :], "", "cxi")
+            dma("S", T.sfi[:], T.suf[:, :], "", "sfi")
+    dma("S", T.lki[:], T.lnk[:, :], "", "lki")
+
+    def iota(out, pat, base, cm, w, small=True):
+        if small:
+            g_(lambda: g.iota(out, pat, base, cm, allow_small_or_imprecise_dtypes=True), "", w)
+        else:
+            g_(lambda: g.iota(out, pat, base, cm), "", w)
+    iota(T.ip[:], [[0, 128]], 0, 1, "ip", False)
+    iota(T.im[:], [[1, 128]], 0, 0, "im", False)
+    iota(T.TS[:, TW:TW + 2176], [[0, 2176]], 0, 0, "TSF0")
+    iota(T.TS[:, TW + 2176:2 * TW], [[0, 2176]], 0, 0, "TSF1")
+    iota(T.TC[:, W0:TW], [[0, TW - W0]], 0, 0, "TCz")
+    iota(T.TS[:, W0:TW], [[0, TW - W0]], 0, 0, "TSz")
+    iota(T.mi[:], [[16, 32]], 129, 0, "mi")
+    iota(T.io3[:], [[0, 16], [1, 16]], 0, 0, "io3", False)
+    iota(T.krow[:], [[1, 128]], 0, 0, "krow")
+    iota(T.TL[:], [[0, 4096]], 0, 0, "TL")
+    iota(T.mrow[:], [[1, 512]], 129, 0, "mrow")
+    for t in range(RO):
+        iota(T["wr%d" % t][:], [[1, 256]], W0 + B * t - 2048, 0, "wr%d" % t)
+    iota(T.H[:, LN:], [[0, CAP]], 0, 0, "H")
+
+    ts(T.pg[:], T.ip[:], 4, O.arith_shift_right, "ip", "pg")
+    ts(T.mg[:], T.im[:], 4, O.arith_shift_right, "im", "mg")
+    ts(T.pm[:], T.ip[:], 15, O.bitwise_and, "ip", "pm")
+    ts(T.mm[:], T.im[:], 15, O.bitwise_and, "im", "mm")
+    tt(T.BO[:], T.pg[:], T.mg[:], O.is_equal, "pg mg", "BO")
+    tt(T.RS[:], T.pm[:, 0:16], T.mm[:, 0:16], O.is_equal, "pm mm", "RS")
+    ts(T.mm1[:], T.mm[:], 1.0, O.add, "mm", "mm1")
+    tt(T.mv1[:], T.mg[:], T.ip[:], O.is_equal, "mg ip", "mv1")
+    ts(T.RSn[:], T.RS[:], -1.0, O.mult, "RS", "RSn")
+    tt(T.mv1[:], T.mv1[:], T.mm1[:], O.mult, "mv1 mm1", "mv1")
+    tt(T.mm1[:], T.mm1[:], T.BO[:], O.mult, "mm1 BO", "mm1")
+    ts(T.mmV[:], T.mv1[:], -1.0, O.add, "mv1", "mmV")
+    ts(T.mmB[:], T.mm1[:], -1.0, O.add, "mm1", "mmB")
+    for i in range(16):
+        ts(T.EV[0:8, i, :], T.mmV[0:8, :], float(i), O.is_equal, "mmV", "EV%d" % i)
+    for i in range(16):
+        ts(T.ES[:, i, :], T.mmB[:], float(i), O.is_equal, "mmB", "ES%d" % i)
+    wr["EV"] = wr["EV15"]
+    wr["ES"] = wr["ES15"]
+    for i in range(16):
+        act(T.Dn[:, i, :], T.BO[:], AF.Copy, "BO RSn", "Dn%d" % i, scale=T.RSn[:, i:i + 1])
+    wr["Dn"] = wr["Dn15"]
+    cu, cf, nz = T.cu, T.cf, T.nz
+    cp(cu[:], T.cxi[:], "cxi", "cu0 cu1")
+    cp(cf[:], T.cxi[:], "cxi", "cf0 cf1")
+    ts(T.sff[:], T.sfi[:], -2048.0, O.add, "sfi", "sff")
+    ts(nz[:], cf[:], 0.5, O.is_gt, "cf0 cf1", "nz0 nz1", float(TW), O.mult)
+    dma("S", T.TS[15:128:16, TW:TW + W0], T.sff[:], "sff TSF0 TSF1", "TSF")
+    vlist(0)
+    tt(cc(4), T.ip[:], T.im[:], O.is_le, "ip im", "c4")
+    tt(T.PRE[:], T.BO[:], cc(4), O.mult, "BO c4", "PRE")
+    tt(T.ZT[:], T.PRE[:], T.BO[:], O.subtract, "PRE BO", "ZT")
+    for k in range(2 * NCH):
+        sl = slice(k * CH // 2, (k + 1) * CH // 2)
+        ti, tn = T["ti%d" % (k % 2)], "ti%d" % (k % 2)
+        ts(ti[:], T.tk[:, sl], 15, O.bitwise_and, "tk%d" % (k // 2), tn)
+        ts(T.TC[:, sl], ti[:], -D, O.add, tn, "TC_%d" % (k // 2))
+
+    def tables2():
+        for k in range(NCH):
+            sl = slice(k * CH, (k + 1) * CH)
+            ts(T.TS[:, sl], T.tk[:, sl], -7.5, O.add, "tk%d" % k, "TS_%d" % k, MAG, O.add)
+            act(T.TS[:, sl], T.TS[:, sl], AF.Identity, "TS_%d" % k, "TS_%d" % k, bias=-(MAG / 16) - 2048.0, scale=1.0 / 16)
+    v_(lambda: V.memset(sm(0), 0.0), "", "F1")
+
+    def consts2():
+        tt(T.dif[:], T.im[:], T.ip[:], O.subtract, "im ip", "dif")
+        ts(T.cols[:, 0:1], T.RS[:, 15:16], 800.0, O.mult, "RS", "cl0", -400.0, O.add)
+        ts(T.cols[:, 1:2], T.RS[:, 15:16], 1609800.0, O.mult, "RS", "cl1", -409800.0, O.add)
+        ts(cc(0), T.dif[:], 1.0, O.is_equal, "dif", "c0")
+        ts(cc(1), T.dif[:], -15.0, O.is_equal, "dif", "c1")
+        ts(cc(2), T.dif[:], 0.0, O.is_equal, "dif", "c2")
+        tt(cc(0), cc(0), cc(1), O.add, "c0 c1", "c0")
+        ts(cc(3), T.mm[:], 15.0, O.is_lt, "mm", "c3")
+        tt(cc(0), cc(0), T.BO[:], O.mult, "c0 BO", "c0")
+        tt(cc(2), cc(2), cc(3), O.mult, "c2 c3", "c2")
+        ts(T.BN[:], T.BO[:], T.RS[:, 15:16], O.mult, "BO RS", "BN", 1024.0, O.mult)
+        tt(T.DL[:], cc(0), cc(2), O.subtract, "c0 c2", "DL")
+        ts(T.NI[:], T.dif[:], 0.0, O.is_equal, "dif", "NI", -1.0, O.mult)
+        ts(T.cols[:, 2:3], T.pm[:, 0:1], 0.0, O.add, "pm", "cl2")
+        ts(T.cols[:, 3:4], T.RS[:, 0:1], 64.0, O.mult, "RS", "cl3a")
+        tt(T.cols[:, 4:5], T.cols[:, 3:4], T.RS[:, 1:2], O.add, "cl3a RS", "cl3")
+
+    def late():
+        v_(lambda: V.memset(T.zz[:], 0.0), "", "zz")
+        ts(T.lkj[:], T.lki[:], 6, O.arith_shift_right, "lki", "lkj")
+        ts(T.lki[:], T.lki[:], 63, O.bitwise_and, "lki", "lki")
+        cp(T.lhf[:], T.lkj[:], "lkj", "lhf")
+        cp(T.llf[:], T.lki[:], "lki", "llf")
+        dma("S", T.TL[0:128:16, 0:W0], T.lhf[:], "lhf TL", "TLa")
+        dma("S", T.TL[1:128:16, 0:W0], T.llf[:], "llf TL", "TLb")
+        ts(cc(3), T.mm[:], 15.0, O.is_equal, "mm", "c3")
+        ts(T.tri[:], T.io3[:], T.cols[:, 2:3], O.is_gt, "io3 cl2", "tri")
+        tt(T.B15[:], T.BO[:], cc(3), O.mult, "BO c3", "B15")
+        ts(T.mL[:], T.mi[:], T.cols[:, 2:3], O.add, "mi cl2", "mL")
+        for i in range(16):
+            ts(T.EW[:, i, :], T.mmB[:], float(i), O.is_equal, "mmB cl2", "EW%d" % i, T.cols[:, 2:3], O.mult)
+            ts(T.EH[:, i, :], T.mmB[:], float(i), O.is_equal, "mmB cl3", "EH%d" % i, T.cols[:, 4:5], O.mult)
+        wr["EW"] = wr["EW15"]
+        wr["EH"] = wr["EH15"]
+        ts(T.Dm[:], T.mL[:], float(LN - 129), O.add, "mL", "Dm")
+        ts(sm(9), T.mL[:, 0:16], float(4096 - 129 - 2047), O.add, "mL", "bz")
+        ts(sm(10), sm(9), 2047.0, O.add, "bz", "bz16", 16.0, O.mult)
+        for i in range(16):
+            act(T.D15[:, i, :], T.B15[:], AF.Copy, "B15 RSn", "D15%d" % i, scale=T.RSn[:, i:i + 1])
+        wr["D15"] = wr["D1515"]
+
+    TCR = "TC TC_0 TC_1 TC_2 TC_3 TCz"
+    TSR = "TS TS_0 TS_1 TS_2 TS_3 TSz TSF TSF0 TSF1"
+    TLR = "TL TLa TLb"
+    Wt = [W0]
+    PX, PL = (T.PX0, T.PX1), (T.PL0, T.PL1)
+
+    def K(s, h):
+        return s.replace("@", str(h))
+
+    def HL(h):
+        return slice(1024 * h, 1024 * h + 1024)
+
+    def HC(h):
+        return slice(64 * h, 64 * h + 64)
+
+    def S1(h, t, s):
+        win = T.TC[:, 0:Wt[0]].indirect(cu[:, HC(h)])
+        if t == 0 and s == 0:
+            cp(T.q[:, HL(h)], win, TCR + K(" cu@", h), K("q@", h))
+        else:
+            tt(T.q[:, HL(h)], win, T.mk[:, HL(h)], O.mult, TCR + K(" cu@ mk@", h), K("q@", h))
+
+    def S2(h):
+        act(T.G[:, HL(h)], T.q[:, HL(h)], AF.Sigmoid, K("q@", h), K("G@", h), bias=-200.0, scale=400.0)
+
+    def S3q(h):
+        listsum(PL[h][:, 0:64], T.ES, T.q, 1024 * h, 1024 * h + 1024, K("q@ ES", h), K("PL@", h))
+        listsum(PL[h][:, 64:128], T.ES, T.q, 1024 * h, 1024 * h + 1024, K("q@ ES", h), K("PL@", h), stop=False)
+
+    def S3G(h):
+        listsum(PL[h][:, 64:128], T.ES, T.G, 1024 * h, 1024 * h + 1024, K("G@ ES", h), K("PL@", h), start=False)
+
+    def S3p(h):
+        def f():
+            for b in (0, 512):
+                x = P.matmul(PX[h][:, b:b + 512], T.PRE[:], T.q[:, 1024 * h + b:1024 * h + b + 512], True, False)
+            return x
+        p_(f, K("q@ PRE", h), K("PX@0 PX@1", h))
+
+    def S4(h, s, o=None):
+        C = HC(h)
+        fill = [] if o is None else S11(o)
+        tt(T.xx[:, C], PL[h][:, 64:128], T.vl[:, 128 * s + 64 * h:128 * s + 64 * h + 64], O.mult, K("PL@ vl", h), K("xx@", h))
+        tt(T.es[:, C], PL[h][:, 0:64], T.xx[:, C], O.is_le, K("PL@ xx@", h), K("es@", h))
+        for f in fill[0:1]:
+            f()
+        tt(T.es[:, C], T.es[:, C], nz[:, C], O.mult, K("es@ nz@", h), K("es@", h))
+        for f in fill[1:2]:
+            f()
+        tt(T.c2f[:, C], cf[:, C], T.es[:, C], O.add, K("cf@ es@", h), K("c2f@", h))
+        tt(T.x2[:, C], T.xx[:, C], T.es[:, C], O.add, K("xx@ es@", h), K("x2@", h))
+        cp(T.cu2[:, C], T.c2f[:, C], K("c2f@", h), K("cu2@", h))
+        for f in fill[2:3]:
+            f()
+        ts(T.th[:, C], T.x2[:, C], 1025.0 - 0.4975, O.add, K("x2@", h), K("th@", h))
+
+    def flist(s):
+        ts(sm(5), T.es[:, 0:16], 0.5, O.is_gt, "es0", "e01")
+        ts(sm(1), cf[:, 0:16], 1.0, O.add, "cf0", "d1")
+        ts(sm(2), sm(0), 0.5, O.is_lt, "F1", "t1")
+        tt(sm(3), sm(2), sm(1), O.mult, "t1 d1", "t2")
+        tt(sm(4), sm(0), sm(3), O.add, "F1 t2", "Fo")
+        if s == SP - 1:
+            tt(sm(2), sm(0), sm(5), O.is_gt, "F1 e01", "t1")
+            tt(sm(6), sm(2), sm(5), O.subtract, "t1 e01", "t2")
+            ts(sm(6), sm(6), 0.5, O.is_gt, "t2", "ca t2")
+            ts(T.kh[:, 32:48], sm(6), -1.0, O.mult, "ca", "kh2")
+        tt(sm(0), sm(4), sm(5), O.mult, "Fo e01", "F1")
+        if s == SP - 2:
+            ts(sm(7), sm(0), -2048.0, O.add, "F1", "kf")
+            ts(T.kh[:, 0:16], sm(7), -1.0, O.mult, "kf", "kh0")
+
+    def S5(h):
+        act(T.Sg[:, HL(h)], T.TS[:, 0:TW + Wt[0]].indirect(T.cu2[:, HC(h)]), AF.Copy, TSR + K(" cu2@", h), K("Sg@", h))
+
+    def P6(h):
+        for b in (0, 1):
+            spread(PX[h], 512 * b, 512, T.Dn, T.th, 64 * h + 32 * b, K("th@ Dn", h), K("PX@%d" % b, h), start=False)
+
+    def S7(h):
+        for b in (0, 1):
+            act(T.cm[:, 1024 * h + 512 * b:1024 * h + 512 * b + 512], PX[h][:, 512 * b:512 * b + 512], AF.Sigmoid, K("PX@%d cl0 cl1" % b, h),
+                K("cm@%d" % b, h), bias=T.cols[:, 1:2], scale=T.cols[:, 0:1])
+
+    def P8(h, ps, lhs, r, w):
+        for b in (0, 1):
+            p_(lambda: P.matmul(ps[:, 512 * b:512 * b + 512], lhs[:], T.cm[:, 1024 * h + 512 * b:1024 * h + 512 * b + 512], True, True),
+               K(r % b, h), K(w % b, h))
+
+    def P8u(h):
+        P8(h, T.PU, T.DL, "cm@%d DL", "PU%d")
+
+    def P8t(h):
+        P8(h, PX[h], T.BN, "cm@%d BN", "PX@%d")
+
+    def S9(h, s):
+        tt(T.Y[:, HL(h)], T.Sg[:, HL(h)], T.PU[:], O.mult, K("Sg@ PU0 PU1", h), K("Y@", h))
+        if s == SP - 1 and h == 0:
+            act(T.uf[:], T.PU[:, 0:256], AF.Copy, "PU0", "uf")
+
+    def S10(h):
+        listsum(PL[h][:, 128:192], T.ES, T.Y, 1024 * h, 1024 * h + 1024, K("Y@ ES", h), K("PL@", h))
+
+    def M(h):
+        tt(T.mk[:, HL(h)], T.q[:, HL(h)], PX[h][:], O.is_lt, K("q@ PX@0 PX@1", h), K("mk@", h))
+
+    def S11(h):
+        C, y = HC(h), PL[h][:, 128:192]
+        return [lambda: ts(cu[:, C], y, 2048.0, O.add, K("PL@", h), K("cu@", h)),
+                lambda: ts(cf[:, C], y, 2048.0, O.add, K("PL@", h), K("cf@", h)),
+                lambda: ts(nz[:, C], y, -2047.5, O.is_gt, K("PL@", h), K("nz@", h), float(TW), O.mult)]
+
+    def eqs(x):
+        def one(k):
+            return lambda: ts(T["EQ%d" % x][:, k, 0:256 - 16 * k], T.R[:, 256 * x + 16 * k:256 * x + 256], T.sm[:, 112 + 16 * x + k:113 + 16 * x + k],
+                              O.is_equal, "R%d %s" % (x, ("kf", "kd")[x]), "E%d_%d" % (x, k))
+        alle = " ".join("E%d_%d" % (x, k) for k in range(16))
+        d = T["EQ%d" % x][:, :, 0:16]
+        return [one(k) for k in range(16)] + [lambda: tt(d, d, T.tri[:], O.mult, alle + " tri", alle)]
+
+    def rows(c, kn, ps, base, key):
+        spread(ps, base, 256, T.Dn, T.kh, c, "Dn " + kn, key)
+
+    def slot(h, t, s, o, so):
+        keyf, keyd, cand = h == 1 and s == SP - 2, h == 0 and s == SP - 1, h == 1 and s == SP - 1
+        eq = eqs(0)[0:9] if keyd else eqs(0)[9:] if cand else []
+        S1(h, t, s)
+        if o is not None:
+            P8u(o)
+        S2(h)
+        S3q(h)
+        if keyd:
+            ts(sm(8), cf[:, 0:16], 1.0 - 2048.0, O.add, "cf0", "kd")
+            ts(T.kh[:, 16:32], sm(8), -1.0, O.mult, "kd", "kh1")
+        for f in eq[0:2]:
+            f()
+        if o is not None:
+            S9(o, so)
+        if h == 1:
+            flist(s)
+        else:
+            for f in eq[2:]:
+                f()
+        S3G(h)
+        if o is not None:
+            S10(o)
+            if marks(t, so):
+                P8t(o)
+        S3p(h)
+        if keyf:
+            rows(0, "kh0", T.PU, 0, "PU0")
+        if keyd:
+            rows(16, "kh1", T.PU, 0, "PU0")
+        if t == s == 0 and h == 0:
+            tables2()
+        S4(h, s, o)
+        P6(h)
+        if cand:
+            rows(32, "kh2", T.PL0, 256, "PL0")
+        S5(h)
+        if cand:
+            act(T.cr[:], T.PL0[:, 256:512], AF.Copy, "PL0", "cr")
+        if t == s == 0 and h == 0:
+            consts2()
+        if keyf:
+            cp(T.R[:, 0:256], T.PU[:, 0:256], "PU0", "R0")
+        if keyd:
+            cp(T.R[:, 256:512], T.PU[:, 0:256], "PU0", "R1")
+        if o is not None and marks(t, so):
+            M(o)
+        S7(h)
+        if cand:
+            for f in eq[2:]:
+                f()
+            for k in range(16):
+                act(T.BC[:, k, :], T.BO[:], AF.Copy, "BO ca", "BC%d" % k, scale=T.sm[:, 96 + k:97 + k])
+
+    def dups(x):
+        def f():
+            for k in range(16):
+                y = P.matmul(PL[x][:, 256 + 16 * k:512], T.BC[:, k, :], T["EQ%d" % x][:, k, 0:256 - 16 * k], k == 0, k == 15)
+            return y
+        p_(f, " ".join("E%d_%d BC%d" % (x, k, k) for k in range(16)), "PL%d" % x)
+
+    def firsts(x):
+        sl = slice(256 * x, 256 * x + 256)
+        tt(T.fr[:, sl], PL[x][:, 256:512], T.cr[:], O.is_lt, "PL%d cr" % x, "fr%d" % x)
+        listsum(PL[x][:, 192:208], T.ES, T.fr, 256 * x, 256 * x + 256, "fr%d ES" % x, "PL%d" % x)
+
+    def offs(x):
+        kk, o, kn = 7 + x, slice(16 * x, 16 * x + 16), ("kf", "kd")[x]
+        tt(T.o1[:, o], sm(kk), sm(9), O.subtract, kn + " bz", "o1%d" % x)
+        tt(T.o2[:, o], T.o1[:, o], PL[x][:, 192:208], O.mult, "o1%d PL%d" % (x, x), "o2%d" % x)
+        tt(T.o1[:, o], T.o2[:, o], sm(10), O.add, "o2%d bz16" % x, "o1%d" % x)
+        ts(T.ou[:, o], T.o1[:, o], 1.0 / 16, O.mult, "o1%d" % x, "ou%d" % x)
+
+    for t in range(RO):
+        last = t == RO - 1
+        iota(T.MK[:], [[0, 640]], 0, 0, "MK")
+        iota(T.H[:, 0:LN], [[0, LN]], 0, 0, "H")
+        for s in range(SP):
+            slot(0, t, s, 1 if s else None, s - 1)
+            slot(1, t, s, 0, s)
+            if t == s == 0:
+                late()
+        if not last:
+            loadv("S", t + 1)
+        tot = T.PX0[:, 0:128]
+        ts(T.eb[:], T.es[:], 0.5, O.is_gt, "es0 es1", "eb")
+        p_(lambda: P.matmul(tot, T.BO[:], T.eb[:], True, True), "BO eb", "PX00")
+        p_(lambda: P.matmul(T.PX0[:, 512:640], T.ZT[:], T.eb[:], True, True), "ZT eb", "PX01")
+        v_(lambda: V.tensor_tensor_scan(T.inc[:], tot, T.zz[:], 128.0, O.add, O.add), "PX00 zz", "inc")
+        ts(T.hc[:], tot, 0.5, O.is_gt, "PX00", "hc")
+        tt(T.ha[:], T.inc[:], tot, O.subtract, "inc PX00", "ha")
+        tt(T.X[:], T.inc[:], T.PX0[:, 512:640], O.add, "inc PX01", "X")
+        ts(T.hb[:], T.ha[:], 639.5, O.is_lt, "ha", "hb")
+        tt(T.ha[:], T.ha[:], T.hc[:], O.mult, "ha hc", "ha")
+        tt(T.ha[:], T.ha[:], T.hb[:], O.mult, "ha hb", "ha")
+        tt(T.off[:], T.ha[:], T.krow[:], O.max, "ha krow", "off")
+        listsum(T.PX0[:, 0:8], T.ES, T.off, 0, 128, "off ES", "PX00")
+        P8u(1)
+        if not last:
+            def f():
+                for b in (0, 512):
+                    P.matmul(T.PX1[:, b:b + 512], T.NI[:], T.q[:, 1024 + b:1536 + b], True, False)
+                    x = P.matmul(T.PX1[:, b:b + 512], T.BN[:], T.cm[:, 1024 + b:1536 + b], False, True)
+                return x
+            p_(f, "q1 cm10 cm11 NI BN", "PX10 PX11")
+        ts(T.tot[:, 0:1], T.inc[:, 127:128], -128.0, O.add, "inc", "tot")
+        send(T["lT%d" % t][:, 0:1], T.tot[:, 0:1], "T", t, "tot")
+        tt(T.X[:], T.X[:], T.eb[:], O.mult, "X eb", "X")
+        eq = eqs(1)
+        for f in eq[0:4]:
+            f()
+        ts(T.ofu[:], T.PX0[:, 0:8], 1.0 / 16, O.mult, "PX00", "ofu")
+        cp(T.MK[:, 0:640].indirect(T.ofu[:]), T.krow[:], "krow ofu", "MK")
+        for f in eq[4:6]:
+            f()
+        v_(lambda: V.tensor_tensor_scan(T.kr[:], T.MK[:, 128:640], T.MK[:, 128:640], 0.0, O.max, O.max), "MK", "kr")
+        S9(1, SP - 1)
+        S10(1)
+        listsum(T.PX0[:, 0:32], T.ES, T.kr, 0, 512, "kr ES", "PX00")
+        dups(0)
+        for f in eq[6:12]:
+            f()
+        if not last:
+            act(T.mk[:, HL(1)], T.PX1[:], AF.Sigmoid, "PX10 PX11", "mk1", bias=-200.0, scale=400.0 / D)
+        act(T.nu[:], T.uf[:], AF.Identity, "uf", "nu", bias=1.0, scale=-1.0)
+        act(T.u1[:], T.uf[:], AF.Copy, "uf", "u1", scale=1.0 - D)
+        for f in S11(1):
+            f()
+        ts(T.klu[:], T.PX0[:, 0:32], 1.0 / 16, O.mult, "PX00", "klu")
+        ts(T.Yl[:], cf[:], -2048.0, O.add, "cf0 cf1", "Yl")
+        tt(T.OH[:], T.X[:].indirect(T.klu[:]), T.mrow[:], O.is_equal, "X klu mrow", "OH")
+        tt(T.CG[:], T.Yl[:].indirect(T.klu[:]), T.OH[:], O.mult, "Yl klu OH", "CG")
+        for f in eq[12:]:
+            f()
+        if not last:
+            listsum(T.PX0[:, 0:32], T.ES, T.kr, 0, 512, "kr ES", "PX00", stop=False)
+            listsum(T.PX0[:, 0:32], T.EW, T.OH, 0, 512, "OH EW", "PX00", start=False)
+            listsum(T.PX0[:, 512:544], T.ES, T.CG, 0, 512, "CG ES", "PX01")
+        else:
+            listsum(T.PX0[:, 512:544], T.ES, T.CG, 0, 512, "CG ES", "PX01")
+            listsum(T.PX0[:, 0:32], T.ES, T.kr, 0, 512, "kr ES", "PX00", stop=False)
+            listsum(T.PX0[:, 0:32], T.EW, T.OH, 0, 512, "OH EW", "PX00", start=False)
+        firsts(0)
+        dups(1)
+        if not last:
+            cp(T.lnu[:], T.PX0[:, 0:32], "PX00", "lnu")
+            act(T.MS[:], T.mk[:, 0:LN].indirect(T.lnu[:]), AF.Copy, "mk0 mk1 lnu", "MS")
+            send(T["lM%d" % t][:], T.MS[:], "M", t, "MS")
+        ts(T.cmu[:], T.PX0[:, 512:544], 2048.0, O.add, "PX01", "cmu")
+        act(T.Lg[:], T.TL[:, 0:Wt[0]].indirect(T.cmu[:]), AF.Copy, TLR + " cmu", "Lg")
+        send(T["lL%d" % t][:], T.Lg[:], "L", t, "Lg")
+        offs(0)
+        firsts(1)
+        act(T.lnf[:], T.PX0[:, 0:32], AF.Copy, "PX00", "lnf")
+        wb = slice(W0 + B * t, W0 + B * (t + 1))
+        wf = slice(TW + W0 + B * t, TW + W0 + B * (t + 1))
+        if not last:
+            act(T.TS[:, wb], T.TS[:, 0:Wt[0]].indirect(cu[:, 0:16]), AF.Copy, TSR + " cu0", "TS")
+            act(T.TL[:, wb], T.TL[:, 0:Wt[0]].indirect(cu[:, 0:16]), AF.Copy, TLR + " cu0", "TL")
+            ts(T.kh[:, 48:64], T.Yl[:, 0:16], -1.0, O.mult, "Yl", "kh3")
+            spread(T.PU, 0, 256, T.D15, T.kh, 48, "D15 kh3", "PU0")
+            act(T.TS[:, wf], T.PU[:, 0:256], AF.Copy, "PU0", "TS")
+            tt(T.uw[:], T.uf[:], T["wr%d" % t][:], O.mult, "uf wr%d" % t, "uw")
+        v_(lambda: V.tensor_scalar(T.rr[:], T.TC[:, 0:Wt[0]].indirect(cu[:, 0:16]), 0.5, 0.25, O.mult, O.add), TCR + " cu0", "rr")
+        offs(1)
+        tt(T.r2[:], T.rr[:], T.fr[:, 0:256], O.mult, "rr fr0", "r2")
+        if not last:
+            vlist(t + 1)
+        ts(T.TC[:, wb], T.r2[:], -D, O.add, "r2", "TC")
+        tt(T.aC[:], T.TC[:].indirect(T.ou[:, 0:16]), T.nu[:], O.mult, TCR + " ou0 nu", "aC")
+        tt(T.TC[:].indirect(T.ou[:, 0:16]), T.aC[:], T.u1[:], O.add, "aC u1 ou0", "TC")
+        if not last:
+            tt(T.aS[:], T.TS[:, 0:TW].indirect(T.ou[:, 0:16]), T.nu[:], O.mult, TSR + " ou0 nu", "aS")
+            tt(T.TS[:, 0:TW].indirect(T.ou[:, 0:16]), T.aS[:], T.uw[:], O.add, "aS uw ou0", "TS")
+        tt(T.aC[:], T.TC[:].indirect(T.ou[:, 16:32]), T.uf[:], O.add, TCR + " ou1 uf", "aC")
+        ts(T.aC[:], T.aC[:], 15.0 - D, O.min, "aC", "aC")
+        cp(T.TC[:].indirect(T.ou[:, 16:32]), T.aC[:], "aC ou1", "TC")
+        Wt[0] += B
+        if last:
+            for k in range(4):
+                for b in (0, 1):
+                    o = slice(1024 * k + 512 * b, 1024 * k + 512 * b + 512)
+                    if b or k == 3:
+                        act(T.yb[:, o], T.TC[:, o], AF.Relu, TCR, "yb%d%d" % (k, b))
+                    else:
+                        ts(T.yb[:, o], T.TC[:, o], 0.0, O.max, TCR, "yb%d%d" % (k, b))
+                o = slice(1024 * k, 1024 * k + 1024)
+                dma("S", T.yn[:, o], T.yb[:, o], "yb%d0 yb%d1" % (k, k), "yn%d" % k)
+        tt(T.tot[:, 1:2], T.tot[:, 0:1], T["lT%d" % t][:, 0:1], O.min, "tot lT%d" % t, "tm1")
+        tt(T.so[:], T.lnf[:], T.Dm[:], O.subtract, "lnf Dm", "so")
+        ts(T.tot[:, 2:3], T.tot[:, 1:2], float(CAP), O.min, "tm1", "tm2", 128.0, O.add)
+        tm = T.tot[:, 2:3]
+        ts(T.vd[:], T.mL[:], tm, O.is_le, "mL tm2", "vd")
+        ts(T.mvv[:], T.X[:], tm, O.is_le, "X tm2", "mvv")
+        tt(T.so[:], T.so[:], T.vd[:], O.mult, "so vd", "so")
+        tt(T.mvv[:], T.mvv[:], T.eb[:], O.mult, "mvv eb", "mvv")
+        tt(T.so[:], T.so[:], T.Dm[:], O.add, "so Dm", "so")
+        ts(T.nmv[:], T.mvv[:], -1.0, O.mult, "mvv", "nmv", 1.0, O.add)
+        cp(T.sou[:], T.so[:], "so", "sou")
+        tt(cf[:], cf[:], T.nmv[:], O.mult, "cf0 cf1 nmv", "cf0 cf1")
+        if not last:
+            tt(sm(0), sm(0), T.nmv[:, 0:16], O.mult, "F1 nmv", "F1")
+        cp(T.H[:].indirect(T.sou[:]), T["lL%d" % t][:], "sou lL%d" % t, "H")
+        listsum(T.PX0[:, 0:128], T.EH, T.H, 0, LN, "EH H", "PX00")
+        if not last:
+            cp(T.mk[:].indirect(T.sou[:]), T["lM%d" % t][:], "sou lM%d" % t, "mk0 mk1")
+        tt(cf[:], cf[:], T.PX0[:, 0:128], O.add, "cf0 cf1 PX00", "cf0 cf1")
+        if not last:
+            cp(cu[:], cf[:], "cf0 cf1", "cu0 cu1")
+            ts(nz[:], cf[:], 0.5, O.is_gt, "cf0 cf1", "nz0 nz1", float(TW), O.mult)
+    dma("A", T.yc[:, :], cf[:], "cf0 cf1", "yc")
+    for s in sorted(left):
+        if seen["G"].get(s, 0) < left[s]:
+            g.wait_ge(T.sem[s], left[s])

@@ -1,33 +1,107 @@
 from concourse.mybir import AluOpType as O, ActivationFunctionType as AF
 
 W0, B, LN, RO, SP, CAP = 3328, 256, 2048, 3, 3, 512
-TW = 4352
+TW = 4096
+CO = 1920
+DU = 3840
 D = 2.0 ** -14
 MAG = 1.5 * 2.0 ** 27
+R12 = 1.5 * 2.0 ** 19
 NCH, CH = 4, 832
+PC, NB4 = 416, 4
+TAG = [""]
+EST = dict(cy=0.83e-3, pe=0.42e-3, ga=1.5, sc=3.5, call=0.03, wait=0.08, dma=1.3, rem=2.0, turns=4)
+ORDER = []
 
 
 def _sb(dtype, **shapes):
-    return {k: ("sbuf", [128] + ([n] if n > 0 else [16, -n]), dtype) for k, n in shapes.items()}
+    return {k: ("sbuf", [128] + ([n] if n > 0 else [-n, 128]), dtype) for k, n in shapes.items()}
 
 
 SCRATCH = {}
-SCRATCH.update(_sb("int32", tk=W0, ti0=CH // 2, ti1=CH // 2, ip=128, im=128, pg=128, mg=128, pm=128, mm=128, io3=-16, sfi=208, lki=208, lkj=208,
-                   cxi=128, rr=256))
-SCRATCH.update(_sb("float32", TC=TW, TS=2 * TW, TL=4096, vl=384, Sg=LN, MK=640, sm=176, RS=16, RSn=16, dif=128, mrow=512, krow=128,
-                   mi=32, mL=32, Dm=32, wr0=256, wr1=256, wr2=256, zz=128, cols=16, sff=208, lhf=208, llf=208, cf=128, nz=128, c2f=128,
-                   xx=128, es=128, x2=128, o1=32, o2=32, uf=256, nu=256, u1=256, uw=256, r2=256, aC=256, aS=256,
-                   inc=128, X=128, ha=128, hb=128, hc=128, Yl=128, lnf=32, tot=8, lT0=8, lT1=8, lT2=8, vd=32, so=32, mvv=128, nmv=128))
-SCRATCH.update(_sb("bfloat16", vvr=SP * LN, G=LN, cm=LN, mk=LN + CAP, H=LN + CAP, EQ0=-256, EQ1=-256, BC=-128, yb=4096, ES=-128, Dn=-128, D15=-128,
-                   EV=-128, EW=-128, EH=-128, BO=128, PRE=128, ZT=128, NI=128, DL=128, BN=128, B15=128, cc=640, tri=-16, eb=128, cr=256, fr=512,
+SCRATCH.update(_sb("int32", tk=W0, ti=2 * PC, ip=128, im=128, pg=128, mg=128, pm=128, mm=128, m8=128, sfi=208, lki=208, lkj=208, cxi=128, fi=32))
+SCRATCH.update(_sb("float32", TC=TW + 16, TS=TW + DU, tr=NB4 * PC, vl=768, xx=256, MK=2192, sm=192, RS=16, LT=16, mrow=512, krow=128, mi=32, mL=32, Dm=32,
+                   zz=128, cols=8, sff=208, cf=128, cr=128, X=128, K=32, dk=32, dum=32, dus=32, mo=32, nu=256, u1=256, om=256, dsg=256, nD=256, aC=256, aD=256, aE=256,
+                   aF=256, tot=8, lT=24, so=32, nmv=128, o8=16))
+SCRATCH.update(_sb("bfloat16", vvr=SP * LN, s=LN, mk=LN + CAP, H=LN + CAP, EQ0=4096, EQ1=4096, yb=TW + 16, TL=4096, ES=-16, Dn=-16, E8=-8, EV=-8,
+                   EW=-16, EH=-16, TR=-16, M=-16, cd=256, rt=128, ry=128, rb=NB4 * PC, eb=128, du=512, lhf=208, llf=208, Cb=256, Cc=256, nb=256, ob=256, ab=256, r2=256,
                    OH=512, MS=512, Lg=512, lM0=512, lM1=512, lL0=512, lL1=512, lL2=512))
-SCRATCH.update(_sb("float16", q=LN, Y=LN, th=128, mmB=128, mm1=128, mmV=128, mv1=128, kh=64, R=512, off=128, kr=512, CG=512))
-SCRATCH.update(_sb("uint16", cu=128, cu2=128, ou=32, ofu=8, klu=32, cmu=32, lnu=32, sou=32))
+SCRATCH.update(_sb("float16", q=LN, Y=LN, p=256, th=256, c16=128, cm=128, sh=NB4 * PC, mmB=128, m8B=128, mmV=128, t16=128, o64=128, K16=32, R=512, inc=144,
+                   kL=16, kr=512, CG=512, Yf=256, wn=512))
+SCRATCH.update(_sb("uint16", cu=128, cu2=128, ou=32, su=16, ofu=8, klu=32, cmu=32, lnu=32, sou=32))
 SCRATCH.update({k: ("psum", [128, n], "float32") for k, n in (("PX0", 1024), ("PX1", 1024), ("PU", 1024), ("PL0", 512), ("PL1", 512))})
 DMAS = ["d%d" % i for i in range(24)]
 REM = [a + str(t) for t in range(RO) for a in ("aT", "aM", "aL", "nT", "nM", "nL") if not (t == RO - 1 and a[1] == "M")]
 SEMAPHORES = ["sV", "sA", "sP", "sG"] + DMAS + REM
 BANKS = {"PX00", "PX01", "PX10", "PX11", "PU0", "PU1", "PL0", "PL1"}
+BO, PRE, DX, ID, NI, NQ, I65, RL0, RL1, SL0, SL1, ZT, DL, DD, NB, IK = range(16)
+
+
+def bank(k):
+    k = k.split(".")[0]
+    return k if k in BANKS else None
+
+
+def order(ops):
+    wr, rd, pre = {}, {}, []
+    for n, o in enumerate(ops):
+        p = {}
+        for k in o["r"]:
+            if k in wr:
+                p[wr[k]] = 1
+        for k in o["w"]:
+            for j in rd.get(k, []) + ([wr[k]] if k in wr and o["q"] == "P" else []):
+                p.setdefault(j, 0 if ops[j]["q"] == o["q"] == "P" else 1)
+            if k in wr:
+                p.setdefault(wr[k], 1)
+        p.pop(n, None)
+        pre.append(p)
+        for k in o["r"]:
+            rd.setdefault(k, []).append(n)
+        for k in o["w"]:
+            wr[k], rd[k] = n, []
+    N = len(ops)
+    suc = [{} for _ in ops]
+    for n, p in enumerate(pre):
+        for j, w in p.items():
+            suc[j][n] = w
+
+    def place(seq, dep, back):
+        st, busy = [0.0] * N, {}
+        for n in seq:
+            o = ops[n]
+            t = max([st[j] + ops[j]["c"] + ops[n if back else j]["lat"] + EST["wait"] * w for j, w in dep[n].items()], default=o["lat"] if back else 0.0)
+            res = [(o["q"], 0.0)] + [(b, EST["wait"]) for b in o["b"]]
+            moved = True
+            while moved:
+                moved = False
+                for r, gap in res:
+                    for a, e, q in busy.get(r, []):
+                        m = gap if q != o["q"] else 0.0
+                        if a - m < t + o["c"] - 1e-9 and t < e + m - 1e-9:
+                            t, moved = e + m, True
+            st[n] = t
+            for r, gap in res:
+                x = busy.setdefault(r, [])
+                k = len(x)
+                while k and x[k - 1][0] > t:
+                    k -= 1
+                x.insert(k, (t, t + o["c"], o["q"]))
+        return st
+
+    def end(st):
+        return max(st[n] + ops[n]["c"] + ops[n]["lat"] for n in range(N))
+    way = [0.0] * N
+    for n in range(N - 1, -1, -1):
+        way[n] = ops[n]["c"] + ops[n]["lat"] + max([way[j] + EST["wait"] for j in suc[n]], default=0.0)
+    st = best = place(sorted(range(N), key=lambda n: (-way[n], n)), pre, False)
+    for _ in range(EST["turns"]):
+        bk = place(sorted(range(N), key=lambda n: (-(st[n] + ops[n]["c"] + ops[n]["lat"]), -n)), suc, True)
+        st = place(sorted(range(N), key=lambda n: (-(bk[n] + ops[n]["c"]), n)), pre, False)
+        if end(st) < end(best):
+            best = st
+    TAG.append(end(best))
+    return sorted(range(N), key=lambda n: (best[n], n))
 
 
 def rank_program(g, core, T, topo):
@@ -36,570 +110,529 @@ def rank_program(g, core, T, topo):
         return
     V, A, P, S = g.vector, g.scalar, g.tensor, g.sync
     eng = {"V": V, "A": A, "P": P, "S": S, "G": g}
-    seen = {k: {} for k in eng}
-    cnt = {k: 0 for k in "VAPG"}
-    wr, rd, left = {}, {}, {}
-    ndma = [0]
+    ops, alias, ndma = [], {}, [0]
 
-    def run(qn, fn, r, w, acc=False, sem=None, remote=False, n=1):
-        r, w = r.split(), w.split()
-        own = "s" + qn
-        need = {}
+    def run(qn, fn, r, w, c, sem=None, remote=False, n=1, lat=0.0):
+        r = [x for k in r.split() for x in alias.get(k, [k])]
+        w = w.split()
+        ops.append(dict(q=qn, fn=fn, r=r, w=w, c=c, sem=sem, remote=remote, n=n, lat=lat, b={bank(k) for k in r + w} - {None}, tag=TAG[0]))
 
-        def want(toks, skip):
-            for s, v in toks.items():
-                if not (skip and s == own):
-                    need[s] = max(need.get(s, 0), v)
-        for k in r:
-            want(wr.get(k, {}), False)
-            if k in BANKS:
-                want(rd.get(k, {}), True)
-        for k in w:
-            want(wr.get(k, {}), acc)
-            want(rd.get(k, {}), sem is None)
-        for s in sorted(need):
-            if seen[qn].get(s, 0) < need[s]:
-                eng[qn].wait_ge(T.sem[s], need[s])
-                seen[qn][s] = need[s]
-        inst = fn()
-        if sem is None:
-            cnt[qn] += 1
-            s, v = own, cnt[qn]
-        else:
-            s, v = sem, n
-        if not remote:
-            inst.then_inc(T.sem[s], n)
-        left[s] = v
-        for k in r:
-            rd.setdefault(k, {})[s] = v
-        for k in w:
-            wr[k] = {s: v}
-            rd[k] = {}
+    def issue():
+        seen = {k: {} for k in eng}
+        cnt = {k: 0 for k in "VAPG"}
+        wr, rd, bk, left = {}, {}, {}, {}
+        if not ORDER:
+            ORDER.extend(order(ops))
+        for n in ORDER:
+            o = ops[n]
+            qn, sem = o["q"], o["sem"]
+            own, need = "s" + qn, {}
 
-    def v_(fn, r, w): run("V", fn, r, w)
-    def a_(fn, r, w): run("A", fn, r, w)
-    def p_(fn, r, w): run("P", fn, r, w, acc=True)
-    def g_(fn, r, w): run("G", fn, r, w)
+            def want(toks, skip):
+                for s, v in toks.items():
+                    if not (skip and s == own):
+                        need[s] = max(need.get(s, 0), v)
+            for k in o["r"]:
+                want(wr.get(k, {}), qn == "P" and k[0] == "*")
+            for k in o["w"]:
+                want(wr.get(k, {}), qn == "P")
+                want(rd.get(k, {}), qn == "P")
+            for b in o["b"]:
+                want(bk.get(b, {}), True)
+            for s in sorted(need):
+                if seen[qn].get(s, 0) < need[s]:
+                    eng[qn].wait_ge(T.sem[s], need[s])
+                    seen[qn][s] = need[s]
+            TAG[0] = o["tag"]
+            inst = o["fn"]()
+            if sem is None:
+                cnt[qn] += 1
+                s, v = own, cnt[qn]
+            else:
+                s, v = sem, o["n"]
+            if not o["remote"]:
+                inst.then_inc(T.sem[s], o["n"])
+            left[s] = v
+            for k in o["r"]:
+                rd.setdefault(k, {})[s] = v
+            for k in o["w"]:
+                wr[k], rd[k] = {s: v}, {}
+            if o["remote"]:
+                wr[o["w"][0]] = {"a" + s[1:]: v}
+                left["a" + s[1:]] = v
+            for b in o["b"]:
+                bk.setdefault(b, {})[s] = v
+        for s in sorted(left):
+            if seen["G"].get(s, 0) < left[s]:
+                g.wait_ge(T.sem[s], left[s])
 
-    def dma(qn, out, in_, r, w):
+    def size(ap):
+        n = 1
+        for d in ap.shape[1:]:
+            n *= d
+        return n
+
+    def ind(win, off):
+        return (win.indirect(off), 16 * off.shape[1])
+
+    def cost(out, ins, r, w, two=False, fast=True):
+        if isinstance(out, tuple):
+            return 0.05 + out[1] * EST["sc"] * EST["cy"]
+        if ins and isinstance(ins[0], tuple):
+            return 0.05 + ins[0][1] * EST["ga"] * EST["cy"]
+        ps = any(bank(k) for k in (r + " " + w).split())
+        rate = (1.0 if ps else 2.0) if two else 0.5 if fast and all("16" in str(a.dtype) for a in [out] + ins) else 1.0
+        return EST["call"] + max(64, size(out) * rate) * EST["cy"]
+
+    def ap(x):
+        return x[0] if isinstance(x, tuple) else x
+
+    def dma(qn, out, in_, r, w, kb):
         s = DMAS[ndma[0]]
         ndma[0] += 1
-        run(qn, lambda: eng[qn].dma_start(out, in_), r, w, sem=s, n=16)
+        run(qn, lambda: eng[qn].dma_start(out, in_), r, w, 0.05, sem=s, n=16, lat=EST["dma"] + kb / 180.0)
 
     def ts(out, in0, s1, op0, r, w, s2=None, op1=None):
+        c = cost(out, [in0], r, w)
         if op1 is None:
-            v_(lambda: V.tensor_scalar(out, in0, s1, None, op0), r, w)
+            run("V", lambda: V.tensor_scalar(out, ap(in0), s1, None, op0), r, w, c)
         else:
-            v_(lambda: V.tensor_scalar(out, in0, s1, s2, op0, op1), r, w)
+            run("V", lambda: V.tensor_scalar(out, ap(in0), s1, s2, op0, op1), r, w, c)
 
     def tt(out, in0, in1, op, r, w):
-        v_(lambda: V.tensor_tensor(out, in0, in1, op), r, w)
+        run("V", lambda: V.tensor_tensor(ap(out), ap(in0), in1, op), r, w, cost(out, [in0, in1], r, w, True))
 
     def cp(out, in_, r, w):
-        v_(lambda: V.tensor_copy(out, in_), r, w)
+        run("V", lambda: V.tensor_copy(ap(out), ap(in_)), r, w, cost(out, [in_], r, w))
+
+    def fill(out, x, w):
+        run("V", lambda: V.memset(out, x), "", w, cost(out, [], "", w))
+
+    def scan(out, a, b, op, r, w):
+        run("V", lambda: V.tensor_tensor_scan(out, a, b, 0.0, op, op), r, w, cost(out, [a], r, w, fast=False))
 
     def act(out, in_, func, r, w, bias=0.0, scale=1.0):
-        a_(lambda: A.activation(out, in_, func, bias=bias, scale=scale), r, w)
+        run("A", lambda: A.activation(out, ap(in_), func, bias=bias, scale=scale), r, w, cost(out, [in_], r, w, fast=False))
 
-    def listsum(out, fam, src, lo, hi, r, w, start=True, stop=True):
+    def mm(group, r, w, more=False):
         def f():
-            for i in range(16):
-                x = P.matmul(out, fam[:, i, :], src[:, lo + i:hi:16], start and i == 0, stop and i == 15)
-            return x
-        p_(f, r, w)
+            for n, (o, l, x, st) in enumerate(group):
+                i = P.matmul(o, l, x, st, group[n + 1][3] if n + 1 < len(group) else not more)
+            return i
+        star = " ".join({"*" + bank(k) for k in w.split()})
+        c = sum(max(64, size(x)) for o, l, x, st in group) * EST["pe"]
+        if group[0][3]:
+            run("P", f, r, w + " " + star, c)
+        else:
+            run("P", f, r + " " + star, w, c)
 
-    def spread(out, base, n, fam, src, lo, r, w, start=True):
-        def f():
-            for i in range(16):
-                x = P.matmul(out[:, base + i:base + n:16], fam[:, i, :], src[:, lo:lo + n // 16], start, start or i == 15)
-            return x
-        p_(f, r, w)
+    def acc(out, terms, start=True):
+        return [(out, l, x, start and n == 0) for n, (l, x) in enumerate(terms)]
+
+    def lsum(fam, src, lo, hi, n=16):
+        return [(fam[:, i, :], src[:, lo + i:hi:n]) for i in range(n)]
+
+    def spread(out, base, w, src, n, start):
+        return [(out[:, base + i:base + w:n], T.Dn[:, i, :], src, start) for i in range(n)]
+
+    def m_(k):
+        return T.M[:, k, :]
 
     nxt = T.cores[(rank + 1) % len(T.cores)]
     rid, pid, _se = topo.addr(nxt)
     emask = topo.mask(core, nxt)
     ne = len(topo.engines(core, nxt))
 
-    def send(dst, src, name, t, r):
+    def send(dst, src, name, t, r, kb):
         s, rs = "n%s%d" % (name, t), "a%s%d" % (name, t)
-        run("G", lambda: g.remote_dma(dst, src, T.sem[rs], T.sem[s], pid, rid, emask), r, "", sem=s, remote=True, n=ne)
-
-    for t in range(RO):
-        for a in "TML":
-            if t < RO - 1 or a != "M":
-                wr["l%s%d" % (a, t)] = {"a%s%d" % (a, t): ne}
-                left["a%s%d" % (a, t)] = ne
-
-    def marks(t, s):
-        return not (t == RO - 1 and s == SP - 1)
+        run("G", lambda: g.remote_dma(dst, src, T.sem[rs], T.sem[s], pid, rid, emask), r, "l%s%d" % (name, t), 0.1, sem=s, remote=True, n=ne,
+            lat=EST["rem"] + kb / 60.0 + (2.0 if t == 0 and name == "T" else 0.0))
 
     def sm(k):
         return T.sm[:, 16 * k:16 * k + 16]
 
-    def cc(k):
-        return T.cc[:, 128 * k:128 * k + 128]
-
     def loadv(qn, t):
-        dma(qn, T.vvr[0:8, :], T.vv[:, SP * LN * t:SP * LN * (t + 1)], "", "vvr")
+        dma(qn, T.vvr[0:8, :], T.vv[:, SP * LN * t:SP * LN * (t + 1)], "", "vvr", 100)
 
-    def vlist(t):
-        for s in range(SP):
-            def f(s=s):
-                for i in range(16):
-                    x = P.matmul(T.PU[:, 512 + 128 * s:640 + 128 * s], T.EV[0:8, i, :], T.vvr[0:8, LN * s + i:LN * (s + 1):16], i == 0, i == 15)
-                return x
-            p_(f, "EV vvr", "PU1")
-        act(T.vl[:], T.PU[:, 512:512 + 128 * SP], AF.Copy, "PU1", "vl", scale=1.0 / 256)
+    PX, PL = (T.PX0, T.PX1), (T.PL0, T.PL1)
+
+    def K(s, h, b=0):
+        return s.replace("@", str(h)).replace("#", str(b))
+
+    def vlist(h, s):
+        lo = LN * s + 1024 * h
+        mm(acc(PL[h][:, 384:512], [(T.EV[0:8, j, :], T.vvr[0:8, lo + j:lo + 1024:8]) for j in range(8)]), "EV vvr", K("PL@.v", h))
+        act(T.vl[:, 256 * s + 128 * h:256 * s + 128 * h + 128], PL[h][:, 384:512], AF.Copy, K("PL@.v", h), K("vl@#", h, s), scale=-1.0 / 256)
 
     loadv("A", 0)
     for k in range(NCH):
-        dma("S", T.tk[:, k * CH:(k + 1) * CH], T.tab[:, k * CH:(k + 1) * CH], "", "tk%d" % k)
+        dma("S", T.tk[:, k * CH:(k + 1) * CH], T.tab[:, k * CH:(k + 1) * CH], "ld%d" % k, "tk%d ld%d" % (k, k + 1), 100 + 430 * (k + 1))
+        ops[-1]["r"], ops[-1]["w"] = [], ["tk%d" % k]
         if k == 0:
-            dma("S", T.cxi[:], T.cx[:, :], "", "cxi")
-            dma("S", T.sfi[:], T.suf[:, :], "", "sfi")
-    dma("S", T.lki[:], T.lnk[:, :], "", "lki")
+            dma("S", T.cxi[:], T.cx[:, :], "", "cxi", 600)
+            dma("S", T.sfi[:], T.suf[:, :], "", "sfi", 700)
+    dma("S", T.lki[:], T.lnk[:, :], "", "lki", 2000)
 
     def iota(out, pat, base, cm, w, small=True):
+        c = 0.13 + 2 * size(out) * EST["cy"]
         if small:
-            g_(lambda: g.iota(out, pat, base, cm, allow_small_or_imprecise_dtypes=True), "", w)
+            run("G", lambda: g.iota(out, pat, base, cm, allow_small_or_imprecise_dtypes=True), "", w, c)
         else:
-            g_(lambda: g.iota(out, pat, base, cm), "", w)
+            run("G", lambda: g.iota(out, pat, base, cm), "", w, c)
+
+    def zero(buf, lo, hi, w, n=1):
+        st = (hi - lo) // n
+        for k in range(n):
+            iota(buf[:, lo + k * st:lo + (k + 1) * st], [[0, st]], 0, 0, w if n == 1 else "%s_%d" % (w, k))
+        if n > 1:
+            alias[w] = ["%s_%d" % (w, k) for k in range(n)]
     iota(T.ip[:], [[0, 128]], 0, 1, "ip", False)
     iota(T.im[:], [[1, 128]], 0, 0, "im", False)
-    iota(T.TS[:, TW:TW + 2176], [[0, 2176]], 0, 0, "TSF0")
-    iota(T.TS[:, TW + 2176:2 * TW], [[0, 2176]], 0, 0, "TSF1")
-    iota(T.TC[:, W0:TW], [[0, TW - W0]], 0, 0, "TCz")
-    iota(T.TS[:, W0:TW], [[0, TW - W0]], 0, 0, "TSz")
-    iota(T.mi[:], [[16, 32]], 129, 0, "mi")
-    iota(T.io3[:], [[0, 16], [1, 16]], 0, 0, "io3", False)
+    zero(T.TC, W0, TW + 16, "TCz")
+    zero(T.TS, TW, TW + DU, "TSF0")
+    zero(T.TS, W0, TW, "TSz")
+    iota(T.mi[:], [[16, 32]], 0, 0, "mi")
     iota(T.krow[:], [[1, 128]], 0, 0, "krow")
-    iota(T.TL[:], [[0, 4096]], 0, 0, "TL")
-    iota(T.mrow[:], [[1, 512]], 129, 0, "mrow")
-    for t in range(RO):
-        iota(T["wr%d" % t][:], [[1, 256]], W0 + B * t - 2048, 0, "wr%d" % t)
-    iota(T.H[:, LN:], [[0, CAP]], 0, 0, "H")
+    zero(T.MK, 0, 2192, "MK")
+    zero(T.TL, 0, 4096, "TL")
+    iota(T.mrow[:], [[1, 512]], 1 - 4096, 0, "mrow")
+    zero(T.H, 0, LN + CAP, "H")
+    zero(T.mk, LN, LN + CAP, "mkz")
+
+    def fam(name, key, n, kn, rows=128):
+        for i in range(n):
+            ts(T[name][0:rows, i, :], key[0:rows, :], float(i), O.is_equal, kn, "%s_%d" % (name, i))
+        alias[name] = ["%s_%d" % (name, i) for i in range(n)]
 
     ts(T.pg[:], T.ip[:], 4, O.arith_shift_right, "ip", "pg")
     ts(T.mg[:], T.im[:], 4, O.arith_shift_right, "im", "mg")
     ts(T.pm[:], T.ip[:], 15, O.bitwise_and, "ip", "pm")
     ts(T.mm[:], T.im[:], 15, O.bitwise_and, "im", "mm")
-    tt(T.BO[:], T.pg[:], T.mg[:], O.is_equal, "pg mg", "BO")
+    ts(T.m8[:], T.im[:], 7, O.bitwise_and, "im", "m8")
+    tt(m_(BO), T.pg[:], T.mg[:], O.is_equal, "pg mg", "BO")
     tt(T.RS[:], T.pm[:, 0:16], T.mm[:, 0:16], O.is_equal, "pm mm", "RS")
-    ts(T.mm1[:], T.mm[:], 1.0, O.add, "mm", "mm1")
-    tt(T.mv1[:], T.mg[:], T.ip[:], O.is_equal, "mg ip", "mv1")
-    ts(T.RSn[:], T.RS[:], -1.0, O.mult, "RS", "RSn")
-    tt(T.mv1[:], T.mv1[:], T.mm1[:], O.mult, "mv1 mm1", "mv1")
-    tt(T.mm1[:], T.mm1[:], T.BO[:], O.mult, "mm1 BO", "mm1")
-    ts(T.mmV[:], T.mv1[:], -1.0, O.add, "mv1", "mmV")
-    ts(T.mmB[:], T.mm1[:], -1.0, O.add, "mm1", "mmB")
+    tt(T.mmV[:], T.mg[:], T.ip[:], O.not_equal, "mg ip", "mmV")
+    ts(T.o64[:], m_(BO), -64.0, O.mult, "BO", "o64", 64.0, O.add)
+    ts(T.mmV[:], T.mmV[:], 64.0, O.mult, "mmV", "mmV")
+    tt(T.m8B[:], T.m8[:], T.o64[:], O.add, "m8 o64", "m8B")
+    tt(T.mmV[:], T.mmV[:], T.m8[:], O.add, "mmV m8", "mmV")
+    tt(T.mmB[:], T.mm[:], T.o64[:], O.add, "mm o64", "mmB")
+    fam("EV", T.mmV, 8, "mmV", 8)
+    fam("E8", T.m8B, 8, "m8B")
+    fam("ES", T.mmB, 16, "mmB")
     for i in range(16):
-        ts(T.EV[0:8, i, :], T.mmV[0:8, :], float(i), O.is_equal, "mmV", "EV%d" % i)
-    for i in range(16):
-        ts(T.ES[:, i, :], T.mmB[:], float(i), O.is_equal, "mmB", "ES%d" % i)
-    wr["EV"] = wr["EV15"]
-    wr["ES"] = wr["ES15"]
-    for i in range(16):
-        act(T.Dn[:, i, :], T.BO[:], AF.Copy, "BO RSn", "Dn%d" % i, scale=T.RSn[:, i:i + 1])
-    wr["Dn"] = wr["Dn15"]
-    cu, cf, nz = T.cu, T.cf, T.nz
+        act(T.Dn[:, i, :], m_(BO), AF.Copy, "BO RS", "Dn_%d" % i, scale=T.RS[:, i:i + 1])
+    alias["Dn"] = ["Dn_%d" % i for i in range(16)]
+    alias["Dn8"] = alias["Dn"][0:8]
+    cu, c16, rt = T.cu, T.c16, T.rt
     cp(cu[:], T.cxi[:], "cxi", "cu0 cu1")
-    cp(cf[:], T.cxi[:], "cxi", "cf0 cf1")
-    ts(T.sff[:], T.sfi[:], -2048.0, O.add, "sfi", "sff")
-    ts(nz[:], cf[:], 0.5, O.is_gt, "cf0 cf1", "nz0 nz1", float(TW), O.mult)
-    dma("S", T.TS[15:128:16, TW:TW + W0], T.sff[:], "sff TSF0 TSF1", "TSF")
-    vlist(0)
-    tt(cc(4), T.ip[:], T.im[:], O.is_le, "ip im", "c4")
-    tt(T.PRE[:], T.BO[:], cc(4), O.mult, "BO c4", "PRE")
-    tt(T.ZT[:], T.PRE[:], T.BO[:], O.subtract, "PRE BO", "ZT")
-    for k in range(2 * NCH):
-        sl = slice(k * CH // 2, (k + 1) * CH // 2)
-        ti, tn = T["ti%d" % (k % 2)], "ti%d" % (k % 2)
-        ts(ti[:], T.tk[:, sl], 15, O.bitwise_and, "tk%d" % (k // 2), tn)
-        ts(T.TC[:, sl], ti[:], -D, O.add, tn, "TC_%d" % (k // 2))
+    ts(c16[:], T.cxi[:], -float(CO), O.add, "cxi", "c160 c161")
+    ts(rt[:], T.cxi[:], 0.5, O.is_lt, "cxi", "rt0 rt1")
+    ts(T.sff[:], T.sfi[:], -float(CO), O.add, "sfi", "sff")
+    dma("S", T.TS[0:128:16, TW:TW + W0], T.sff[:], "sff TSF0", "TSF", 110)
+    ts(T.cols[:, 0:1], T.pm[:, 0:1], 0.0, O.add, "pm", "cl0")
+    ts(T.t16[:], T.mmB[:], T.cols[:, 0:1], O.subtract, "mmB cl0", "t16")
+    ts(m_(ID), T.t16[:], 0.0, O.is_equal, "t16", "ID")
+    ts(m_(DL), T.t16[:], 1.0, O.is_equal, "t16", "DL")
+    ts(m_(ZT), T.t16[:], 0.5, O.is_gt, "t16", "ZT")
+    tt(m_(DX), m_(ID), m_(DL), O.subtract, "ID DL", "DX")
+    tt(m_(ZT), m_(ZT), m_(BO), O.mult, "ZT BO", "ZT")
+    act(m_(PRE), m_(ZT), AF.Copy, "ZT", "PRE", scale=-1.0 / 64)
+    act(m_(NI), m_(ID), AF.Copy, "ID", "NI", scale=-1.0)
+    ts(T.cols[:, 1:2], T.pm[:, 0:1], 7.5, O.is_lt, "pm", "cl1", -4096.0, O.mult)
+    ts(T.cols[:, 2:3], T.pm[:, 0:1], 7.5, O.is_gt, "pm", "cl2", -4096.0, O.mult)
+    ts(T.cols[:, 3:4], T.pm[:, 0:1], -8.0, O.add, "pm", "cl3")
+    ts(m_(RL0), T.m8B[:], T.cols[:, 0:1], O.is_equal, "m8B cl0", "RL0", -512.0, O.mult)
+    ts(m_(RL1), T.m8B[:], T.cols[:, 3:4], O.is_equal, "m8B cl3", "RL1", -512.0, O.mult)
+    act(m_(SL0), m_(ID), AF.Copy, "ID cl1", "SL0", scale=T.cols[:, 1:2])
+    act(m_(SL1), m_(ID), AF.Copy, "ID cl2", "SL1", scale=T.cols[:, 2:3])
+    act(m_(NQ), m_(ID), AF.Copy, "ID", "NQ", scale=-1.0 / 1024)
+    fill(sm(0), 0.0, "F")
+    for h in (0, 1):
+        vlist(h, 0)
 
-    def tables2():
-        for k in range(NCH):
-            sl = slice(k * CH, (k + 1) * CH)
-            ts(T.TS[:, sl], T.tk[:, sl], -7.5, O.add, "tk%d" % k, "TS_%d" % k, MAG, O.add)
-            act(T.TS[:, sl], T.TS[:, sl], AF.Identity, "TS_%d" % k, "TS_%d" % k, bias=-(MAG / 16) - 2048.0, scale=1.0 / 16)
-    v_(lambda: V.memset(sm(0), 0.0), "", "F1")
+    NP = W0 // PC
+    for k in range(NP):
+        sl = slice(k * PC, (k + 1) * PC)
+        ti, tn = T.ti[:, PC * (k % 2):PC * (k % 2 + 1)], "ti%d" % (k % 2)
+        ts(ti, T.tk[:, sl], 15, O.bitwise_and, "tk%d" % (k // 2), tn)
+        ts(T.TC[:, sl], ti, -1.0 / 64, O.add, tn, "TC_%d" % k, -D / 64, O.max)
+        act(T.TC[:, sl], T.TC[:, sl], AF.Copy, "TC_%d" % k, "TC_%d" % k, scale=64.0)
+    for k in range(NP):
+        sl = slice(k * PC, (k + 1) * PC)
+        b = k % NB4
+        o = slice(b * PC, (b + 1) * PC)
+        ps, pn = (T.PU, T.PX1)[b // 2][:, 512 * (b % 2):512 * (b % 2) + PC], ("PU0", "PU1", "PX10", "PX11")[b]
+        ts(T.tr[:, o], T.tk[:, sl], -7.5, O.add, "tk%d" % (k // 2), "tr%d" % b, MAG, O.add)
+        act(T.sh[:, o], T.tr[:, o], AF.Identity, "tr%d" % b, "sh%d" % b, bias=-(MAG / 16) - CO, scale=1.0 / 16)
+        mm(acc(ps, [(m_(DX), T.sh[:, o])]), "DX sh%d" % b, pn)
+        act(T.rb[:, o], ps, AF.Identity, pn, "rb%d" % b, bias=R12)
+        mm(acc(ps, [(m_(DX), T.sh[:, o]), (m_(NI), T.rb[:, o])]), "DX NI sh%d rb%d" % (b, b), pn)
+        ts(T.TS[:, sl], ps, R12, O.add, pn, "TS_%d" % k)
 
-    def consts2():
-        tt(T.dif[:], T.im[:], T.ip[:], O.subtract, "im ip", "dif")
-        ts(T.cols[:, 0:1], T.RS[:, 15:16], 800.0, O.mult, "RS", "cl0", -400.0, O.add)
-        ts(T.cols[:, 1:2], T.RS[:, 15:16], 1609800.0, O.mult, "RS", "cl1", -409800.0, O.add)
-        ts(cc(0), T.dif[:], 1.0, O.is_equal, "dif", "c0")
-        ts(cc(1), T.dif[:], -15.0, O.is_equal, "dif", "c1")
-        ts(cc(2), T.dif[:], 0.0, O.is_equal, "dif", "c2")
-        tt(cc(0), cc(0), cc(1), O.add, "c0 c1", "c0")
-        ts(cc(3), T.mm[:], 15.0, O.is_lt, "mm", "c3")
-        tt(cc(0), cc(0), T.BO[:], O.mult, "c0 BO", "c0")
-        tt(cc(2), cc(2), cc(3), O.mult, "c2 c3", "c2")
-        ts(T.BN[:], T.BO[:], T.RS[:, 15:16], O.mult, "BO RS", "BN", 1024.0, O.mult)
-        tt(T.DL[:], cc(0), cc(2), O.subtract, "c0 c2", "DL")
-        ts(T.NI[:], T.dif[:], 0.0, O.is_equal, "dif", "NI", -1.0, O.mult)
-        ts(T.cols[:, 2:3], T.pm[:, 0:1], 0.0, O.add, "pm", "cl2")
-        ts(T.cols[:, 3:4], T.RS[:, 0:1], 64.0, O.mult, "RS", "cl3a")
-        tt(T.cols[:, 4:5], T.cols[:, 3:4], T.RS[:, 1:2], O.add, "cl3a RS", "cl3")
+    fill(T.zz[:], 0.0, "zz")
+    fill(T.inc[:, 0:16], 0.0, "inc")
+    fill(T.nD[:], -D, "nD")
+    ts(T.lkj[:], T.lki[:], 6, O.arith_shift_right, "lki", "lkj")
+    ts(T.lki[:], T.lki[:], 63, O.bitwise_and, "lki", "lki")
+    ts(T.lhf[:], T.lkj[:], -float(CO // 64), O.add, "lkj", "lhf")
+    cp(T.llf[:], T.lki[:], "lki", "llf")
+    dma("S", T.TL[0:128:16, 0:W0], T.lhf[:], "lhf TL", "TLa", 60)
+    dma("S", T.TL[1:128:16, 0:W0], T.llf[:], "llf TL", "TLb", 60)
+    ts(T.mL[:], T.mi[:], T.cols[:, 0:1], O.add, "mi cl0", "mL")
+    ts(T.cols[:, 4:5], T.RS[:, 0:1], 64.0, O.mult, "RS", "cl4")
+    ts(T.LT[:], T.mm[:, 0:16], T.cols[:, 0:1], O.is_gt, "mm cl0", "LT")
+    ts(T.Dm[:], T.mL[:], float(LN), O.add, "mL", "Dm")
+    tt(T.cols[:, 5:6], T.cols[:, 4:5], T.RS[:, 1:2], O.add, "cl4 RS", "cl5")
+    for x in (0, 1):
+        ts(T.dum[:, 16 * x:16 * x + 16], T.mL[:, 0:16], float(DU - 2048), O.add, "mL", "dum%d" % x)
+    ts(T.kL[:, 0:8], T.mL[:, 0:8], 1.0, O.mult, "mL", "kL")
+    ts(T.dus[:], T.dum[:], 1.0 / 4096, O.mult, "dum0 dum1", "dus")
+    tt(m_(ZT), m_(ZT), m_(BO), O.subtract, "ZT BO", "ZT")
+    ts(m_(DD), T.t16[:], -1.0, O.is_equal, "t16", "DD")
+    act(m_(NB), m_(BO), AF.Copy, "BO", "NB", scale=-1.0)
+    tt(m_(DL), m_(ID), m_(DD), O.subtract, "ID DD", "DL")
+    act(T.EW[:], T.ES[:], AF.Copy, "ES cl0", "EW", scale=T.cols[:, 0:1])
+    act(T.EH[:], T.ES[:], AF.Copy, "ES cl5", "EH", scale=T.cols[:, 5:6])
+    for i in range(16):
+        act(T.TR[:, i, :], T.ES[:, i, :], AF.Copy, "ES_%d LT" % i, "TR_%d" % i, scale=T.LT[:, i:i + 1])
+    alias["TR"] = ["TR_%d" % i for i in range(16)]
+    tt(m_(DD), m_(DL), m_(DX), O.add, "DL DX", "DD")
+    ts(T.cols[:, 6:7], T.RS[:, 0:1], -1.0, O.mult, "RS", "cl6")
+    act(m_(IK), m_(ID), AF.Copy, "ID", "IK", scale=1.0 / 4096)
+    for t in range(RO - 1):
+        ts(T.wn[:, B * t:B * t + B], T.mrow[:, 0:256], float(4095 + W0 + B * t - CO), O.add, "mrow", "wr%d" % t)
 
-    def late():
-        v_(lambda: V.memset(T.zz[:], 0.0), "", "zz")
-        ts(T.lkj[:], T.lki[:], 6, O.arith_shift_right, "lki", "lkj")
-        ts(T.lki[:], T.lki[:], 63, O.bitwise_and, "lki", "lki")
-        cp(T.lhf[:], T.lkj[:], "lkj", "lhf")
-        cp(T.llf[:], T.lki[:], "lki", "llf")
-        dma("S", T.TL[0:128:16, 0:W0], T.lhf[:], "lhf TL", "TLa")
-        dma("S", T.TL[1:128:16, 0:W0], T.llf[:], "llf TL", "TLb")
-        ts(cc(3), T.mm[:], 15.0, O.is_equal, "mm", "c3")
-        ts(T.tri[:], T.io3[:], T.cols[:, 2:3], O.is_gt, "io3 cl2", "tri")
-        tt(T.B15[:], T.BO[:], cc(3), O.mult, "BO c3", "B15")
-        ts(T.mL[:], T.mi[:], T.cols[:, 2:3], O.add, "mi cl2", "mL")
-        for i in range(16):
-            ts(T.EW[:, i, :], T.mmB[:], float(i), O.is_equal, "mmB cl2", "EW%d" % i, T.cols[:, 2:3], O.mult)
-            ts(T.EH[:, i, :], T.mmB[:], float(i), O.is_equal, "mmB cl3", "EH%d" % i, T.cols[:, 4:5], O.mult)
-        wr["EW"] = wr["EW15"]
-        wr["EH"] = wr["EH15"]
-        ts(T.Dm[:], T.mL[:], float(LN - 129), O.add, "mL", "Dm")
-        ts(sm(9), T.mL[:, 0:16], float(4096 - 129 - 2047), O.add, "mL", "bz")
-        ts(sm(10), sm(9), 2047.0, O.add, "bz", "bz16", 16.0, O.mult)
-        for i in range(16):
-            act(T.D15[:, i, :], T.B15[:], AF.Copy, "B15 RSn", "D15%d" % i, scale=T.RSn[:, i:i + 1])
-        wr["D15"] = wr["D1515"]
-
-    TCR = "TC TC_0 TC_1 TC_2 TC_3 TCz"
-    TSR = "TS TS_0 TS_1 TS_2 TS_3 TSz TSF TSF0 TSF1"
+    TCR = "TC TCz " + " ".join("TC_%d" % k for k in range(NP))
+    TSR = "TS TSz TSF TSF0 " + " ".join("TS_%d" % k for k in range(NP))
     TLR = "TL TLa TLb"
-    Wt = [W0]
-    PX, PL = (T.PX0, T.PX1), (T.PL0, T.PL1)
+    YBR = "yb " + " ".join("yb%d" % k for k in range(8))
 
-    def K(s, h):
-        return s.replace("@", str(h))
-
-    def HL(h):
-        return slice(1024 * h, 1024 * h + 1024)
+    def HB(h, b):
+        return slice(1024 * h + 512 * b, 1024 * h + 512 * b + 512)
 
     def HC(h):
         return slice(64 * h, 64 * h + 64)
 
-    def S1(h, t, s):
-        win = T.TC[:, 0:Wt[0]].indirect(cu[:, HC(h)])
-        if t == 0 and s == 0:
-            cp(T.q[:, HL(h)], win, TCR + K(" cu@", h), K("q@", h))
-        else:
-            tt(T.q[:, HL(h)], win, T.mk[:, HL(h)], O.mult, TCR + K(" cu@ mk@", h), K("q@", h))
+    def OB(h, b):
+        return slice(64 * h + 32 * b, 64 * h + 32 * b + 32)
 
-    def S2(h):
-        act(T.G[:, HL(h)], T.q[:, HL(h)], AF.Sigmoid, K("q@", h), K("G@", h), bias=-200.0, scale=400.0)
+    def newc(h, y, yn, off):
+        ts(cu[:, HC(h)], y, off + CO, O.add, yn, K("cu@", h))
+        act(c16[:, HC(h)], y, AF.Identity, yn, K("c16@", h), bias=off)
+        act(rt[:, HC(h)], y, AF.Relu, yn, K("rt@", h), bias=1.0 - CO - off, scale=-1.0)
 
-    def S3q(h):
-        listsum(PL[h][:, 0:64], T.ES, T.q, 1024 * h, 1024 * h + 1024, K("q@ ES", h), K("PL@", h))
-        listsum(PL[h][:, 64:128], T.ES, T.q, 1024 * h, 1024 * h + 1024, K("q@ ES", h), K("PL@", h), stop=False)
-
-    def S3G(h):
-        listsum(PL[h][:, 64:128], T.ES, T.G, 1024 * h, 1024 * h + 1024, K("G@ ES", h), K("PL@", h), start=False)
-
-    def S3p(h):
-        def f():
-            for b in (0, 512):
-                x = P.matmul(PX[h][:, b:b + 512], T.PRE[:], T.q[:, 1024 * h + b:1024 * h + b + 512], True, False)
-            return x
-        p_(f, K("q@ PRE", h), K("PX@0 PX@1", h))
-
-    def S4(h, s, o=None):
-        C = HC(h)
-        fill = [] if o is None else S11(o)
-        tt(T.xx[:, C], PL[h][:, 64:128], T.vl[:, 128 * s + 64 * h:128 * s + 64 * h + 64], O.mult, K("PL@ vl", h), K("xx@", h))
-        tt(T.es[:, C], PL[h][:, 0:64], T.xx[:, C], O.is_le, K("PL@ xx@", h), K("es@", h))
-        for f in fill[0:1]:
-            f()
-        tt(T.es[:, C], T.es[:, C], nz[:, C], O.mult, K("es@ nz@", h), K("es@", h))
-        for f in fill[1:2]:
-            f()
-        tt(T.c2f[:, C], cf[:, C], T.es[:, C], O.add, K("cf@ es@", h), K("c2f@", h))
-        tt(T.x2[:, C], T.xx[:, C], T.es[:, C], O.add, K("xx@ es@", h), K("x2@", h))
-        cp(T.cu2[:, C], T.c2f[:, C], K("c2f@", h), K("cu2@", h))
-        for f in fill[2:3]:
-            f()
-        ts(T.th[:, C], T.x2[:, C], 1025.0 - 0.4975, O.add, K("x2@", h), K("th@", h))
-
-    def flist(s):
-        ts(sm(5), T.es[:, 0:16], 0.5, O.is_gt, "es0", "e01")
-        ts(sm(1), cf[:, 0:16], 1.0, O.add, "cf0", "d1")
-        ts(sm(2), sm(0), 0.5, O.is_lt, "F1", "t1")
-        tt(sm(3), sm(2), sm(1), O.mult, "t1 d1", "t2")
-        tt(sm(4), sm(0), sm(3), O.add, "F1 t2", "Fo")
+    def flist(n, s):
+        ts(sm(1), c16[:, 0:16], float(CO + 4096 * (RO * SP + 1 - n)), O.add, "c160", "val")
+        ts(sm(2), T.PL0[:, 256:272], -2100.0, O.is_gt, "PL0.c", "e16")
         if s == SP - 1:
-            tt(sm(2), sm(0), sm(5), O.is_gt, "F1 e01", "t1")
-            tt(sm(6), sm(2), sm(5), O.subtract, "t1 e01", "t2")
-            ts(sm(6), sm(6), 0.5, O.is_gt, "t2", "ca t2")
-            ts(T.kh[:, 32:48], sm(6), -1.0, O.mult, "ca", "kh2")
-        tt(sm(0), sm(4), sm(5), O.mult, "Fo e01", "F1")
-        if s == SP - 2:
-            ts(sm(7), sm(0), -2048.0, O.add, "F1", "kf")
-            ts(T.kh[:, 0:16], sm(7), -1.0, O.mult, "kf", "kh0")
+            cp(T.fi[:, 0:16], sm(0), "F", "fi")
+            ts(sm(3), sm(0), 0.5, O.is_gt, "F", "hf")
+            ts(T.fi[:, 16:32], T.fi[:, 0:16], 4095, O.bitwise_and, "fi", "fj")
+            ts(T.dk[:, 16:32], c16[:, 0:16], float(CO - 2048), O.add, "c160", "dk1")
+            ts(T.dk[:, 0:16], T.fi[:, 16:32], -2048.0, O.add, "fj", "dk0")
+            tt(T.dk[:], T.dk[:], T.dum[:], O.subtract, "dk0 dk1 dum0 dum1", "dk0 dk1")
+            tt(sm(4), sm(3), sm(2), O.is_gt, "hf e16", "ca")
+            for x in (0, 1):
+                tt(T.dk[:, 16 * x:16 * x + 16], T.dk[:, 16 * x:16 * x + 16], sm(4), O.mult, "dk%d ca" % x, "dk%d" % x)
+            tt(T.K[:], T.dk[:], T.dum[:], O.add, "dk0 dk1 dum0 dum1", "K")
+        if n < RO * SP - 1:
+            tt(sm(1), sm(1), sm(0), O.max, "val F", "val")
+            tt(sm(0), sm(1), sm(2), O.mult, "val e16", "F")
 
-    def S5(h):
-        act(T.Sg[:, HL(h)], T.TS[:, 0:TW + Wt[0]].indirect(T.cu2[:, HC(h)]), AF.Copy, TSR + K(" cu2@", h), K("Sg@", h))
+    def ranks(t):
+        tot = T.PL1[:, 0:128]
+        mm(acc(tot, [(m_(BO), T.eb[:])]), "BO eb0 eb1", "PL1.w")
+        mm(acc(T.PL0[:, 128:136], [(m_(IK), T.kL[:, 0:8])] + lsum(T.ES, T.eb, 0, 128)), "IK kL ES eb0 eb1", "PL0.d")
+        mm(acc(T.PL0[:, 0:128], [(m_(ZT), T.eb[:]), (m_(SL0), T.eb[:]), (m_(SL1), T.eb[:]), (m_(ID), T.eb[:])]), "ZT SL0 SL1 ID eb0 eb1", "PL0.w")
+        scan(T.inc[:, 1:129], tot, T.zz[:], O.add, "PL1.w zz", "inc")
+        mm(acc(T.PL0[:, 384:392], lsum(T.ES, T.inc, 0, 128)), "inc ES", "PL0.v")
+        ts(T.tot[:, 0:1], T.inc[:, 128:129], 0.0, O.add, "inc", "tot")
+        send(T.lT[:, 8 * t:8 * t + 1], T.tot[:, 0:1], "T", t, "tot", 1)
+        ts(T.o8[:, 0:8], T.PL0[:, 384:392], 2048.0, O.add, "PL0.v", "o8a", 2.0 ** -16, O.mult)
+        tt(T.X[:], T.inc[:, 1:129], T.PL0[:, 0:128], O.add, "inc PL0.w", "X")
+        tt(T.o8[:, 8:16], T.o8[:, 0:8], T.PL0[:, 128:136], O.min, "o8a PL0.d", "o8b")
+        ts(T.ofu[:], T.o8[:, 8:16], 4096.0, O.mult, "o8b", "ofu")
+        cp(ind(T.MK[:], T.ofu[:]), T.krow[:], "krow ofu", "MK")
+        scan(T.kr[:], T.MK[:, 128:640], T.MK[:, 128:640], O.max, "MK", "kr")
+        if t < RO - 1:
+            zero(T.MK, 0, 640, "MK")
 
-    def P6(h):
-        for b in (0, 1):
-            spread(PX[h], 512 * b, 512, T.Dn, T.th, 64 * h + 32 * b, K("th@ Dn", h), K("PX@%d" % b, h), start=False)
-
-    def S7(h):
-        for b in (0, 1):
-            act(T.cm[:, 1024 * h + 512 * b:1024 * h + 512 * b + 512], PX[h][:, 512 * b:512 * b + 512], AF.Sigmoid, K("PX@%d cl0 cl1" % b, h),
-                K("cm@%d" % b, h), bias=T.cols[:, 1:2], scale=T.cols[:, 0:1])
-
-    def P8(h, ps, lhs, r, w):
-        for b in (0, 1):
-            p_(lambda: P.matmul(ps[:, 512 * b:512 * b + 512], lhs[:], T.cm[:, 1024 * h + 512 * b:1024 * h + 512 * b + 512], True, True),
-               K(r % b, h), K(w % b, h))
-
-    def P8u(h):
-        P8(h, T.PU, T.DL, "cm@%d DL", "PU%d")
-
-    def P8t(h):
-        P8(h, PX[h], T.BN, "cm@%d BN", "PX@%d")
-
-    def S9(h, s):
-        tt(T.Y[:, HL(h)], T.Sg[:, HL(h)], T.PU[:], O.mult, K("Sg@ PU0 PU1", h), K("Y@", h))
-        if s == SP - 1 and h == 0:
-            act(T.uf[:], T.PU[:, 0:256], AF.Copy, "PU0", "uf")
-
-    def S10(h):
-        listsum(PL[h][:, 128:192], T.ES, T.Y, 1024 * h, 1024 * h + 1024, K("Y@ ES", h), K("PL@", h))
-
-    def M(h):
-        tt(T.mk[:, HL(h)], T.q[:, HL(h)], PX[h][:], O.is_lt, K("q@ PX@0 PX@1", h), K("mk@", h))
-
-    def S11(h):
-        C, y = HC(h), PL[h][:, 128:192]
-        return [lambda: ts(cu[:, C], y, 2048.0, O.add, K("PL@", h), K("cu@", h)),
-                lambda: ts(cf[:, C], y, 2048.0, O.add, K("PL@", h), K("cf@", h)),
-                lambda: ts(nz[:, C], y, -2047.5, O.is_gt, K("PL@", h), K("nz@", h), float(TW), O.mult)]
-
-    def eqs(x):
-        def one(k):
-            return lambda: ts(T["EQ%d" % x][:, k, 0:256 - 16 * k], T.R[:, 256 * x + 16 * k:256 * x + 256], T.sm[:, 112 + 16 * x + k:113 + 16 * x + k],
-                              O.is_equal, "R%d %s" % (x, ("kf", "kd")[x]), "E%d_%d" % (x, k))
-        alle = " ".join("E%d_%d" % (x, k) for k in range(16))
-        d = T["EQ%d" % x][:, :, 0:16]
-        return [one(k) for k in range(16)] + [lambda: tt(d, d, T.tri[:], O.mult, alle + " tri", alle)]
-
-    def rows(c, kn, ps, base, key):
-        spread(ps, base, 256, T.Dn, T.kh, c, "Dn " + kn, key)
-
-    def slot(h, t, s, o, so):
-        keyf, keyd, cand = h == 1 and s == SP - 2, h == 0 and s == SP - 1, h == 1 and s == SP - 1
-        eq = eqs(0)[0:9] if keyd else eqs(0)[9:] if cand else []
-        S1(h, t, s)
-        if o is not None:
-            P8u(o)
-        S2(h)
-        S3q(h)
-        if keyd:
-            ts(sm(8), cf[:, 0:16], 1.0 - 2048.0, O.add, "cf0", "kd")
-            ts(T.kh[:, 16:32], sm(8), -1.0, O.mult, "kd", "kh1")
-        for f in eq[0:2]:
-            f()
-        if o is not None:
-            S9(o, so)
-        if h == 1:
-            flist(s)
+    def keys(last):
+        act(T.K16[:], T.K[:], AF.Copy, "K", "K16")
+        mm(spread(T.PX0, 512, 256, T.K16[:, 0:16], 16, True) + spread(T.PX0, 768, 256, T.K16[:, 16:32], 16, True), "K16 Dn", "PX01")
+        act(T.R[:], T.PX0[:, 512:1024], AF.Copy, "PX01", "R")
+        oh = T.PX0[:, 0:256]
+        mm(acc(oh, [(m_(DL), T.s[:, 0:256])]) + ([] if last else acc(T.PX0[:, 256:512], [(m_(DD), T.s[:, 0:256])])), "DL DD s00", "PX00")
+        if last:
+            act(T.nb[:], oh, AF.Identity, "PX00", "nu", bias=1.0, scale=-1.0)
+            act(T.ob[:], oh, AF.Copy, "PX00", "u1")
         else:
-            for f in eq[2:]:
-                f()
-        S3G(h)
-        if o is not None:
-            S10(o)
-            if marks(t, so):
-                P8t(o)
-        S3p(h)
-        if keyf:
-            rows(0, "kh0", T.PU, 0, "PU0")
-        if keyd:
-            rows(16, "kh1", T.PU, 0, "PU0")
-        if t == s == 0 and h == 0:
-            tables2()
-        S4(h, s, o)
-        P6(h)
-        if cand:
-            rows(32, "kh2", T.PL0, 256, "PL0")
-        S5(h)
-        if cand:
-            act(T.cr[:], T.PL0[:, 256:512], AF.Copy, "PL0", "cr")
-        if t == s == 0 and h == 0:
-            consts2()
-        if keyf:
-            cp(T.R[:, 0:256], T.PU[:, 0:256], "PU0", "R0")
-        if keyd:
-            cp(T.R[:, 256:512], T.PU[:, 0:256], "PU0", "R1")
-        if o is not None and marks(t, so):
-            M(o)
-        S7(h)
-        if cand:
-            for f in eq[2:]:
-                f()
-            for k in range(16):
-                act(T.BC[:, k, :], T.BO[:], AF.Copy, "BO ca", "BC%d" % k, scale=T.sm[:, 96 + k:97 + k])
+            act(T.nu[:], oh, AF.Identity, "PX00", "nu", bias=1.0, scale=-1.0)
+            act(T.u1[:], oh, AF.Copy, "PX00", "u1", scale=63.0)
+            act(T.om[:], oh, AF.Identity, "PX00", "om", bias=-128.0 - 1.0 / 64)
+            act(T.dsg[:], T.PX0[:, 256:512], AF.Identity, "PX00 cl6", "dsg", bias=T.cols[:, 6:7])
 
-    def dups(x):
-        def f():
-            for k in range(16):
-                y = P.matmul(PL[x][:, 256 + 16 * k:512], T.BC[:, k, :], T["EQ%d" % x][:, k, 0:256 - 16 * k], k == 0, k == 15)
-            return y
-        p_(f, " ".join("E%d_%d BC%d" % (x, k, k) for k in range(16)), "PL%d" % x)
+    def step(h, t, s):
+        n, wt = SP * t + s, W0 + B * t
+        L, HP = PL[h], slice(128 * h, 128 * h + 128)
+        for b in (0, 1):
+            win = ind(T.TC[:, 0:wt], cu[:, OB(h, b)])
+            if n == 0:
+                cp(T.q[:, HB(h, b)], win, TCR + K(" cu@", h), K("q@#", h, b))
+            else:
+                tt(T.q[:, HB(h, b)], win, T.mk[:, HB(h, b)], O.mult, TCR + K(" cu@ mk@#", h, b), K("q@#", h, b))
+        mm(acc(L[:, 0:128], lsum(T.E8, T.q, 1024 * h, 1024 * h + 1024, 8)), K("q@0 q@1 E8", h), K("PL@.w", h))
+        for b in (0, 1):
+            mm([(PX[h][:, 512 * b:512 * b + 512], m_(PRE), T.q[:, HB(h, b)], True)], K("q@# PRE", h, b), K("PX@#", h, b), True)
+        act(T.p[:, HP], L[:, 0:128], AF.Identity, K("PL@.w", h), K("p@", h), bias=1025.0, scale=1.0 / 64)
+        act(T.xx[:, HP], T.p[:, HP], AF.Identity, K("p@", h), K("xx@", h), bias=65.0 * 1025, scale=-65.0)
+        tt(L[:, 0:128], L[:, 0:128], T.xx[:, HP], O.add, K("PL@.w xx@", h), K("PL@.w", h))
+        tt(T.xx[:, HP], L[:, 0:128], T.vl[:, 256 * s + 128 * h:256 * s + 128 * h + 128], O.mult, K("PL@.w vl@#", h, s), K("xx@", h))
+        act(T.th[:, HP], T.xx[:, HP], AF.Identity, K("xx@", h), K("th@", h), bias=1024.5015)
+        for b in (0, 1):
+            mm(spread(PX[h], 512 * b, 512, T.th[:, 128 * h + 64 * b:128 * h + 64 * b + 64], 8, False), K("th@ Dn8", h), K("PX@#", h, b))
+            act(T.s[:, HB(h, b)], PX[h][:, 512 * b:512 * b + 512], AF.Sigmoid, K("PX@#", h, b), K("s@#", h, b), bias=600.0 * (0.375 - 1025), scale=600.0)
+        mm(acc(L[:, 128:256], [(m_(ID), T.th[:, HP]), (m_(NI), T.p[:, HP])]) +
+           [(L[:, 128 + b:256:2], m_(RL0 + b), rt[:, HC(h)], False) for b in (0, 1)], K("th@ p@ rt@ ID NI RL0 RL1", h), K("PL@.d", h))
+        act(T.cd[:, HP], L[:, 128:256], AF.Sigmoid, K("PL@.d", h), K("cd@", h), bias=-200.0, scale=-400.0)
+        mm(acc(L[:, 256:320], [(m_(ID), c16[:, HC(h)])] + [(m_(SL0 + b), T.cd[:, 128 * h + b:128 * h + 128:2]) for b in (0, 1)]),
+           K("c16@ cd@ ID SL0 SL1", h), K("PL@.c", h))
+        ts(T.cu2[:, HC(h)], L[:, 256:320], float(TW + CO), O.add, K("PL@.c", h), K("cu2@", h))
+        if s == SP - 1:
+            ts(T.eb[:, HC(h)], L[:, 256:320], -2100.0, O.is_gt, K("PL@.c", h), K("eb@", h))
+        else:
+            vlist(h, s + 1)
+        if h == 0:
+            flist(n, s)
+        elif s == SP - 1:
+            ranks(t)
+        for b in (0, 1):
+            tt(T.Y[:, HB(h, b)], ind(T.TS[:, 0:TW + wt], T.cu2[:, OB(h, b)]), T.s[:, HB(h, b)], O.mult, TSR + K(" cu2@ s@#", h, b), K("Y@#", h, b))
+            if n < RO * SP - 1:
+                mm([(T.PU[:, 512 * b:512 * b + 512], m_(NQ), T.q[:, HB(h, b)], True)] +
+                   spread(T.PU, 512 * b, 512, T.cd[:, 128 * h + 64 * b:128 * h + 64 * b + 64], 8, False), K("q@# cd@ NQ Dn8", h, b), K("PU#", h, b))
+                act(T.mk[:, HB(h, b)], T.PU[:, 512 * b:512 * b + 512], AF.Sigmoid, K("PU#", h, b), K("mk@#", h, b), bias=-200.0, scale=400.0 * 1024 / D)
+        y, yn = L[:, 320:384], K("PL@.y", h)
+        mm(acc(y, lsum(T.ES, T.Y, 1024 * h, 1024 * h + 1024)), K("Y@0 Y@1 ES", h), yn)
+        act(T.ry[:, HC(h)], y, AF.Identity, yn, K("ry@", h), bias=R12)
+        cr, cn = T.cr[:, HC(h)], K("cr@", h)
+        tt(cr, y, T.ry[:, HC(h)], O.subtract, K("PL@.y ry@", h), cn)
+        if s < SP - 1:
+            newc(h, cr, cn, R12)
+        else:
+            if h == 0 and t < RO - 1:
+                ts(cu[:, 0:16], T.cr[:, 0:16], R12 + CO, O.add, cn, "cu0")
+            act(T.cf[:, HC(h)], cr, AF.Identity, cn, K("cf@", h), bias=R12)
+            act(c16[:, HC(h)], cr, AF.Identity, cn, K("c16@", h), bias=R12)
 
     def firsts(x):
-        sl = slice(256 * x, 256 * x + 256)
-        tt(T.fr[:, sl], PL[x][:, 256:512], T.cr[:], O.is_lt, "PL%d cr" % x, "fr%d" % x)
-        listsum(PL[x][:, 192:208], T.ES, T.fr, 256 * x, 256 * x + 256, "fr%d ES" % x, "PL%d" % x)
-
-    def offs(x):
-        kk, o, kn = 7 + x, slice(16 * x, 16 * x + 16), ("kf", "kd")[x]
-        tt(T.o1[:, o], sm(kk), sm(9), O.subtract, kn + " bz", "o1%d" % x)
-        tt(T.o2[:, o], T.o1[:, o], PL[x][:, 192:208], O.mult, "o1%d PL%d" % (x, x), "o2%d" % x)
-        tt(T.o1[:, o], T.o2[:, o], sm(10), O.add, "o2%d bz16" % x, "o1%d" % x)
-        ts(T.ou[:, o], T.o1[:, o], 1.0 / 16, O.mult, "o1%d" % x, "ou%d" % x)
+        E, En = T["EQ%d" % x], " ".join("E%d_%d" % (x, k) for k in range(16))
+        for k in range(16):
+            ts(E[:, 256 * k:256 * k + 256 - 16 * k], T.R[:, 256 * x + 16 * k:256 * x + 256], T.K[:, 16 * x + k:16 * x + k + 1],
+               O.is_equal, "R K", "E%d_%d" % (x, k))
+        ps, pn = T.PX1[:, 512 * x:512 * x + 512], "PX1%d" % x
+        mm([(ps[:, 16 * k + 16:256], m_(BO), E[:, 256 * k + 16:256 * k + 256 - 16 * k], k == 0) for k in range(15)], "BO " + En, pn)
+        act(T.du[:, 256 * x + 16:256 * x + 256], ps[:, 16:256], AF.Copy, pn, "du%d" % x)
+        mm(acc(ps[:, 256:272], [(m_(IK), T.K16[:, 16 * x:16 * x + 16])] + [(T.TR[:, i, :], E[:, i:4096:256]) for i in range(16)]), "IK K16 TR " + En, pn, True)
+        mm(acc(ps[:, 257:272], lsum(T.ES, T.du, 256 * x + 16, 256 * x + 256), False), "ES du%d" % x, pn)
+        o = slice(16 * x, 16 * x + 16)
+        tt(T.mo[:, o], ps[:, 256:272], T.dus[:, o], O.min, pn + " dus", "mo%d" % x)
+        ts(T.ou[:, o], T.mo[:, o], 4096.0, O.mult, "mo%d" % x, "ou%d" % x, 2048.0, O.add)
 
     for t in range(RO):
-        last = t == RO - 1
-        iota(T.MK[:], [[0, 640]], 0, 0, "MK")
-        iota(T.H[:, 0:LN], [[0, LN]], 0, 0, "H")
+        last, wt = t == RO - 1, W0 + B * t
+        if last:
+            for k in range(8):
+                o = slice(514 * k, 514 * (k + 1))
+                act(T.yb[:, o], T.TC[:, o], AF.Identity, TCR, "yb%d" % k, bias=128.0, scale=1.0 / 64)
+                ts(T.yb[:, o], T.yb[:, o], -128.0, O.add, "yb%d" % k, "yb%d" % k)
         for s in range(SP):
-            slot(0, t, s, 1 if s else None, s - 1)
-            slot(1, t, s, 0, s)
-            if t == s == 0:
-                late()
+            TAG[0] = "s%d" % (SP * t + s)
+            step(0, t, s)
+            if s == SP - 1:
+                keys(last)
+            step(1, t, s)
+        TAG[0] = "h%d" % t
         if not last:
             loadv("S", t + 1)
-        tot = T.PX0[:, 0:128]
-        ts(T.eb[:], T.es[:], 0.5, O.is_gt, "es0 es1", "eb")
-        p_(lambda: P.matmul(tot, T.BO[:], T.eb[:], True, True), "BO eb", "PX00")
-        p_(lambda: P.matmul(T.PX0[:, 512:640], T.ZT[:], T.eb[:], True, True), "ZT eb", "PX01")
-        v_(lambda: V.tensor_tensor_scan(T.inc[:], tot, T.zz[:], 128.0, O.add, O.add), "PX00 zz", "inc")
-        ts(T.hc[:], tot, 0.5, O.is_gt, "PX00", "hc")
-        tt(T.ha[:], T.inc[:], tot, O.subtract, "inc PX00", "ha")
-        tt(T.X[:], T.inc[:], T.PX0[:, 512:640], O.add, "inc PX01", "X")
-        ts(T.hb[:], T.ha[:], 639.5, O.is_lt, "ha", "hb")
-        tt(T.ha[:], T.ha[:], T.hc[:], O.mult, "ha hc", "ha")
-        tt(T.ha[:], T.ha[:], T.hb[:], O.mult, "ha hb", "ha")
-        tt(T.off[:], T.ha[:], T.krow[:], O.max, "ha krow", "off")
-        listsum(T.PX0[:, 0:8], T.ES, T.off, 0, 128, "off ES", "PX00")
-        P8u(1)
+        lane = T.PX0[:, 0:32]
+        mm(acc(lane, lsum(T.ES, T.kr, 0, 512)), "kr ES", "PX00")
+        ts(T.klu[:], lane, 1.0 / 16, O.mult, "PX00", "klu")
+        tt(T.OH[:], ind(T.X[:], T.klu[:]), T.mrow[:], O.is_equal, "X klu mrow", "OH")
+        tt(T.CG[:], ind(T.cf[:], T.klu[:]), T.OH[:], O.mult, "cf0 cf1 klu OH", "CG")
+        mm(acc(lane, lsum(T.ES, T.kr, 0, 512)), "kr ES", "PX00", True)
+        mm(acc(lane, lsum(T.EW, T.OH, 0, 512), False), "OH EW", "PX00")
+        mm(acc(T.PX0[:, 512:544], lsum(T.ES, T.CG, 0, 512)), "CG ES", "PX01")
         if not last:
-            def f():
-                for b in (0, 512):
-                    P.matmul(T.PX1[:, b:b + 512], T.NI[:], T.q[:, 1024 + b:1536 + b], True, False)
-                    x = P.matmul(T.PX1[:, b:b + 512], T.BN[:], T.cm[:, 1024 + b:1536 + b], False, True)
-                return x
-            p_(f, "q1 cm10 cm11 NI BN", "PX10 PX11")
-        ts(T.tot[:, 0:1], T.inc[:, 127:128], -128.0, O.add, "inc", "tot")
-        send(T["lT%d" % t][:, 0:1], T.tot[:, 0:1], "T", t, "tot")
-        tt(T.X[:], T.X[:], T.eb[:], O.mult, "X eb", "X")
-        eq = eqs(1)
-        for f in eq[0:4]:
-            f()
-        ts(T.ofu[:], T.PX0[:, 0:8], 1.0 / 16, O.mult, "PX00", "ofu")
-        cp(T.MK[:, 0:640].indirect(T.ofu[:]), T.krow[:], "krow ofu", "MK")
-        for f in eq[4:6]:
-            f()
-        v_(lambda: V.tensor_tensor_scan(T.kr[:], T.MK[:, 128:640], T.MK[:, 128:640], 0.0, O.max, O.max), "MK", "kr")
-        S9(1, SP - 1)
-        S10(1)
-        listsum(T.PX0[:, 0:32], T.ES, T.kr, 0, 512, "kr ES", "PX00")
-        dups(0)
-        for f in eq[6:12]:
-            f()
-        if not last:
-            act(T.mk[:, HL(1)], T.PX1[:], AF.Sigmoid, "PX10 PX11", "mk1", bias=-200.0, scale=400.0 / D)
-        act(T.nu[:], T.uf[:], AF.Identity, "uf", "nu", bias=1.0, scale=-1.0)
-        act(T.u1[:], T.uf[:], AF.Copy, "uf", "u1", scale=1.0 - D)
-        for f in S11(1):
-            f()
-        ts(T.klu[:], T.PX0[:, 0:32], 1.0 / 16, O.mult, "PX00", "klu")
-        ts(T.Yl[:], cf[:], -2048.0, O.add, "cf0 cf1", "Yl")
-        tt(T.OH[:], T.X[:].indirect(T.klu[:]), T.mrow[:], O.is_equal, "X klu mrow", "OH")
-        tt(T.CG[:], T.Yl[:].indirect(T.klu[:]), T.OH[:], O.mult, "Yl klu OH", "CG")
-        for f in eq[12:]:
-            f()
-        if not last:
-            listsum(T.PX0[:, 0:32], T.ES, T.kr, 0, 512, "kr ES", "PX00", stop=False)
-            listsum(T.PX0[:, 0:32], T.EW, T.OH, 0, 512, "OH EW", "PX00", start=False)
-            listsum(T.PX0[:, 512:544], T.ES, T.CG, 0, 512, "CG ES", "PX01")
-        else:
-            listsum(T.PX0[:, 512:544], T.ES, T.CG, 0, 512, "CG ES", "PX01")
-            listsum(T.PX0[:, 0:32], T.ES, T.kr, 0, 512, "kr ES", "PX00", stop=False)
-            listsum(T.PX0[:, 0:32], T.EW, T.OH, 0, 512, "OH EW", "PX00", start=False)
+            cp(T.lnu[:], lane, "PX00", "lnu")
+            act(T.MS[:], ind(T.mk[:, 0:LN], T.lnu[:]), AF.Copy, "mk00 mk01 mk10 mk11 lnu", "MS")
+            send(T["lM%d" % t][:], T.MS[:], "M", t, "MS", 128)
+        ts(T.cmu[:], T.PX0[:, 512:544], float(CO), O.add, "PX01", "cmu")
+        act(T.Lg[:], ind(T.TL[:, 0:wt], T.cmu[:]), AF.Copy, TLR + " cmu", "Lg")
+        send(T["lL%d" % t][:], T.Lg[:], "L", t, "Lg", 128)
         firsts(0)
-        dups(1)
-        if not last:
-            cp(T.lnu[:], T.PX0[:, 0:32], "PX00", "lnu")
-            act(T.MS[:], T.mk[:, 0:LN].indirect(T.lnu[:]), AF.Copy, "mk0 mk1 lnu", "MS")
-            send(T["lM%d" % t][:], T.MS[:], "M", t, "MS")
-        ts(T.cmu[:], T.PX0[:, 512:544], 2048.0, O.add, "PX01", "cmu")
-        act(T.Lg[:], T.TL[:, 0:Wt[0]].indirect(T.cmu[:]), AF.Copy, TLR + " cmu", "Lg")
-        send(T["lL%d" % t][:], T.Lg[:], "L", t, "Lg")
-        offs(0)
         firsts(1)
-        act(T.lnf[:], T.PX0[:, 0:32], AF.Copy, "PX00", "lnf")
-        wb = slice(W0 + B * t, W0 + B * (t + 1))
-        wf = slice(TW + W0 + B * t, TW + W0 + B * (t + 1))
-        if not last:
-            act(T.TS[:, wb], T.TS[:, 0:Wt[0]].indirect(cu[:, 0:16]), AF.Copy, TSR + " cu0", "TS")
-            act(T.TL[:, wb], T.TL[:, 0:Wt[0]].indirect(cu[:, 0:16]), AF.Copy, TLR + " cu0", "TL")
-            ts(T.kh[:, 48:64], T.Yl[:, 0:16], -1.0, O.mult, "Yl", "kh3")
-            spread(T.PU, 0, 256, T.D15, T.kh, 48, "D15 kh3", "PU0")
-            act(T.TS[:, wf], T.PU[:, 0:256], AF.Copy, "PU0", "TS")
-            tt(T.uw[:], T.uf[:], T["wr%d" % t][:], O.mult, "uf wr%d" % t, "uw")
-        v_(lambda: V.tensor_scalar(T.rr[:], T.TC[:, 0:Wt[0]].indirect(cu[:, 0:16]), 0.5, 0.25, O.mult, O.add), TCR + " cu0", "rr")
-        offs(1)
-        tt(T.r2[:], T.rr[:], T.fr[:, 0:256], O.mult, "rr fr0", "r2")
-        if not last:
-            vlist(t + 1)
-        ts(T.TC[:, wb], T.r2[:], -D, O.add, "r2", "TC")
-        tt(T.aC[:], T.TC[:].indirect(T.ou[:, 0:16]), T.nu[:], O.mult, TCR + " ou0 nu", "aC")
-        tt(T.TC[:].indirect(T.ou[:, 0:16]), T.aC[:], T.u1[:], O.add, "aC u1 ou0", "TC")
-        if not last:
-            tt(T.aS[:], T.TS[:, 0:TW].indirect(T.ou[:, 0:16]), T.nu[:], O.mult, TSR + " ou0 nu", "aS")
-            tt(T.TS[:, 0:TW].indirect(T.ou[:, 0:16]), T.aS[:], T.uw[:], O.add, "aS uw ou0", "TS")
-        tt(T.aC[:], T.TC[:].indirect(T.ou[:, 16:32]), T.uf[:], O.add, TCR + " ou1 uf", "aC")
-        ts(T.aC[:], T.aC[:], 15.0 - D, O.min, "aC", "aC")
-        cp(T.TC[:].indirect(T.ou[:, 16:32]), T.aC[:], "aC ou1", "TC")
-        Wt[0] += B
+        wb = slice(wt, wt + B)
+        of, od = T.ou[:, 0:16], T.ou[:, 16:32]
+        ts(sm(5), T.mo[:, 0:16], (DU - 2048.5) / 4096, O.is_gt, "mo0", "nf", 8192.0, O.mult)
+        tt(sm(5), sm(5), c16[:, 0:16], O.add, "nf c160", "nf")
+        ts(T.su[:], sm(5), float(CO), O.add, "nf", "su", float(TW), O.min)
         if last:
-            for k in range(4):
-                for b in (0, 1):
-                    o = slice(1024 * k + 512 * b, 1024 * k + 512 * b + 512)
-                    if b or k == 3:
-                        act(T.yb[:, o], T.TC[:, o], AF.Relu, TCR, "yb%d%d" % (k, b))
-                    else:
-                        ts(T.yb[:, o], T.TC[:, o], 0.0, O.max, TCR, "yb%d%d" % (k, b))
-                o = slice(1024 * k, 1024 * k + 1024)
-                dma("S", T.yn[:, o], T.yb[:, o], "yb%d0 yb%d1" % (k, k), "yn%d" % k)
-        tt(T.tot[:, 1:2], T.tot[:, 0:1], T["lT%d" % t][:, 0:1], O.min, "tot lT%d" % t, "tm1")
-        tt(T.so[:], T.lnf[:], T.Dm[:], O.subtract, "lnf Dm", "so")
-        ts(T.tot[:, 2:3], T.tot[:, 1:2], float(CAP), O.min, "tm1", "tm2", 128.0, O.add)
-        tm = T.tot[:, 2:3]
-        ts(T.vd[:], T.mL[:], tm, O.is_le, "mL tm2", "vd")
-        ts(T.mvv[:], T.X[:], tm, O.is_le, "X tm2", "mvv")
-        tt(T.so[:], T.so[:], T.vd[:], O.mult, "so vd", "so")
-        tt(T.mvv[:], T.mvv[:], T.eb[:], O.mult, "mvv eb", "mvv")
-        tt(T.so[:], T.so[:], T.Dm[:], O.add, "so Dm", "so")
-        ts(T.nmv[:], T.mvv[:], -1.0, O.mult, "mvv", "nmv", 1.0, O.add)
+            act(T.Cc[:], ind(T.yb[:], T.su[:]), AF.Identity, YBR + " su", "Cc", bias=128.25, scale=0.5)
+            tt(T.ab[:], ind(T.yb[:], of), T.nb[:], O.mult, YBR + " ou0 nu", "ab")
+            tt(ind(T.yb[:], of), T.ab[:], T.ob[:], O.add, "ab u1 ou0", "yb")
+            tt(T.ab[:], ind(T.yb[:], od), T.ob[:], O.add, YBR + " ou1 u1", "ab")
+            ts(T.ab[:], T.ab[:], 15.0, O.min, "ab", "ab")
+            cp(ind(T.yb[:], od), T.ab[:], "ab ou1", "yb")
+            ts(T.yb[:, wb], T.Cc[:], -128.0, O.add, "Cc", "yb")
+            for k in range(2):
+                o = slice(2048 * k, 2048 * k + 2048)
+                dma("SA"[k], T.yn[:, o], T.yb[:, o], YBR, "yn%d" % k, 512 * (k + 1))
+        else:
+            act(T.TS[:, wb], ind(T.TS[:, 0:wt], cu[:, 0:16]), AF.Copy, TSR + " cu0", "TS")
+            act(T.TL[:, wb], ind(T.TL[:, 0:wt], cu[:, 0:16]), AF.Copy, TLR + " cu0", "TL")
+            mm(spread(T.PU, 0, 256, c16[:, 0:16], 16, True), "c160 Dn", "PU0")
+            act(T.TS[:, TW + wt:TW + wt + B], T.PU[:, 0:256], AF.Copy, "PU0 RS", "TSF", scale=T.RS[:, 0:1])
+            act(T.Cc[:], ind(T.TC[:], T.su[:]), AF.Identity, TCR + " su", "Cc", bias=128.26, scale=1.0 / 128)
+            tt(T.aC[:], ind(T.TC[:], of), T.nu[:], O.mult, TCR + " ou0 nu", "aC")
+            tt(ind(T.TC[:], of), T.aC[:], T.u1[:], O.add, "aC u1 ou0", "TC")
+            act(T.Cb[:], ind(T.TC[:], od), AF.Identity, TCR + " ou1", "Cb", bias=128.0, scale=1.0 / 64)
+            ts(T.aF[:], T.Cc[:], -128.0 - 1.0 / 64, O.add, "Cc", "aF", -D / 64, O.max)
+            act(T.TC[:, wb], T.aF[:], AF.Copy, "aF", "TC", scale=64.0)
+            tt(T.aC[:], T.Cb[:], T.om[:], O.add, "Cb om", "aC")
+            ts(T.aC[:], T.aC[:], 15.0 - 1.0 / 64, O.min, "aC", "aC", 64.0, O.mult)
+            tt(ind(T.TC[:], od), T.aC[:], T.nD[:], O.max, "aC nD ou1", "TC")
+            tt(T.Yf[:], ind(T.TS[:, 0:TW], of), T.s[:, 0:256], O.mult, TSR + " ou0 s00", "Yf")
+            mm(acc(T.PU[:, 0:256], [(m_(ID), T.wn[:, B * t:B * t + B]), (m_(NB), T.Yf[:])]), "ID NB Yf wr%d" % t, "PU0")
+            tt(T.aD[:], T.PU[:, 0:256], T.dsg[:], O.mult, "PU0 dsg", "aD")
+            tt(T.aE[:], ind(T.TS[:, 0:TW], of), T.aD[:], O.add, TSR + " ou0 aD", "aE")
+            act(T.r2[:], T.aE[:], AF.Identity, "aE", "r2", bias=R12)
+            act(T.aD[:], T.r2[:], AF.Identity, "r2", "aD", bias=-R12)
+            tt(ind(T.TS[:, 0:TW], of), T.aE[:], T.aD[:], O.subtract, "aE aD ou0", "TS")
+            for h in (0, 1):
+                vlist(h, 0)
+        tt(T.tot[:, 1:2], T.tot[:, 0:1], T.lT[:, 8 * t:8 * t + 1], O.min, "tot lT%d" % t, "tm1")
+        ts(T.tot[:, 2:3], T.tot[:, 1:2], float(CAP), O.min, "tm1", "tm2", -0.5, O.add)
+        ts(T.tot[:, 3:4], T.tot[:, 1:2], float(CAP), O.min, "tm1", "tm3", 0.5 - 4096, O.add)
+        ts(T.so[:], T.mL[:], T.tot[:, 2:3], O.is_gt, "mL tm2", "so", 4096.0, O.mult)
+        ts(T.nmv[:], T.X[:], T.tot[:, 3:4], O.is_gt, "X tm3", "nmv")
+        tt(T.so[:], T.so[:], lane, O.add, "so PX00", "so")
+        tt(T.cm[:], c16[:], T.nmv[:], O.mult, "c160 c161 nmv", "cm")
+        tt(T.so[:], T.so[:], T.Dm[:], O.min, "so Dm", "so")
+        if not last:
+            tt(sm(0), sm(0), T.nmv[:, 0:16], O.mult, "F nmv", "F")
         cp(T.sou[:], T.so[:], "so", "sou")
-        tt(cf[:], cf[:], T.nmv[:], O.mult, "cf0 cf1 nmv", "cf0 cf1")
-        if not last:
-            tt(sm(0), sm(0), T.nmv[:, 0:16], O.mult, "F1 nmv", "F1")
-        cp(T.H[:].indirect(T.sou[:]), T["lL%d" % t][:], "sou lL%d" % t, "H")
-        listsum(T.PX0[:, 0:128], T.EH, T.H, 0, LN, "EH H", "PX00")
-        if not last:
-            cp(T.mk[:].indirect(T.sou[:]), T["lM%d" % t][:], "sou lM%d" % t, "mk0 mk1")
-        tt(cf[:], cf[:], T.PX0[:, 0:128], O.add, "cf0 cf1 PX00", "cf0 cf1")
-        if not last:
-            cp(cu[:], cf[:], "cf0 cf1", "cu0 cu1")
-            ts(nz[:], cf[:], 0.5, O.is_gt, "cf0 cf1", "nz0 nz1", float(TW), O.mult)
-    dma("A", T.yc[:, :], cf[:], "cf0 cf1", "yc")
-    for s in sorted(left):
-        if seen["G"].get(s, 0) < left[s]:
-            g.wait_ge(T.sem[s], left[s])
+        cp(ind(T.H[:], T.sou[:]), T["lL%d" % t][:], "sou lL%d" % t, "H")
+        for h in (0, 1):
+            mm(acc(PL[h][:, 320:384], [(m_(ID), T.cm[:, HC(h)])] + lsum(T.EH, T.H, 1024 * h, 1024 * h + 1024)), "ID cm EH H", K("PL@.y", h))
+        if last:
+            for h in (0, 1):
+                ts(T.cf[:, HC(h)], PL[h][:, 320:384], float(CO), O.add, K("PL@.y", h), K("cf@", h))
+            dma("A", T.yc[:, :], T.cf[:], "cf0 cf1", "yc", 64)
+        else:
+            zero(T.H, 0, LN, "H")
+            cp(ind(T.mk[:], T.sou[:]), T["lM%d" % t][:], "sou mkz lM%d" % t, "mk00 mk01 mk10 mk11")
+            for h in (0, 1):
+                newc(h, PL[h][:, 320:384], K("PL@.y", h), 0.0)
+    issue()

@@ -1,16 +1,23 @@
 from concourse.mybir import AluOpType as O, ActivationFunctionType as AF
 
 W0, B, LN, RO, SP, CAP = 3328, 256, 2048, 3, 3, 512
+CS = CAP + 16
 TW = 4096
 CO = 1920
 DU = 3840
-D = 2.0 ** -14
+D = 2.0 ** -13
+KC = 63.0
+PLAN = dict(V="q00 q01 a1- p00 u1- T00 q10 p01 x00 T01 x01 q11 p10 T10 x10 f0 p11 T11 x11 o0 Y01 g0 Y00 o1 Y10 Y11 a0 u0",
+            A="m01- m10- R0- r1- m11- t00 t01 R1- e0 s01 t10 t11 s00 e1 s10 s11 m00 r0",
+            P="M10- y1- W00 M11- W01 U01 U00 W10 U10 d0 X01 W11 c0 X00 X10 d1 U11 X11 c1 M00 y0 M01")
+UNITS = ((0, 1),)
+MKV = ()
 MAG = 1.5 * 2.0 ** 27
 R12 = 1.5 * 2.0 ** 19
 NCH, CH = 4, 832
 PC, NB4 = 416, 4
 TAG = [""]
-EST = dict(cy=0.83e-3, pe=0.42e-3, ga=1.5, sc=3.5, call=0.03, wait=0.08, dma=1.3, rem=2.0, turns=4)
+EST = dict(cy=0.83e-3, pe=0.42e-3, ga=1.56, two=0.0, sc=3.8, call=0.03, act=0.02, own=0.04, wait=0.24, dma=1.0, rem=1.8, turns=8)
 ORDER = []
 
 
@@ -20,21 +27,21 @@ def _sb(dtype, **shapes):
 
 SCRATCH = {}
 SCRATCH.update(_sb("int32", tk=W0, ti=2 * PC, ip=128, im=128, pg=128, mg=128, pm=128, mm=128, m8=128, sfi=208, lki=208, lkj=208, cxi=128, fi=32))
-SCRATCH.update(_sb("float32", TC=TW + 16, TS=TW + DU, tr=NB4 * PC, vl=768, xx=256, MK=2192, sm=192, RS=16, LT=16, mrow=512, krow=128, mi=32, mL=32, Dm=32,
-                   zz=128, cols=8, sff=208, cf=128, cr=128, X=128, K=32, dk=32, dum=32, dus=32, mo=32, nu=256, u1=256, om=256, dsg=256, nD=256, aC=256, aD=256, aE=256,
-                   aF=256, tot=8, lT=24, so=32, nmv=128, o8=16))
-SCRATCH.update(_sb("bfloat16", vvr=SP * LN, s=LN, mk=LN + CAP, H=LN + CAP, EQ0=4096, EQ1=4096, yb=TW + 16, TL=4096, ES=-16, Dn=-16, E8=-8, EV=-8,
-                   EW=-16, EH=-16, TR=-16, M=-16, cd=256, rt=128, ry=128, rb=NB4 * PC, eb=128, du=512, lhf=208, llf=208, Cb=256, Cc=256, nb=256, ob=256, ab=256, r2=256,
-                   OH=512, MS=512, Lg=512, lM0=512, lM1=512, lL0=512, lL1=512, lL2=512))
-SCRATCH.update(_sb("float16", q=LN, Y=LN, p=256, th=256, c16=128, cm=128, sh=NB4 * PC, mmB=128, m8B=128, mmV=128, t16=128, o64=128, K16=32, R=512, inc=144,
+SCRATCH.update(_sb("float32", TC=TW + 16, TS=TW + DU, tr=NB4 * PC, vl=768, xx=256, MK=2192, sm=192, RS=16, mrow=512, krow=128, mi=128, mL=128, Dm=128,
+                   zz=128, cols=8, sff=208, cf=128, cr=128, I32=128, X=128, K=32, dk=32, dum=32, dus=32, mo=32, nu=256, u1=256, om=256, dsg=256, nD=256, aC=256, aD=256, aE=256,
+                   aF=256, tot=8, lT=24, so=128, o8=16))
+SCRATCH.update(_sb("bfloat16", vvr=SP * LN, s=LN, mk0=LN + CS, mk1=LN + CS, H=LN, nmv=128, EQ0=4096, EQ1=4096, yb=TW + 16, TL=4096, ES=-16, Dn=-16, E8=-8, EV=-8,
+                   EW=-16, n128=1040, TR=-16, M=-19, one=16, cd=256, rt=128, ry=128, rb=NB4 * PC, eb=128, du=512, lhf=208, llf=208, Cb=256, Cc=256, nb=256, ob=256, ab=256, r2=256,
+                   OH=512, MS=512, Lg=512, mk2=CS))
+SCRATCH.update(_sb("float16", q=LN, Y=LN, p=256, th=256, c16=16, cm=128, X16=128, k1=64, sh=NB4 * PC, mmB=128, m8B=128, mmV=128, t16=128, o64=128, K16=32, R=512, inc=144,
                    kL=16, kr=512, CG=512, Yf=256, wn=512))
-SCRATCH.update(_sb("uint16", cu=128, cu2=128, ou=32, su=16, ofu=8, klu=32, cmu=32, lnu=32, sou=32))
-SCRATCH.update({k: ("psum", [128, n], "float32") for k, n in (("PX0", 1024), ("PX1", 1024), ("PU", 1024), ("PL0", 512), ("PL1", 512))})
+SCRATCH.update(_sb("uint16", cu=128, cu2=128, ou=32, su=16, ofu=8, klu=32, cmu=32, lnu=32, hu=128, mu=128))
+SCRATCH.update({k: ("psum", [128, n], "float32") for k, n in (("PX0", 1024), ("PX1", 1024), ("PL0", 1024), ("PL1", 1024))})
 DMAS = ["d%d" % i for i in range(24)]
-REM = [a + str(t) for t in range(RO) for a in ("aT", "aM", "aL", "nT", "nM", "nL") if not (t == RO - 1 and a[1] == "M")]
+REM = [a + str(t) for t in range(RO) for a in ("aT", "aL", "nT", "nL")]
 SEMAPHORES = ["sV", "sA", "sP", "sG"] + DMAS + REM
-BANKS = {"PX00", "PX01", "PX10", "PX11", "PU0", "PU1", "PL0", "PL1"}
-BO, PRE, DX, ID, NI, NQ, I65, RL0, RL1, SL0, SL1, ZT, DL, DD, NB, IK = range(16)
+BANKS = {"PX00", "PX01", "PX10", "PX11", "PL00", "PL01", "PL10", "PL11"}
+BO, PRE, DX, ID, NI, NQ, N2, RL0, RL1, SL0, SL1, ZT, DL, DD, NB, IK, P4, SB0, SB1 = range(19)
 
 
 def bank(k):
@@ -48,19 +55,27 @@ def order(ops):
         p = {}
         for k in o["r"]:
             if k in wr:
-                p[wr[k]] = 1
+                p[wr[k]] = max(p.get(wr[k], 0), k[0] != "*")
         for k in o["w"]:
             for j in rd.get(k, []) + ([wr[k]] if k in wr and o["q"] == "P" else []):
                 p.setdefault(j, 0 if ops[j]["q"] == o["q"] == "P" else 1)
             if k in wr:
-                p.setdefault(wr[k], 1)
+                p.setdefault(wr[k], -1 if k[0] == "~" else 1)
         p.pop(n, None)
+        p = {j: EST["own"] / EST["wait"] if w == 1 and ops[j]["q"] == o["q"] and ops[j]["sem"] is None else w for j, w in p.items()}
         pre.append(p)
         for k in o["r"]:
             rd.setdefault(k, []).append(n)
         for k in o["w"]:
             wr[k], rd[k] = n, []
     N = len(ops)
+    named = {o["lab"]: n for n, o in enumerate(ops)}
+    for plan in PLAN.values():
+        seq = [named.get((n - (x[-1] == "-"), x.strip("-"))) for n in range(RO * SP + 1)
+               for x in sorted(plan.split(), key=lambda x: n % SP == 0 and x[-1] != "-")]
+        seq = [n for n in seq if n is not None]
+        for j, n in zip(seq, seq[1:]):
+            pre[n].setdefault(j, -1)
     suc = [{} for _ in ops]
     for n, p in enumerate(pre):
         for j, w in p.items():
@@ -70,7 +85,7 @@ def order(ops):
         st, busy = [0.0] * N, {}
         for n in seq:
             o = ops[n]
-            t = max([st[j] + ops[j]["c"] + ops[n if back else j]["lat"] + EST["wait"] * w for j, w in dep[n].items()], default=o["lat"] if back else 0.0)
+            t = max([st[j] + ops[j]["c"] + (0.0 if w < 0 else ops[n if back else j]["lat"] + EST["wait"] * w) for j, w in dep[n].items()], default=o["lat"] if back else 0.0)
             res = [(o["q"], 0.0)] + [(b, EST["wait"]) for b in o["b"]]
             moved = True
             while moved:
@@ -91,9 +106,16 @@ def order(ops):
 
     def end(st):
         return max(st[n] + ops[n]["c"] + ops[n]["lat"] for n in range(N))
+    todo = [len(p) for p in pre]
+    top = [n for n in range(N) if not todo[n]]
+    for n in top:
+        for j in suc[n]:
+            todo[j] -= 1
+            if not todo[j]:
+                top.append(j)
     way = [0.0] * N
-    for n in range(N - 1, -1, -1):
-        way[n] = ops[n]["c"] + ops[n]["lat"] + max([way[j] + EST["wait"] for j in suc[n]], default=0.0)
+    for n in top[::-1]:
+        way[n] = ops[n]["c"] + max([ops[n]["lat"]] + [way[j] + (0.0 if w < 0 else ops[n]["lat"] + EST["wait"] * w) for j, w in suc[n].items()])
     st = best = place(sorted(range(N), key=lambda n: (-way[n], n)), pre, False)
     for _ in range(EST["turns"]):
         bk = place(sorted(range(N), key=lambda n: (-(st[n] + ops[n]["c"] + ops[n]["lat"]), -n)), suc, True)
@@ -110,12 +132,13 @@ def rank_program(g, core, T, topo):
         return
     V, A, P, S = g.vector, g.scalar, g.tensor, g.sync
     eng = {"V": V, "A": A, "P": P, "S": S, "G": g}
-    ops, alias, ndma = [], {}, [0]
+    ops, alias, ndma, label = [], {}, [0], [None]
 
     def run(qn, fn, r, w, c, sem=None, remote=False, n=1, lat=0.0):
         r = [x for k in r.split() for x in alias.get(k, [k])]
         w = w.split()
-        ops.append(dict(q=qn, fn=fn, r=r, w=w, c=c, sem=sem, remote=remote, n=n, lat=lat, b={bank(k) for k in r + w} - {None}, tag=TAG[0]))
+        ops.append(dict(q=qn, fn=fn, r=r, w=w, c=c, sem=sem, remote=remote, n=n, lat=lat, b={bank(k) for k in r + w} - {None}, tag=TAG[0], lab=label[0]))
+        label[0] = None
 
     def issue():
         seen = {k: {} for k in eng}
@@ -135,7 +158,7 @@ def rank_program(g, core, T, topo):
             for k in o["r"]:
                 want(wr.get(k, {}), qn == "P" and k[0] == "*")
             for k in o["w"]:
-                want(wr.get(k, {}), qn == "P")
+                want(wr.get(k, {}) if k[0] != "~" else {}, qn == "P")
                 want(rd.get(k, {}), qn == "P")
             for b in o["b"]:
                 want(bk.get(b, {}), True)
@@ -179,7 +202,7 @@ def rank_program(g, core, T, topo):
         if isinstance(out, tuple):
             return 0.05 + out[1] * EST["sc"] * EST["cy"]
         if ins and isinstance(ins[0], tuple):
-            return 0.05 + ins[0][1] * EST["ga"] * EST["cy"]
+            return 0.05 + ins[0][1] * (EST["ga"] + two * EST["two"]) * EST["cy"]
         ps = any(bank(k) for k in (r + " " + w).split())
         rate = (1.0 if ps else 2.0) if two else 0.5 if fast and all("16" in str(a.dtype) for a in [out] + ins) else 1.0
         return EST["call"] + max(64, size(out) * rate) * EST["cy"]
@@ -187,10 +210,11 @@ def rank_program(g, core, T, topo):
     def ap(x):
         return x[0] if isinstance(x, tuple) else x
 
-    def dma(qn, out, in_, r, w, kb):
+    def dma(qn, out, in_, r, w, kb, add=False):
         s = DMAS[ndma[0]]
         ndma[0] += 1
-        run(qn, lambda: eng[qn].dma_start(out, in_), r, w, 0.05, sem=s, n=16, lat=EST["dma"] + kb / 180.0)
+        more = dict(accum_op=O.add) if add else {}
+        run(qn, lambda: eng[qn].dma_start(out, in_, **more), r, w, 0.05, sem=s, n=16, lat=EST["dma"] + kb / 180.0)
 
     def ts(out, in0, s1, op0, r, w, s2=None, op1=None):
         c = cost(out, [in0], r, w)
@@ -212,7 +236,8 @@ def rank_program(g, core, T, topo):
         run("V", lambda: V.tensor_tensor_scan(out, a, b, 0.0, op, op), r, w, cost(out, [a], r, w, fast=False))
 
     def act(out, in_, func, r, w, bias=0.0, scale=1.0):
-        run("A", lambda: A.activation(out, ap(in_), func, bias=bias, scale=scale), r, w, cost(out, [in_], r, w, fast=False))
+        run("A", lambda: A.activation(out, ap(in_), func, bias=bias, scale=scale), r, w,
+            cost(out, [in_], r, w, fast=False) + (0.0 if isinstance(in_, tuple) else EST["act"]))
 
     def mm(group, r, w, more=False):
         def f():
@@ -221,7 +246,7 @@ def rank_program(g, core, T, topo):
             return i
         star = " ".join({"*" + bank(k) for k in w.split()})
         c = sum(max(64, size(x)) for o, l, x, st in group) * EST["pe"]
-        if group[0][3]:
+        if more or not group[0][3]:
             run("P", f, r, w + " " + star, c)
         else:
             run("P", f, r + " " + star, w, c)
@@ -246,7 +271,7 @@ def rank_program(g, core, T, topo):
     def send(dst, src, name, t, r, kb):
         s, rs = "n%s%d" % (name, t), "a%s%d" % (name, t)
         run("G", lambda: g.remote_dma(dst, src, T.sem[rs], T.sem[s], pid, rid, emask), r, "l%s%d" % (name, t), 0.1, sem=s, remote=True, n=ne,
-            lat=EST["rem"] + kb / 60.0 + (2.0 if t == 0 and name == "T" else 0.0))
+            lat=EST["rem"] + kb / 45.0 + (2.0 if t == 0 and name == "T" else 0.0))
 
     def sm(k):
         return T.sm[:, 16 * k:16 * k + 16]
@@ -260,18 +285,18 @@ def rank_program(g, core, T, topo):
         return s.replace("@", str(h)).replace("#", str(b))
 
     def vlist(h, s):
-        lo = LN * s + 1024 * h
-        mm(acc(PL[h][:, 384:512], [(T.EV[0:8, j, :], T.vvr[0:8, lo + j:lo + 1024:8]) for j in range(8)]), "EV vvr", K("PL@.v", h))
-        act(T.vl[:, 256 * s + 128 * h:256 * s + 128 * h + 128], PL[h][:, 384:512], AF.Copy, K("PL@.v", h), K("vl@#", h, s), scale=-1.0 / 256)
+        lo, o, on = LN * s + 1024 * h, PL[h][:, 896 - 512 * (s % 2):1024 - 512 * (s % 2)], K("PL@#.v", h, 1 - s % 2)
+        mm(acc(o, [(T.EV[0:8, j, :], T.vvr[0:8, lo + j:lo + 1024:8]) for j in range(8)]), "EV vvr", on)
+        act(T.vl[:, 384 * h + 128 * s:384 * h + 128 * s + 128], o, AF.Copy, on, K("vl@#", h, s), scale=0.25)
 
     loadv("A", 0)
     for k in range(NCH):
-        dma("S", T.tk[:, k * CH:(k + 1) * CH], T.tab[:, k * CH:(k + 1) * CH], "ld%d" % k, "tk%d ld%d" % (k, k + 1), 100 + 430 * (k + 1))
-        ops[-1]["r"], ops[-1]["w"] = [], ["tk%d" % k]
+        dma("S", T.tk[:, k * CH:(k + 1) * CH], T.tab[:, k * CH:(k + 1) * CH], "", "~S tk%d" % k, 100 + 430 * (k + 1) + (70 if k > 0 else 0))
         if k == 0:
-            dma("S", T.cxi[:], T.cx[:, :], "", "cxi", 600)
-            dma("S", T.sfi[:], T.suf[:, :], "", "sfi", 700)
-    dma("S", T.lki[:], T.lnk[:, :], "", "lki", 2000)
+            dma("S", T.cxi[:], T.cx[:, :], "", "~S cxi", 600)
+        if k == 3:
+            dma("S", T.sfi[:], T.suf[:, :], "", "~S sfi", 2000)
+    dma("S", T.lki[:], T.lnk[:, :], "", "~S lki", 2100)
 
     def iota(out, pat, base, cm, w, small=True):
         c = 0.13 + 2 * size(out) * EST["cy"]
@@ -279,6 +304,9 @@ def rank_program(g, core, T, topo):
             run("G", lambda: g.iota(out, pat, base, cm, allow_small_or_imprecise_dtypes=True), "", w, c)
         else:
             run("G", lambda: g.iota(out, pat, base, cm), "", w, c)
+
+    def select(out, in_, pat, op, x, base, cm, r, w):
+        run("G", lambda: g.affine_select(out, in_, pat, op, x, base, cm), r, w, 0.17 + 2 * size(out) * EST["cy"])
 
     def zero(buf, lo, hi, w, n=1):
         st = (hi - lo) // n
@@ -291,17 +319,18 @@ def rank_program(g, core, T, topo):
     zero(T.TC, W0, TW + 16, "TCz")
     zero(T.TS, TW, TW + DU, "TSF0")
     zero(T.TS, W0, TW, "TSz")
-    iota(T.mi[:], [[16, 32]], 0, 0, "mi")
+    iota(T.mi[:], [[16, 128]], 0, 0, "mi")
     iota(T.krow[:], [[1, 128]], 0, 0, "krow")
     zero(T.MK, 0, 2192, "MK")
-    zero(T.TL, 0, 4096, "TL")
-    iota(T.mrow[:], [[1, 512]], 1 - 4096, 0, "mrow")
-    zero(T.H, 0, LN + CAP, "H")
-    zero(T.mk, LN, LN + CAP, "mkz")
+    iota(T.TL[:], [[0, 4096]], 1, 0, "TL")
+    iota(T.mrow[:], [[1, 512]], 1 - 2048, 0, "mrow")
+    zero(T.zz, 0, 128, "zz")
+    iota(sm(0), [[0, 16]], -900000, 0, "F")
+    iota(T.one[:], [[0, 16]], 1, 0, "one")
 
-    def fam(name, key, n, kn, rows=128):
+    def fam(name, key, n, kn, rows=128, x=1.0):
         for i in range(n):
-            ts(T[name][0:rows, i, :], key[0:rows, :], float(i), O.is_equal, kn, "%s_%d" % (name, i))
+            ts(T[name][0:rows, i, :], key[0:rows, :], float(i), O.is_equal, kn, "%s_%d" % (name, i), x, O.mult)
         alias[name] = ["%s_%d" % (name, i) for i in range(n)]
 
     ts(T.pg[:], T.ip[:], 4, O.arith_shift_right, "ip", "pg")
@@ -318,16 +347,19 @@ def rank_program(g, core, T, topo):
     tt(T.mmV[:], T.mmV[:], T.m8[:], O.add, "mmV m8", "mmV")
     tt(T.mmB[:], T.mm[:], T.o64[:], O.add, "mm o64", "mmB")
     fam("EV", T.mmV, 8, "mmV", 8)
-    fam("E8", T.m8B, 8, "m8B")
+    fill(T.k1[:], 1025.0, "k1")
+    act(T.cols[:, 7:8], T.RS[:, 0:1], AF.Copy, "RS", "cl7", scale=64.0 / 63)
+    fam("E8", T.m8B, 8, "m8B", x=1.0 / 64)
     fam("ES", T.mmB, 16, "mmB")
-    for i in range(16):
-        act(T.Dn[:, i, :], m_(BO), AF.Copy, "BO RS", "Dn_%d" % i, scale=T.RS[:, i:i + 1])
-    alias["Dn"] = ["Dn_%d" % i for i in range(16)]
-    alias["Dn8"] = alias["Dn"][0:8]
-    cu, c16, rt = T.cu, T.c16, T.rt
-    cp(cu[:], T.cxi[:], "cxi", "cu0 cu1")
-    ts(c16[:], T.cxi[:], -float(CO), O.add, "cxi", "c160 c161")
-    ts(rt[:], T.cxi[:], 0.5, O.is_lt, "cxi", "rt0 rt1")
+    zero(T.H, 0, 1024, "H00 H01")
+    for k in (0, 1):
+        select(T.Dn[:, 8 * k:8 * k + 8, :], T.H[:, 0:1024], [[-1, 8], [-16, 8], [0, 16]], O.not_equal, 63.0 / 64, -8 * k, 1, "H00 H01", ("Dn8", "Dn9")[k])
+    alias["Dn"] = ["Dn8", "Dn9"]
+    cu, rt = T.cu, T.rt
+    cp(cu[:], T.cxi[:], "cxi", "cu00 cu01 cu10 cu11")
+    ts(T.cr[:], T.cxi[:], -CO - R12, O.add, "cxi", "cr00 cr01 cr10 cr11")
+    act(rt[:], T.cr[:], AF.Sigmoid, "cr00 cr01 cr10 cr11", "rt00 rt01 rt10 rt11 ~A", bias=256.0 - 512.0 * (CO + R12), scale=-512.0)
+    ops[-1]["c"] += 1.3
     ts(T.sff[:], T.sfi[:], -float(CO), O.add, "sfi", "sff")
     dma("S", T.TS[0:128:16, TW:TW + W0], T.sff[:], "sff TSF0", "TSF", 110)
     ts(T.cols[:, 0:1], T.pm[:, 0:1], 0.0, O.add, "pm", "cl0")
@@ -338,7 +370,8 @@ def rank_program(g, core, T, topo):
     tt(m_(DX), m_(ID), m_(DL), O.subtract, "ID DL", "DX")
     tt(m_(ZT), m_(ZT), m_(BO), O.mult, "ZT BO", "ZT")
     act(m_(PRE), m_(ZT), AF.Copy, "ZT", "PRE", scale=-1.0 / 64)
-    act(m_(NI), m_(ID), AF.Copy, "ID", "NI", scale=-1.0)
+    for k, kn, x in ((NI, "NI", -1.0), (NQ, "NQ", -1.0 / 1024), (P4, "P4", 4096.0), (N2, "N2", -2048.0), (IK, "IK", 1.0 / 4096)):
+        select(m_(k), T.H[:, 0:128], [[-1, 128]], O.not_equal, x, 0, 1, "H00", kn)
     ts(T.cols[:, 1:2], T.pm[:, 0:1], 7.5, O.is_lt, "pm", "cl1", -4096.0, O.mult)
     ts(T.cols[:, 2:3], T.pm[:, 0:1], 7.5, O.is_gt, "pm", "cl2", -4096.0, O.mult)
     ts(T.cols[:, 3:4], T.pm[:, 0:1], -8.0, O.add, "pm", "cl3")
@@ -346,62 +379,62 @@ def rank_program(g, core, T, topo):
     ts(m_(RL1), T.m8B[:], T.cols[:, 3:4], O.is_equal, "m8B cl3", "RL1", -512.0, O.mult)
     act(m_(SL0), m_(ID), AF.Copy, "ID cl1", "SL0", scale=T.cols[:, 1:2])
     act(m_(SL1), m_(ID), AF.Copy, "ID cl2", "SL1", scale=T.cols[:, 2:3])
-    act(m_(NQ), m_(ID), AF.Copy, "ID", "NQ", scale=-1.0 / 1024)
-    fill(sm(0), 0.0, "F")
+    for b in (0, 1):
+        ts(m_(SB0 + b), m_(SL0 + b), 16.0, O.mult, "SL%d" % b, "SB%d" % b)
+    ts(T.I32[:], T.t16[:], 0.0, O.is_equal, "t16", "I32")
     for h in (0, 1):
-        vlist(h, 0)
+        for s in range(SP):
+            vlist(h, s)
 
     NP = W0 // PC
     for k in range(NP):
         sl = slice(k * PC, (k + 1) * PC)
         ti, tn = T.ti[:, PC * (k % 2):PC * (k % 2 + 1)], "ti%d" % (k % 2)
         ts(ti, T.tk[:, sl], 15, O.bitwise_and, "tk%d" % (k // 2), tn)
-        ts(T.TC[:, sl], ti, -1.0 / 64, O.add, tn, "TC_%d" % k, -D / 64, O.max)
-        act(T.TC[:, sl], T.TC[:, sl], AF.Copy, "TC_%d" % k, "TC_%d" % k, scale=64.0)
+        ts(T.TC[:, sl], ti, -1.0 / KC, O.add, tn, "TC_%d" % k, -D / KC, O.max)
+        act(T.TC[:, sl], T.TC[:, sl], AF.Copy, "TC_%d" % k, "TC_%d" % k + " ~A" * (k == 2), scale=KC)
     for k in range(NP):
         sl = slice(k * PC, (k + 1) * PC)
         b = k % NB4
         o = slice(b * PC, (b + 1) * PC)
-        ps, pn = (T.PU, T.PX1)[b // 2][:, 512 * (b % 2):512 * (b % 2) + PC], ("PU0", "PU1", "PX10", "PX11")[b]
+        ps, pn = PX[b // 2][:, 512 * (b % 2):512 * (b % 2) + PC], ("PX00", "PX01", "PX10", "PX11")[b]
         ts(T.tr[:, o], T.tk[:, sl], -7.5, O.add, "tk%d" % (k // 2), "tr%d" % b, MAG, O.add)
         act(T.sh[:, o], T.tr[:, o], AF.Identity, "tr%d" % b, "sh%d" % b, bias=-(MAG / 16) - CO, scale=1.0 / 16)
         mm(acc(ps, [(m_(DX), T.sh[:, o])]), "DX sh%d" % b, pn)
         act(T.rb[:, o], ps, AF.Identity, pn, "rb%d" % b, bias=R12)
         mm(acc(ps, [(m_(DX), T.sh[:, o]), (m_(NI), T.rb[:, o])]), "DX NI sh%d rb%d" % (b, b), pn)
-        ts(T.TS[:, sl], ps, R12, O.add, pn, "TS_%d" % k)
+        act(T.TS[:, sl], ps, AF.Identity, pn, "TS_%d" % k, bias=R12)
 
-    fill(T.zz[:], 0.0, "zz")
     fill(T.inc[:, 0:16], 0.0, "inc")
     fill(T.nD[:], -D, "nD")
     ts(T.lkj[:], T.lki[:], 6, O.arith_shift_right, "lki", "lkj")
     ts(T.lki[:], T.lki[:], 63, O.bitwise_and, "lki", "lki")
-    ts(T.lhf[:], T.lkj[:], -float(CO // 64), O.add, "lkj", "lhf")
-    cp(T.llf[:], T.lki[:], "lki", "llf")
+    ts(T.lhf[:], T.lkj[:], 1.0, O.add, "lkj", "lhf", 64.0, O.mult)
+    ts(T.llf[:], T.lki[:], 1.0, O.add, "lki", "llf")
+    act(T.cols[:, 4:5], T.RS[:, 0:1], AF.Identity, "RS", "cl4", scale=CO + 63.0, bias=1.0)
+    for t in range(RO):
+        act(T["mk%d" % t][:, CAP:CS], T.RS[:], AF.Identity, "RS cl4", "lz%d" % t, scale=0.0, bias=T.cols[:, 4:5])
     dma("S", T.TL[0:128:16, 0:W0], T.lhf[:], "lhf TL", "TLa", 60)
     dma("S", T.TL[1:128:16, 0:W0], T.llf[:], "llf TL", "TLb", 60)
-    ts(T.mL[:], T.mi[:], T.cols[:, 0:1], O.add, "mi cl0", "mL")
-    ts(T.cols[:, 4:5], T.RS[:, 0:1], 64.0, O.mult, "RS", "cl4")
-    ts(T.LT[:], T.mm[:, 0:16], T.cols[:, 0:1], O.is_gt, "mm cl0", "LT")
-    ts(T.Dm[:], T.mL[:], float(LN), O.add, "mL", "Dm")
-    tt(T.cols[:, 5:6], T.cols[:, 4:5], T.RS[:, 1:2], O.add, "cl4 RS", "cl5")
+    act(T.mL[:], T.mi[:], AF.Identity, "mi cl0", "mL", bias=T.cols[:, 0:1])
+    act(T.Dm[:], T.mL[:], AF.Identity, "mL", "Dm", bias=float(CS - 2047))
     for x in (0, 1):
-        ts(T.dum[:, 16 * x:16 * x + 16], T.mL[:, 0:16], float(DU - 2048), O.add, "mL", "dum%d" % x)
-    ts(T.kL[:, 0:8], T.mL[:, 0:8], 1.0, O.mult, "mL", "kL")
-    ts(T.dus[:], T.dum[:], 1.0 / 4096, O.mult, "dum0 dum1", "dus")
-    tt(m_(ZT), m_(ZT), m_(BO), O.subtract, "ZT BO", "ZT")
+        act(T.dum[:, 16 * x:16 * x + 16], T.mL[:, 0:16], AF.Identity, "mL", "dum%d" % x, bias=float(DU - 2048))
+    act(T.kL[:, 0:8], T.mL[:, 0:8], AF.Copy, "mL", "kL")
+    act(T.dus[:], T.dum[:], AF.Copy, "dum0 dum1", "dus", scale=1.0 / 4096)
+    ts(m_(ZT), T.t16[:], -0.5, O.is_lt, "t16 PRE", "ZT", -1.0, O.mult)
     ts(m_(DD), T.t16[:], -1.0, O.is_equal, "t16", "DD")
     act(m_(NB), m_(BO), AF.Copy, "BO", "NB", scale=-1.0)
     tt(m_(DL), m_(ID), m_(DD), O.subtract, "ID DD", "DL")
-    act(T.EW[:], T.ES[:], AF.Copy, "ES cl0", "EW", scale=T.cols[:, 0:1])
-    act(T.EH[:], T.ES[:], AF.Copy, "ES cl5", "EH", scale=T.cols[:, 5:6])
-    for i in range(16):
-        act(T.TR[:, i, :], T.ES[:, i, :], AF.Copy, "ES_%d LT" % i, "TR_%d" % i, scale=T.LT[:, i:i + 1])
-    alias["TR"] = ["TR_%d" % i for i in range(16)]
+    for k in range(4):
+        act(T.EW[:, 4 * k:4 * k + 4, :], T.ES[:, 4 * k:4 * k + 4, :], AF.Copy, "ES cl0", "EW%d" % k, scale=T.cols[:, 0:1])
+    alias["EW"] = ["EW0", "EW1", "EW2", "EW3"]
+    select(T.TR[:], T.ES[:], [[1, 16], [16, 8], [0, 16]], O.is_gt, 0.0, 0, -1, "ES", "TR")
     tt(m_(DD), m_(DL), m_(DX), O.add, "DL DX", "DD")
     ts(T.cols[:, 6:7], T.RS[:, 0:1], -1.0, O.mult, "RS", "cl6")
-    act(m_(IK), m_(ID), AF.Copy, "ID", "IK", scale=1.0 / 4096)
     for t in range(RO - 1):
-        ts(T.wn[:, B * t:B * t + B], T.mrow[:, 0:256], float(4095 + W0 + B * t - CO), O.add, "mrow", "wr%d" % t)
+        act(T.wn[:, B * t:B * t + B], T.mrow[:, 0:256], AF.Identity, "mrow", "wr%d" % t, bias=float(2047 + W0 + B * t - CO))
+    iota(T.n128[:], [[0, 1040]], -128, 0, "n128")
 
     TCR = "TC TCz " + " ".join("TC_%d" % k for k in range(NP))
     TSR = "TS TSz TSF TSF0 " + " ".join("TS_%d" % k for k in range(NP))
@@ -417,41 +450,54 @@ def rank_program(g, core, T, topo):
     def OB(h, b):
         return slice(64 * h + 32 * b, 64 * h + 32 * b + 32)
 
-    def newc(h, y, yn, off):
-        ts(cu[:, HC(h)], y, off + CO, O.add, yn, K("cu@", h))
-        act(c16[:, HC(h)], y, AF.Identity, yn, K("c16@", h), bias=off)
-        act(rt[:, HC(h)], y, AF.Relu, yn, K("rt@", h), bias=1.0 - CO - off, scale=-1.0)
+    def marks(t, h, b):
+        o = CS + 1024 * h + 512 * b
+        return T["mk%d" % (t % 2)][:, o:o + 512]
+    MKR = "mk%d00 mk%d01 mk%d10 mk%d11"
+
+    def unit(h, bs):
+        return (str(h) + (str(bs[0]) if len(bs) == 1 else ""), lambda x: " ".join(K(k + "@#", h, b) for k in x.split() for b in bs),
+                slice(64 * h + 32 * bs[0], 64 * h + 32 * bs[-1] + 32), slice(128 * h + 64 * bs[0], 128 * h + 64 * bs[-1] + 64))
+    for x in ("eb", "cf"):
+        alias[x] = [x + k for k in ("00", "01", "10", "11")]
+
+    def newc(h, bs, n=None):
+        u, N, oc, pr = unit(h, bs)
+        label[0] = (n, "u" + u)
+        ts(cu[:, oc], T.cr[:, oc], R12 + CO, O.add, N("cr"), N("cu"))
+        label[0] = (n, "R" + u)
+        act(rt[:, oc], T.cr[:, oc], AF.Relu, N("cr"), N("rt"), bias=1.0 - CO - R12, scale=-1.0)
 
     def flist(n, s):
-        ts(sm(1), c16[:, 0:16], float(CO + 4096 * (RO * SP + 1 - n)), O.add, "c160", "val")
-        ts(sm(2), T.PL0[:, 256:272], -2100.0, O.is_gt, "PL0.c", "e16")
+        age = T.PL0[:, 320:336]
+        mm(acc(age, [(m_(P4), T.one[:])] + [(m_(SB0 + b), T.cd[:, b:32:2]) for b in (0, 1)]), "P4 one SB0 SB1 cd00", "PL00.a")
         if s == SP - 1:
-            cp(T.fi[:, 0:16], sm(0), "F", "fi")
-            ts(sm(3), sm(0), 0.5, O.is_gt, "F", "hf")
-            ts(T.fi[:, 16:32], T.fi[:, 0:16], 4095, O.bitwise_and, "fi", "fj")
-            ts(T.dk[:, 16:32], c16[:, 0:16], float(CO - 2048), O.add, "c160", "dk1")
-            ts(T.dk[:, 0:16], T.fi[:, 16:32], -2048.0, O.add, "fj", "dk0")
-            tt(T.dk[:], T.dk[:], T.dum[:], O.subtract, "dk0 dk1 dum0 dum1", "dk0 dk1")
-            tt(sm(4), sm(3), sm(2), O.is_gt, "hf e16", "ca")
-            for x in (0, 1):
-                tt(T.dk[:, 16 * x:16 * x + 16], T.dk[:, 16 * x:16 * x + 16], sm(4), O.mult, "dk%d ca" % x, "dk%d" % x)
-            tt(T.K[:], T.dk[:], T.dum[:], O.add, "dk0 dk1 dum0 dum1", "K")
+            act(T.r2[:, 0:16], sm(0), AF.Identity, "F", "r2", bias=2 * R12)
+            tt(sm(3), age, sm(0), O.subtract, "PL00.a F", "hf")
+            tt(sm(2), sm(0), T.r2[:, 0:16], O.subtract, "F r2", "fj")
+            for x, key, kn in ((0, sm(2), "fj"), (1, T.cr[:, 0:16], "cr00")):
+                o, base = slice(16 * x, 16 * x + 16), (2 - x) * R12 + CO - 2048
+                ts(T.dk[:, o], sm(3), base + 61440.0 - 790000.0, O.add, "hf", "dk%d" % x, base, O.max)
+                tt(T.dk[:, o], T.dk[:, o], key, O.add, "dk%d %s" % (x, kn), "dk%d" % x)
+            tt(T.K[:], T.dk[:], T.dum[:], O.min, "dk0 dk1 dum0 dum1", "K")
         if n < RO * SP - 1:
-            tt(sm(1), sm(1), sm(0), O.max, "val F", "val")
-            tt(sm(0), sm(1), sm(2), O.mult, "val e16", "F")
+            label[0] = (n, "f0")
+            tt(sm(1), T.cr[:, 0:16], sm(0), O.max, "cr00 F", "val")
+            label[0] = (n, "g0")
+            tt(sm(0), age, sm(1), O.add, "val PL00.a", "F")
 
     def ranks(t):
-        tot = T.PL1[:, 0:128]
-        mm(acc(tot, [(m_(BO), T.eb[:])]), "BO eb0 eb1", "PL1.w")
-        mm(acc(T.PL0[:, 128:136], [(m_(IK), T.kL[:, 0:8])] + lsum(T.ES, T.eb, 0, 128)), "IK kL ES eb0 eb1", "PL0.d")
-        mm(acc(T.PL0[:, 0:128], [(m_(ZT), T.eb[:]), (m_(SL0), T.eb[:]), (m_(SL1), T.eb[:]), (m_(ID), T.eb[:])]), "ZT SL0 SL1 ID eb0 eb1", "PL0.w")
-        scan(T.inc[:, 1:129], tot, T.zz[:], O.add, "PL1.w zz", "inc")
-        mm(acc(T.PL0[:, 384:392], lsum(T.ES, T.inc, 0, 128)), "inc ES", "PL0.v")
-        ts(T.tot[:, 0:1], T.inc[:, 128:129], 0.0, O.add, "inc", "tot")
+        tot = T.PL1[:, 896:1024]
+        mm(acc(tot, [(m_(BO), T.eb[:])]), "BO eb", "PL11.v")
+        mm(acc(T.PL1[:, 320:328], [(m_(IK), T.kL[:, 0:8])] + lsum(T.ES, T.eb, 0, 128)), "IK kL ES eb", "PL10.a")
+        mm(acc(T.PL1[:, 384:512], [(m_(ZT), T.eb[:]), (m_(N2), T.eb[:])]), "ZT N2 eb", "PL10.v")
+        scan(T.inc[:, 1:129], tot, T.zz[:], O.add, "PL11.v zz", "inc")
+        mm(acc(T.PL1[:, 832:840], lsum(T.ES, T.inc, 0, 128)), "inc ES", "PL11.a")
+        act(T.tot[:, 0:1], T.inc[:, 128:129], AF.Identity, "inc", "tot", bias=-2047.5)
         send(T.lT[:, 8 * t:8 * t + 1], T.tot[:, 0:1], "T", t, "tot", 1)
-        ts(T.o8[:, 0:8], T.PL0[:, 384:392], 2048.0, O.add, "PL0.v", "o8a", 2.0 ** -16, O.mult)
-        tt(T.X[:], T.inc[:, 1:129], T.PL0[:, 0:128], O.add, "inc PL0.w", "X")
-        tt(T.o8[:, 8:16], T.o8[:, 0:8], T.PL0[:, 128:136], O.min, "o8a PL0.d", "o8b")
+        ts(T.o8[:, 0:8], T.PL1[:, 832:840], 2048.0, O.add, "PL11.a", "o8a", 2.0 ** -16, O.mult)
+        tt(T.X[:], T.inc[:, 1:129], T.PL1[:, 384:512], O.add, "inc PL10.v", "X")
+        tt(T.o8[:, 8:16], T.o8[:, 0:8], T.PL1[:, 320:328], O.min, "o8a PL10.a", "o8b")
         ts(T.ofu[:], T.o8[:, 8:16], 4096.0, O.mult, "o8b", "ofu")
         cp(ind(T.MK[:], T.ofu[:]), T.krow[:], "krow ofu", "MK")
         scan(T.kr[:], T.MK[:, 128:640], T.MK[:, 128:640], O.max, "MK", "kr")
@@ -460,8 +506,10 @@ def rank_program(g, core, T, topo):
 
     def keys(last):
         act(T.K16[:], T.K[:], AF.Copy, "K", "K16")
-        mm(spread(T.PX0, 512, 256, T.K16[:, 0:16], 16, True) + spread(T.PX0, 768, 256, T.K16[:, 16:32], 16, True), "K16 Dn", "PX01")
-        act(T.R[:], T.PX0[:, 512:1024], AF.Copy, "PX01", "R")
+        for x in (0, 1):
+            o, on = 768 - 512 * x, "PL0#.c PL0#.a PL0#.v".replace("#", str(1 - x))
+            mm(spread(T.PL0, o, 256, T.K16[:, 16 * x:16 * x + 16], 16, True), "K16 Dn", on)
+            act(T.R[:, 256 * x:256 * x + 256], T.PL0[:, o:o + 256], AF.Copy, on, "R%d" % x, scale=64.0 / 63)
         oh = T.PX0[:, 0:256]
         mm(acc(oh, [(m_(DL), T.s[:, 0:256])]) + ([] if last else acc(T.PX0[:, 256:512], [(m_(DD), T.s[:, 0:256])])), "DL DD s00", "PX00")
         if last:
@@ -469,68 +517,92 @@ def rank_program(g, core, T, topo):
             act(T.ob[:], oh, AF.Copy, "PX00", "u1")
         else:
             act(T.nu[:], oh, AF.Identity, "PX00", "nu", bias=1.0, scale=-1.0)
-            act(T.u1[:], oh, AF.Copy, "PX00", "u1", scale=63.0)
-            act(T.om[:], oh, AF.Identity, "PX00", "om", bias=-128.0 - 1.0 / 64)
+            act(T.u1[:], oh, AF.Copy, "PX00", "u1", scale=KC - 1)
             act(T.dsg[:], T.PX0[:, 256:512], AF.Identity, "PX00 cl6", "dsg", bias=T.cols[:, 6:7])
 
     def step(h, t, s):
         n, wt = SP * t + s, W0 + B * t
-        L, HP = PL[h], slice(128 * h, 128 * h + 128)
+        L = PL[h]
+
+        def lab(x, b=0):
+            label[0] = (n, K(x, h, b))
         for b in (0, 1):
             win = ind(T.TC[:, 0:wt], cu[:, OB(h, b)])
+            w, wn, pr = L[:, 512 * b:512 * b + 64], K("PL@#.w", h, b), slice(128 * h + 64 * b, 128 * h + 64 * b + 64)
+            X, xn = PX[h][:, 512 * b:512 * b + 512], K("PX@#", h, b)
+            lab("q@#", b)
             if n == 0:
-                cp(T.q[:, HB(h, b)], win, TCR + K(" cu@", h), K("q@#", h, b))
+                cp(T.q[:, HB(h, b)], win, TCR[7:] + K(" cu@#", h, b), K("q@#", h, b))
             else:
-                tt(T.q[:, HB(h, b)], win, T.mk[:, HB(h, b)], O.mult, TCR + K(" cu@ mk@#", h, b), K("q@#", h, b))
-        mm(acc(L[:, 0:128], lsum(T.E8, T.q, 1024 * h, 1024 * h + 1024, 8)), K("q@0 q@1 E8", h), K("PL@.w", h))
-        for b in (0, 1):
-            mm([(PX[h][:, 512 * b:512 * b + 512], m_(PRE), T.q[:, HB(h, b)], True)], K("q@# PRE", h, b), K("PX@#", h, b), True)
-        act(T.p[:, HP], L[:, 0:128], AF.Identity, K("PL@.w", h), K("p@", h), bias=1025.0, scale=1.0 / 64)
-        act(T.xx[:, HP], T.p[:, HP], AF.Identity, K("p@", h), K("xx@", h), bias=65.0 * 1025, scale=-65.0)
-        tt(L[:, 0:128], L[:, 0:128], T.xx[:, HP], O.add, K("PL@.w xx@", h), K("PL@.w", h))
-        tt(T.xx[:, HP], L[:, 0:128], T.vl[:, 256 * s + 128 * h:256 * s + 128 * h + 128], O.mult, K("PL@.w vl@#", h, s), K("xx@", h))
-        act(T.th[:, HP], T.xx[:, HP], AF.Identity, K("xx@", h), K("th@", h), bias=1024.5015)
-        for b in (0, 1):
-            mm(spread(PX[h], 512 * b, 512, T.th[:, 128 * h + 64 * b:128 * h + 64 * b + 64], 8, False), K("th@ Dn8", h), K("PX@#", h, b))
-            act(T.s[:, HB(h, b)], PX[h][:, 512 * b:512 * b + 512], AF.Sigmoid, K("PX@#", h, b), K("s@#", h, b), bias=600.0 * (0.375 - 1025), scale=600.0)
-        mm(acc(L[:, 128:256], [(m_(ID), T.th[:, HP]), (m_(NI), T.p[:, HP])]) +
-           [(L[:, 128 + b:256:2], m_(RL0 + b), rt[:, HC(h)], False) for b in (0, 1)], K("th@ p@ rt@ ID NI RL0 RL1", h), K("PL@.d", h))
-        act(T.cd[:, HP], L[:, 128:256], AF.Sigmoid, K("PL@.d", h), K("cd@", h), bias=-200.0, scale=-400.0)
-        mm(acc(L[:, 256:320], [(m_(ID), c16[:, HC(h)])] + [(m_(SL0 + b), T.cd[:, 128 * h + b:128 * h + 128:2]) for b in (0, 1)]),
-           K("c16@ cd@ ID SL0 SL1", h), K("PL@.c", h))
-        ts(T.cu2[:, HC(h)], L[:, 256:320], float(TW + CO), O.add, K("PL@.c", h), K("cu2@", h))
-        if s == SP - 1:
-            ts(T.eb[:, HC(h)], L[:, 256:320], -2100.0, O.is_gt, K("PL@.c", h), K("eb@", h))
-        else:
-            vlist(h, s + 1)
+                tt(T.q[:, HB(h, b)], win, marks(t, h, b), O.mult, TCR + K(" cu@# mk%d@#" % (t % 2), h, b), K("q@#", h, b))
+            lab("W@#", b)
+            mm(acc(w, [(m_(ID), T.k1[:])] + lsum(T.E8, T.q, 1024 * h + 512 * b, 1024 * h + 512 * b + 512, 8)), K("ID k1 E8 q@#", h, b), wn)
+            lab("p@#", b)
+            ts(T.p[:, pr], w, 64.0 / 63, O.mult, wn, K("p@#", h, b), -1025.0 / 63, O.add)
+            lab("T@#", b)
+            tt(w, T.p[:, pr], w, O.subtract, wn + K(" p@#", h, b), wn)
+            lab("x@#", b)
+            tt(T.xx[:, pr], w, T.vl[:, 384 * h + 128 * s + 64 * b:384 * h + 128 * s + 64 * b + 64], O.mult, wn + K(" vl@#", h, s), K("xx@#", h, b))
+            lab("t@#", b)
+            act(T.th[:, pr], T.xx[:, pr], AF.Identity, K("xx@#", h, b), K("th@#", h, b), bias=1024.5015)
+            lab("U@#", b)
+            mm([(X, m_(PRE), T.q[:, HB(h, b)], True)], K("q@# PRE", h, b), xn, True)
+            lab("X@#", b)
+            mm(spread(PX[h], 512 * b, 512, T.th[:, pr], 8, False), K("th@# Dn8", h, b), xn)
+            lab("s@#", b)
+            act(T.s[:, HB(h, b)], X, AF.Sigmoid, xn, K("s@#", h, b), bias=600.0 * (23.5 - 63 * 1025) / 64, scale=600.0)
+        for bs in UNITS:
+            u, N, oc, pr = unit(h, bs)
+            b0, b1, k = 512 * bs[0], 512 * bs[-1], len(bs)
+            d, dn, c, cn = L[:, b0 + 64:b0 + 64 + 64 * k], K("PL@#.d", h, bs[0]), L[:, b1 + 256:b1 + 256 + 32 * k], K("PL@#.c", h, bs[-1])
+            label[0] = (n, "d" + u)
+            mm(acc(d, [(m_(ID), T.th[:, pr]), (m_(NI), T.p[:, pr])]) +
+               [(L[:, b0 + 64 + b:b0 + 64 + 64 * k:2], m_(RL0 + b), rt[:, oc], False) for b in (0, 1)], N("th p rt") + " ID NI RL0 RL1", dn)
+            label[0] = (n, "e" + u)
+            act(T.cd[:, pr], d, AF.Sigmoid, dn, N("cd"), bias=-200.0, scale=-400.0)
+            label[0] = (n, "c" + u)
+            mm(acc(c, [(T.I32[:], T.cr[:, oc])] + [(m_(SL0 + b), T.cd[:, pr.start + b:pr.stop:2]) for b in (0, 1)]), N("cr cd") + " I32 SL0 SL1", cn)
+            ops[-1]["c"] += 192 * EST["pe"]
+            label[0] = (n, "o" + u)
+            ts(T.cu2[:, oc], c, R12 + TW + CO, O.add, cn, N("cu2"))
+            if s == SP - 1:
+                ts(T.eb[:, oc], c, -R12 - 2100.0, O.is_gt, cn, N("eb"))
         if h == 0:
             flist(n, s)
         elif s == SP - 1:
             ranks(t)
         for b in (0, 1):
-            tt(T.Y[:, HB(h, b)], ind(T.TS[:, 0:TW + wt], T.cu2[:, OB(h, b)]), T.s[:, HB(h, b)], O.mult, TSR + K(" cu2@ s@#", h, b), K("Y@#", h, b))
+            lab("Y@#", b)
+            tt(T.Y[:, HB(h, b)], ind(T.TS[:, 0:TW + wt], T.cu2[:, OB(h, b)]), T.s[:, HB(h, b)], O.mult, TSR + K(" cu2@# s@#", h, b), K("Y@#", h, b))
             if n < RO * SP - 1:
-                mm([(T.PU[:, 512 * b:512 * b + 512], m_(NQ), T.q[:, HB(h, b)], True)] +
-                   spread(T.PU, 512 * b, 512, T.cd[:, 128 * h + 64 * b:128 * h + 64 * b + 64], 8, False), K("q@# cd@ NQ Dn8", h, b), K("PU#", h, b))
-                act(T.mk[:, HB(h, b)], T.PU[:, 512 * b:512 * b + 512], AF.Sigmoid, K("PU#", h, b), K("mk@#", h, b), bias=-200.0, scale=400.0 * 1024 / D)
-        y, yn = L[:, 320:384], K("PL@.y", h)
-        mm(acc(y, lsum(T.ES, T.Y, 1024 * h, 1024 * h + 1024)), K("Y@0 Y@1 ES", h), yn)
-        act(T.ry[:, HC(h)], y, AF.Identity, yn, K("ry@", h), bias=R12)
-        cr, cn = T.cr[:, HC(h)], K("cr@", h)
-        tt(cr, y, T.ry[:, HC(h)], O.subtract, K("PL@.y ry@", h), cn)
-        if s < SP - 1:
-            newc(h, cr, cn, R12)
-        else:
-            if h == 0 and t < RO - 1:
-                ts(cu[:, 0:16], T.cr[:, 0:16], R12 + CO, O.add, cn, "cu0")
-            act(T.cf[:, HC(h)], cr, AF.Identity, cn, K("cf@", h), bias=R12)
-            act(c16[:, HC(h)], cr, AF.Identity, cn, K("c16@", h), bias=R12)
+                X, xn = PX[h][:, 512 * b:512 * b + 512], K("PX@#", h, b)
+                lab("M@#", b)
+                mm([(X, m_(NQ), T.q[:, HB(h, b)], True)] +
+                   spread(PX[h], 512 * b, 512, T.cd[:, 128 * h + 64 * b:128 * h + 64 * b + 64], 8, False), K("q@# cd@# NQ Dn8", h, b), xn)
+                lab("m@#", b)
+                act(marks(t, h, b), X, AF.Sigmoid, xn, K("mk%d@#" % (t % 2), h, b), bias=-200.0, scale=400.0 * 1024 / D)
+        for bs in UNITS:
+            u, N, oc, pr = unit(h, bs)
+            y, yn = L[:, 512 * bs[0] + 192:512 * bs[0] + 192 + 32 * len(bs)], K("PL@#.y", h, bs[0])
+            label[0] = (n, "y" + u)
+            mm(acc(y, lsum(T.ES, T.Y, 16 * oc.start, 16 * oc.stop)), N("Y") + " ES", yn)
+            label[0] = (n, "r" + u)
+            act(T.ry[:, oc], y, AF.Identity, yn, N("ry"), bias=R12)
+            label[0] = (n, "a" + u)
+            tt(T.cr[:, oc], y, T.ry[:, oc], O.subtract, yn + " " + N("ry"), N("cr"))
+            if s < SP - 1:
+                newc(h, bs, n)
+            else:
+                act(T.cf[:, oc], T.cr[:, oc], AF.Identity, N("cr"), N("cf"), bias=R12)
+        if s == SP - 1 and h == 0 and t < RO - 1:
+            ts(cu[:, 0:16], T.cr[:, 0:16], R12 + CO, O.add, "cr00", "cu00")
+            act(T.c16[:], T.cr[:, 0:16], AF.Identity, "cr00", "c16", bias=R12)
 
     def firsts(x):
         E, En = T["EQ%d" % x], " ".join("E%d_%d" % (x, k) for k in range(16))
         for k in range(16):
             ts(E[:, 256 * k:256 * k + 256 - 16 * k], T.R[:, 256 * x + 16 * k:256 * x + 256], T.K[:, 16 * x + k:16 * x + k + 1],
-               O.is_equal, "R K", "E%d_%d" % (x, k))
+               O.is_equal, "R%d K" % x, "E%d_%d" % (x, k))
         ps, pn = T.PX1[:, 512 * x:512 * x + 512], "PX1%d" % x
         mm([(ps[:, 16 * k + 16:256], m_(BO), E[:, 256 * k + 16:256 * k + 256 - 16 * k], k == 0) for k in range(15)], "BO " + En, pn)
         act(T.du[:, 256 * x + 16:256 * x + 256], ps[:, 16:256], AF.Copy, pn, "du%d" % x)
@@ -544,9 +616,12 @@ def rank_program(g, core, T, topo):
         last, wt = t == RO - 1, W0 + B * t
         if last:
             for k in range(8):
-                o = slice(514 * k, 514 * (k + 1))
-                act(T.yb[:, o], T.TC[:, o], AF.Identity, TCR, "yb%d" % k, bias=128.0, scale=1.0 / 64)
-                ts(T.yb[:, o], T.yb[:, o], -128.0, O.add, "yb%d" % k, "yb%d" % k)
+                o = slice(520 * k, min(520 * (k + 1), TW + 16))
+                act(T.yb[:, o], T.TC[:, o], AF.Identity, TCR, "yb%d" % k, bias=128.0, scale=1.0 / KC)
+            for k in range(4):
+                n = min(1040, TW + 16 - 1040 * k)
+                dma("G", T.yb[:, 1040 * k:1040 * k + n], T.n128[:, 0:n], "n128 yb%d yb%d" % (2 * k, 2 * k + 1), "yc%d" % k, 800, True)
+            YBR += " yc0 yc1 yc2 yc3"
         for s in range(SP):
             TAG[0] = "s%d" % (SP * t + s)
             step(0, t, s)
@@ -560,23 +635,25 @@ def rank_program(g, core, T, topo):
         mm(acc(lane, lsum(T.ES, T.kr, 0, 512)), "kr ES", "PX00")
         ts(T.klu[:], lane, 1.0 / 16, O.mult, "PX00", "klu")
         tt(T.OH[:], ind(T.X[:], T.klu[:]), T.mrow[:], O.is_equal, "X klu mrow", "OH")
-        tt(T.CG[:], ind(T.cf[:], T.klu[:]), T.OH[:], O.mult, "cf0 cf1 klu OH", "CG")
-        mm(acc(lane, lsum(T.ES, T.kr, 0, 512)), "kr ES", "PX00", True)
-        mm(acc(lane, lsum(T.EW, T.OH, 0, 512), False), "OH EW", "PX00")
+        tt(T.CG[:], ind(T.cf[:], T.klu[:]), T.OH[:], O.mult, "cf klu OH", "CG")
         mm(acc(T.PX0[:, 512:544], lsum(T.ES, T.CG, 0, 512)), "CG ES", "PX01")
         if not last:
+            mm(acc(lane, lsum(T.ES, T.kr, 0, 512)), "kr ES", "PX00", True)
+            mm(acc(lane, lsum(T.EW, T.OH, 0, 512), False), "OH EW", "PX00")
             cp(T.lnu[:], lane, "PX00", "lnu")
-            act(T.MS[:], ind(T.mk[:, 0:LN], T.lnu[:]), AF.Copy, "mk00 mk01 mk10 mk11 lnu", "MS")
-            send(T["lM%d" % t][:], T.MS[:], "M", t, "MS", 128)
+            act(T.MS[:], ind(T["mk%d" % t][:, CS:], T.lnu[:]), AF.Identity, MKR % ((t,) * 4) + " lnu", "MS", bias=-1.0, scale=2.0)
         ts(T.cmu[:], T.PX0[:, 512:544], float(CO), O.add, "PX01", "cmu")
-        act(T.Lg[:], ind(T.TL[:, 0:wt], T.cmu[:]), AF.Copy, TLR + " cmu", "Lg")
-        send(T["lL%d" % t][:], T.Lg[:], "L", t, "Lg", 128)
+        if last:
+            cp(T.Lg[:], ind(T.TL[:, 0:wt], T.cmu[:]), TLR + " cmu", "Lg")
+        else:
+            tt(T.Lg[:], ind(T.TL[:, 0:wt], T.cmu[:]), T.MS[:], O.mult, TLR + " cmu MS", "Lg")
+        send(T["mk%d" % t][:, 0:CAP], T.Lg[:], "L", t, "Lg", 128)
         firsts(0)
         firsts(1)
         wb = slice(wt, wt + B)
         of, od = T.ou[:, 0:16], T.ou[:, 16:32]
-        ts(sm(5), T.mo[:, 0:16], (DU - 2048.5) / 4096, O.is_gt, "mo0", "nf", 8192.0, O.mult)
-        tt(sm(5), sm(5), c16[:, 0:16], O.add, "nf c160", "nf")
+        act(sm(5), T.mo[:, 0:16], AF.Relu, "mo0", "nf", scale=2.0 ** 26, bias=-(DU - 2048.5) * 2.0 ** 14)
+        tt(sm(5), sm(5), T.cf[:, 0:16], O.add, "nf cf00", "nf")
         ts(T.su[:], sm(5), float(CO), O.add, "nf", "su", float(TW), O.min)
         if last:
             act(T.Cc[:], ind(T.yb[:], T.su[:]), AF.Identity, YBR + " su", "Cc", bias=128.25, scale=0.5)
@@ -590,49 +667,67 @@ def rank_program(g, core, T, topo):
                 o = slice(2048 * k, 2048 * k + 2048)
                 dma("SA"[k], T.yn[:, o], T.yb[:, o], YBR, "yn%d" % k, 512 * (k + 1))
         else:
-            act(T.TS[:, wb], ind(T.TS[:, 0:wt], cu[:, 0:16]), AF.Copy, TSR + " cu0", "TS")
-            act(T.TL[:, wb], ind(T.TL[:, 0:wt], cu[:, 0:16]), AF.Copy, TLR + " cu0", "TL")
-            mm(spread(T.PU, 0, 256, c16[:, 0:16], 16, True), "c160 Dn", "PU0")
-            act(T.TS[:, TW + wt:TW + wt + B], T.PU[:, 0:256], AF.Copy, "PU0 RS", "TSF", scale=T.RS[:, 0:1])
-            act(T.Cc[:], ind(T.TC[:], T.su[:]), AF.Identity, TCR + " su", "Cc", bias=128.26, scale=1.0 / 128)
+            act(T.TS[:, wb], ind(T.TS[:, 0:wt], cu[:, 0:16]), AF.Copy, TSR + " cu00", "TS")
+            act(T.TL[:, wb], ind(T.TL[:, 0:wt], cu[:, 0:16]), AF.Copy, TLR + " cu00", "TL")
+            mm(spread(T.PL0, 768, 256, T.c16[:], 16, True), "c16 Dn", "PL01.c PL01.a PL01.v")
+            act(T.TS[:, TW + wt:TW + wt + B], T.PL0[:, 768:1024], AF.Copy, "PL01.c PL01.a PL01.v cl7", "TSF", scale=T.cols[:, 7:8])
+            act(T.PL1[:, 256:512], T.nu[:], AF.Identity, "nu", "PL10.c PL10.a PL10.v", bias=-127.0 - 1.0 / KC, scale=-1.0)
+            act(T.Cc[:], ind(T.TC[:], T.su[:]), AF.Identity, TCR + " su", "Cc", bias=128.26, scale=0.5 / KC)
             tt(T.aC[:], ind(T.TC[:], of), T.nu[:], O.mult, TCR + " ou0 nu", "aC")
             tt(ind(T.TC[:], of), T.aC[:], T.u1[:], O.add, "aC u1 ou0", "TC")
-            act(T.Cb[:], ind(T.TC[:], od), AF.Identity, TCR + " ou1", "Cb", bias=128.0, scale=1.0 / 64)
-            ts(T.aF[:], T.Cc[:], -128.0 - 1.0 / 64, O.add, "Cc", "aF", -D / 64, O.max)
-            act(T.TC[:, wb], T.aF[:], AF.Copy, "aF", "TC", scale=64.0)
-            tt(T.aC[:], T.Cb[:], T.om[:], O.add, "Cb om", "aC")
-            ts(T.aC[:], T.aC[:], 15.0 - 1.0 / 64, O.min, "aC", "aC", 64.0, O.mult)
+            act(T.Cb[:], ind(T.TC[:], od), AF.Identity, TCR + " ou1", "Cb", bias=128.0, scale=1.0 / KC)
+            act(T.aF[:], T.Cc[:], AF.Relu, "Cc", "aF", bias=D - 1.0 - 128.0 * KC, scale=KC)
+            act(T.TC[:, wb], T.aF[:], AF.Identity, "aF", "TC", bias=-D)
+            tt(T.aC[:], T.Cb[:], T.PL1[:, 256:512], O.add, "Cb PL10.c PL10.a PL10.v", "aC")
+            ts(T.aC[:], T.aC[:], 15.0 - 1.0 / KC, O.min, "aC", "aC", KC, O.mult)
             tt(ind(T.TC[:], od), T.aC[:], T.nD[:], O.max, "aC nD ou1", "TC")
             tt(T.Yf[:], ind(T.TS[:, 0:TW], of), T.s[:, 0:256], O.mult, TSR + " ou0 s00", "Yf")
-            mm(acc(T.PU[:, 0:256], [(m_(ID), T.wn[:, B * t:B * t + B]), (m_(NB), T.Yf[:])]), "ID NB Yf wr%d" % t, "PU0")
-            tt(T.aD[:], T.PU[:, 0:256], T.dsg[:], O.mult, "PU0 dsg", "aD")
-            tt(T.aE[:], ind(T.TS[:, 0:TW], of), T.aD[:], O.add, TSR + " ou0 aD", "aE")
+            mm(acc(T.PL0[:, 256:512], [(m_(ID), T.wn[:, B * t:B * t + B]), (m_(NB), T.Yf[:])]), "ID NB Yf wr%d" % t, "PL00.c PL00.a PL00.v")
+            act(T.aD[:], ind(T.TS[:, 0:TW], of), AF.Copy, TSR + " ou0", "aD")
+            tt(T.PL0[:, 256:512], T.PL0[:, 256:512], T.dsg[:], O.mult, "PL00.c PL00.a PL00.v dsg", "PL00.c PL00.a PL00.v")
+            tt(T.aE[:], T.aD[:], T.PL0[:, 256:512], O.add, "PL00.c PL00.a PL00.v aD", "aE")
             act(T.r2[:], T.aE[:], AF.Identity, "aE", "r2", bias=R12)
             act(T.aD[:], T.r2[:], AF.Identity, "r2", "aD", bias=-R12)
             tt(ind(T.TS[:, 0:TW], of), T.aE[:], T.aD[:], O.subtract, "aE aD ou0", "TS")
             for h in (0, 1):
-                vlist(h, 0)
+                for s in range(SP):
+                    vlist(h, s)
         tt(T.tot[:, 1:2], T.tot[:, 0:1], T.lT[:, 8 * t:8 * t + 1], O.min, "tot lT%d" % t, "tm1")
-        ts(T.tot[:, 2:3], T.tot[:, 1:2], float(CAP), O.min, "tm1", "tm2", -0.5, O.add)
-        ts(T.tot[:, 3:4], T.tot[:, 1:2], float(CAP), O.min, "tm1", "tm3", 0.5 - 4096, O.add)
-        ts(T.so[:], T.mL[:], T.tot[:, 2:3], O.is_gt, "mL tm2", "so", 4096.0, O.mult)
-        ts(T.nmv[:], T.X[:], T.tot[:, 3:4], O.is_gt, "X tm3", "nmv")
-        tt(T.so[:], T.so[:], lane, O.add, "so PX00", "so")
-        tt(T.cm[:], c16[:], T.nmv[:], O.mult, "c160 c161 nmv", "cm")
-        tt(T.so[:], T.so[:], T.Dm[:], O.min, "so Dm", "so")
+        ts(T.tot[:, 2:3], T.tot[:, 1:2], CAP - 2047.5, O.min, "tm1", "tm2", -400.0, O.mult)
+        act(T.nmv[:], T.X[:], AF.Sigmoid, "X tm2", "nmv", bias=T.tot[:, 2:3], scale=400.0)
+        act(T.X16[:], T.X[:], AF.Copy, "X", "X16")
+        slot = T.PX0[:, 640:768]
+        mm(acc(slot, [(m_(ID), T.X16[:]), (m_(P4), T.nmv[:])]), "ID P4 X16 nmv", "PX01")
+        ts(T.hu[:], slot, 2047.0, O.add, "PX01", "hu", float(CAP), O.min)
+        tt(T.cm[:], T.cf[:], T.nmv[:], O.mult, "cf nmv", "cm")
         if not last:
-            tt(sm(0), sm(0), T.nmv[:, 0:16], O.mult, "F nmv", "F")
-        cp(T.sou[:], T.so[:], "so", "sou")
-        cp(ind(T.H[:], T.sou[:]), T["lL%d" % t][:], "sou lL%d" % t, "H")
+            tt(T.so[:], slot, T.Dm[:], O.min, "PX01 Dm", "so")
+            ts(T.mu[:], T.so[:], 2047.0, O.add, "so", "mu")
+            act(sm(1), T.nmv[:, 0:16], AF.Identity, "nmv", "val", scale=65536.0, bias=-65536.0)
+            tt(sm(0), sm(0), sm(1), O.add, "F val", "F")
         for h in (0, 1):
-            mm(acc(PL[h][:, 320:384], [(m_(ID), T.cm[:, HC(h)])] + lsum(T.EH, T.H, 1024 * h, 1024 * h + 1024)), "ID cm EH H", K("PL@.y", h))
+            for b in (0, 1):
+                win = ind(T["mk%d" % t][:, 0:CS], T.hu[:, OB(h, b)])
+                if last and b:
+                    cp(T.H[:, HB(h, b)], win, "hu lz%d lL%d" % (t, t), K("H@#", h, b))
+                else:
+                    act(T.H[:, HB(h, b)], win, AF.Abs, "hu lz%d lL%d" % (t, t), K("H@#", h, b))
+            for bs in UNITS:
+                u, N, oc, pr = unit(h, bs)
+                y, yn = PL[h][:, 512 * bs[0] + 192:512 * bs[0] + 192 + 32 * len(bs)], K("PL@#.y", h, bs[0])
+                mm(acc(y, [(m_(ID), T.cm[:, oc])] + lsum(T.ES, T.H, 16 * oc.start, 16 * oc.stop)), "ID cm ES " + N("H"), yn)
+                if last:
+                    ts(T.cf[:, oc], y, -79.0, O.add, yn, N("cf"))
+                else:
+                    ts(T.cr[:, oc], y, -79.0 - CO - R12, O.add, yn, N("cr"))
+                    newc(h, bs)
+            if not last:
+                for b in (0, 1):
+                    win, r, w = ind(T["mk%d" % t][:], T.mu[:, OB(h, b)]), MKR % ((t,) * 4) + " mu lz%d lL%d" % (t, t), K("mk%d@#" % ((t + 1) % 2), h, b)
+                    if (h, b) in MKV:
+                        ts(marks(t + 1, h, b), win, 0.5, O.is_gt, r, w)
+                    else:
+                        act(marks(t + 1, h, b), win, AF.Sigmoid, r, w, bias=-200.0, scale=400.0)
         if last:
-            for h in (0, 1):
-                ts(T.cf[:, HC(h)], PL[h][:, 320:384], float(CO), O.add, K("PL@.y", h), K("cf@", h))
-            dma("A", T.yc[:, :], T.cf[:], "cf0 cf1", "yc", 64)
-        else:
-            zero(T.H, 0, LN, "H")
-            cp(ind(T.mk[:], T.sou[:]), T["lM%d" % t][:], "sou mkz lM%d" % t, "mk00 mk01 mk10 mk11")
-            for h in (0, 1):
-                newc(h, PL[h][:, 320:384], K("PL@.y", h), 0.0)
+            dma("A", T.yc[:, :], T.cf[:], "cf", "yc", 64)
     issue()

from concourse.mybir import AluOpType as O, ActivationFunctionType as AF

W0, B, LN, RO, SP, CAP = 3328, 256, 2048, 3, 3, 512
CS = CAP + 16
TW = 4096
CO = 1920
DU = 3840
D = 2.0 ** -13
KC = 63.0
PLAN = dict(V="q00 q01 a1- p00 u1- T00 q10 p01 x00 T01 x01 q11 p10 T10 x10 f0 p11 T11 x11 o0 Y01 g0 Y00 o1 Y10 Y11 a0 u0",
            A="m01- m10- R0- r1- m11- t00 t01 R1- e0 s01 t10 t11 s00 e1 s10 s11 m00 r0",
            P="M10- y1- W00 M11- W01 U01 U00 W10 U10 d0 X01 W11 c0 X00 X10 d1 U11 X11 c1 M00 y0 M01")
UNITS = ((0, 1),)
MKV = ()
MAG = 1.5 * 2.0 ** 27
R12 = 1.5 * 2.0 ** 19
NCH, CH = 4, 832
PC, NB4 = 416, 4
TAG = [""]
EST = dict(cy=0.83e-3, pe=0.42e-3, ga=1.56, two=0.0, sc=3.8, call=0.03, act=0.02, own=0.04, wait=0.24, dma=1.0, rem=1.8, turns=8)
ORDER = []


def _sb(dtype, **shapes):
    return {k: ("sbuf", [128] + ([n] if n > 0 else [-n, 128]), dtype) for k, n in shapes.items()}


SCRATCH = {}
SCRATCH.update(_sb("int32", tk=W0, ti=2 * PC, ip=128, im=128, pg=128, mg=128, pm=128, mm=128, m8=128, sfi=208, lki=208, lkj=208, cxi=128, fi=32))
SCRATCH.update(_sb("float32", TC=TW + 16, TS=TW + DU, tr=NB4 * PC, vl=768, xx=256, MK=2192, sm=192, RS=16, mrow=512, krow=128, mi=128, mL=128, Dm=128,
                   zz=128, cols=8, sff=208, cf=128, cr=128, I32=128, X=128, K=32, dk=32, dum=32, dus=32, mo=32, nu=256, u1=256, om=256, dsg=256, nD=256, aC=256, aD=256, aE=256,
                   aF=256, tot=8, lT=24, so=128, o8=16))
SCRATCH.update(_sb("bfloat16", vvr=SP * LN, s=LN, mk0=LN + CS, mk1=LN + CS, H=LN, nmv=128, EQ0=4096, EQ1=4096, yb=TW + 16, TL=4096, ES=-16, Dn=-16, E8=-8, EV=-8,
                   EW=-16, n128=1040, TR=-16, M=-19, one=16, cd=256, rt=128, ry=128, rb=NB4 * PC, eb=128, du=512, lhf=208, llf=208, Cb=256, Cc=256, nb=256, ob=256, ab=256, r2=256,
                   OH=512, MS=512, Lg=512, mk2=CS))
SCRATCH.update(_sb("float16", q=LN, Y=LN, p=256, th=256, c16=16, cm=128, X16=128, k1=64, sh=NB4 * PC, mmB=128, m8B=128, mmV=128, t16=128, o64=128, K16=32, R=512, inc=144,
                   kL=16, kr=512, CG=512, Yf=256, wn=512))
SCRATCH.update(_sb("uint16", cu=128, cu2=128, ou=32, su=16, ofu=8, klu=32, cmu=32, lnu=32, hu=128, mu=128))
SCRATCH.update({k: ("psum", [128, n], "float32") for k, n in (("PX0", 1024), ("PX1", 1024), ("PL0", 1024), ("PL1", 1024))})
DMAS = ["d%d" % i for i in range(24)]
REM = [a + str(t) for t in range(RO) for a in ("aT", "aL", "nT", "nL")]
SEMAPHORES = ["sV", "sA", "sP", "sG"] + DMAS + REM
BANKS = {"PX00", "PX01", "PX10", "PX11", "PL00", "PL01", "PL10", "PL11"}
BO, PRE, DX, ID, NI, NQ, N2, RL0, RL1, SL0, SL1, ZT, DL, DD, NB, IK, P4, SB0, SB1 = range(19)


def bank(k):
    k = k.split(".")[0]
    return k if k in BANKS else None


def order(ops):
    wr, rd, pre = {}, {}, []
    for n, o in enumerate(ops):
        p = {}
        for k in o["r"]:
            if k in wr:
                p[wr[k]] = max(p.get(wr[k], 0), k[0] != "*")
        for k in o["w"]:
            for j in rd.get(k, []) + ([wr[k]] if k in wr and o["q"] == "P" else []):
                p.setdefault(j, 0 if ops[j]["q"] == o["q"] == "P" else 1)
            if k in wr:
                p.setdefault(wr[k], -1 if k[0] == "~" else 1)
        p.pop(n, None)
        p = {j: EST["own"] / EST["wait"] if w == 1 and ops[j]["q"] == o["q"] and ops[j]["sem"] is None else w for j, w in p.items()}
        pre.append(p)
        for k in o["r"]:
            rd.setdefault(k, []).append(n)
        for k in o["w"]:
            wr[k], rd[k] = n, []
    N = len(ops)
    named = {o["lab"]: n for n, o in enumerate(ops)}
    for plan in PLAN.values():
        seq = [named.get((n - (x[-1] == "-"), x.strip("-"))) for n in range(RO * SP + 1)
               for x in sorted(plan.split(), key=lambda x: n % SP == 0 and x[-1] != "-")]
        seq = [n for n in seq if n is not None]
        for j, n in zip(seq, seq[1:]):
            pre[n].setdefault(j, -1)
    suc = [{} for _ in ops]
    for n, p in enumerate(pre):
        for j, w in p.items():
            suc[j][n] = w

    def place(seq, dep, back):
        st, busy = [0.0] * N, {}
        for n in seq:
            o = ops[n]
            t = max([st[j] + ops[j]["c"] + (0.0 if w < 0 else ops[n if back else j]["lat"] + EST["wait"] * w) for j, w in dep[n].items()], default=o["lat"] if back else 0.0)
            res = [(o["q"], 0.0)] + [(b, EST["wait"]) for b in o["b"]]
            moved = True
            while moved:
                moved = False
                for r, gap in res:
                    for a, e, q in busy.get(r, []):
                        m = gap if q != o["q"] else 0.0
                        if a - m < t + o["c"] - 1e-9 and t < e + m - 1e-9:
                            t, moved = e + m, True
            st[n] = t
            for r, gap in res:
                x = busy.setdefault(r, [])
                k = len(x)
                while k and x[k - 1][0] > t:
                    k -= 1
                x.insert(k, (t, t + o["c"], o["q"]))
        return st

    def end(st):
        return max(st[n] + ops[n]["c"] + ops[n]["lat"] for n in range(N))
    todo = [len(p) for p in pre]
    top = [n for n in range(N) if not todo[n]]
    for n in top:
        for j in suc[n]:
            todo[j] -= 1
            if not todo[j]:
                top.append(j)
    way = [0.0] * N
    for n in top[::-1]:
        way[n] = ops[n]["c"] + max([ops[n]["lat"]] + [way[j] + (0.0 if w < 0 else ops[n]["lat"] + EST["wait"] * w) for j, w in suc[n].items()])
    st = best = place(sorted(range(N), key=lambda n: (-way[n], n)), pre, False)
    for _ in range(EST["turns"]):
        bk = place(sorted(range(N), key=lambda n: (-(st[n] + ops[n]["c"] + ops[n]["lat"]), -n)), suc, True)
        st = place(sorted(range(N), key=lambda n: (-(bk[n] + ops[n]["c"]), n)), pre, False)
        if end(st) < end(best):
            best = st
    TAG.append(end(best))
    return sorted(range(N), key=lambda n: (best[n], n))


def rank_program(g, core, T, topo):
    rank = T.rank_of(core)
    if rank is None:
        return
    V, A, P, S = g.vector, g.scalar, g.tensor, g.sync
    eng = {"V": V, "A": A, "P": P, "S": S, "G": g}
    ops, alias, ndma, label = [], {}, [0], [None]

    def run(qn, fn, r, w, c, sem=None, remote=False, n=1, lat=0.0):
        r = [x for k in r.split() for x in alias.get(k, [k])]
        w = w.split()
        ops.append(dict(q=qn, fn=fn, r=r, w=w, c=c, sem=sem, remote=remote, n=n, lat=lat, b={bank(k) for k in r + w} - {None}, tag=TAG[0], lab=label[0]))
        label[0] = None

    def issue():
        seen = {k: {} for k in eng}
        cnt = {k: 0 for k in "VAPG"}
        wr, rd, bk, left = {}, {}, {}, {}
        if not ORDER:
            ORDER.extend(order(ops))
        for n in ORDER:
            o = ops[n]
            qn, sem = o["q"], o["sem"]
            own, need = "s" + qn, {}

            def want(toks, skip):
                for s, v in toks.items():
                    if not (skip and s == own):
                        need[s] = max(need.get(s, 0), v)
            for k in o["r"]:
                want(wr.get(k, {}), qn == "P" and k[0] == "*")
            for k in o["w"]:
                want(wr.get(k, {}) if k[0] != "~" else {}, qn == "P")
                want(rd.get(k, {}), qn == "P")
            for b in o["b"]:
                want(bk.get(b, {}), True)
            for s in sorted(need):
                if seen[qn].get(s, 0) < need[s]:
                    eng[qn].wait_ge(T.sem[s], need[s])
                    seen[qn][s] = need[s]
            TAG[0] = o["tag"]
            inst = o["fn"]()
            if sem is None:
                cnt[qn] += 1
                s, v = own, cnt[qn]
            else:
                s, v = sem, o["n"]
            if not o["remote"]:
                inst.then_inc(T.sem[s], o["n"])
            left[s] = v
            for k in o["r"]:
                rd.setdefault(k, {})[s] = v
            for k in o["w"]:
                wr[k], rd[k] = {s: v}, {}
            if o["remote"]:
                wr[o["w"][0]] = {"a" + s[1:]: v}
                left["a" + s[1:]] = v
            for b in o["b"]:
                bk.setdefault(b, {})[s] = v
        for s in sorted(left):
            if seen["G"].get(s, 0) < left[s]:
                g.wait_ge(T.sem[s], left[s])

    def size(ap):
        n = 1
        for d in ap.shape[1:]:
            n *= d
        return n

    def ind(win, off):
        return (win.indirect(off), 16 * off.shape[1])

    def cost(out, ins, r, w, two=False, fast=True):
        if isinstance(out, tuple):
            return 0.05 + out[1] * EST["sc"] * EST["cy"]
        if ins and isinstance(ins[0], tuple):
            return 0.05 + ins[0][1] * (EST["ga"] + two * EST["two"]) * EST["cy"]
        ps = any(bank(k) for k in (r + " " + w).split())
        rate = (1.0 if ps else 2.0) if two else 0.5 if fast and all("16" in str(a.dtype) for a in [out] + ins) else 1.0
        return EST["call"] + max(64, size(out) * rate) * EST["cy"]

    def ap(x):
        return x[0] if isinstance(x, tuple) else x

    def dma(qn, out, in_, r, w, kb, add=False):
        s = DMAS[ndma[0]]
        ndma[0] += 1
        more = dict(accum_op=O.add) if add else {}
        run(qn, lambda: eng[qn].dma_start(out, in_, **more), r, w, 0.05, sem=s, n=16, lat=EST["dma"] + kb / 180.0)

    def ts(out, in0, s1, op0, r, w, s2=None, op1=None):
        c = cost(out, [in0], r, w)
        if op1 is None:
            run("V", lambda: V.tensor_scalar(out, ap(in0), s1, None, op0), r, w, c)
        else:
            run("V", lambda: V.tensor_scalar(out, ap(in0), s1, s2, op0, op1), r, w, c)

    def tt(out, in0, in1, op, r, w):
        run("V", lambda: V.tensor_tensor(ap(out), ap(in0), in1, op), r, w, cost(out, [in0, in1], r, w, True))

    def cp(out, in_, r, w):
        run("V", lambda: V.tensor_copy(ap(out), ap(in_)), r, w, cost(out, [in_], r, w))

    def fill(out, x, w):
        run("V", lambda: V.memset(out, x), "", w, cost(out, [], "", w))

    def scan(out, a, b, op, r, w):
        run("V", lambda: V.tensor_tensor_scan(out, a, b, 0.0, op, op), r, w, cost(out, [a], r, w, fast=False))

    def act(out, in_, func, r, w, bias=0.0, scale=1.0):
        run("A", lambda: A.activation(out, ap(in_), func, bias=bias, scale=scale), r, w,
            cost(out, [in_], r, w, fast=False) + (0.0 if isinstance(in_, tuple) else EST["act"]))

    def mm(group, r, w, more=False):
        def f():
            for n, (o, l, x, st) in enumerate(group):
                i = P.matmul(o, l, x, st, group[n + 1][3] if n + 1 < len(group) else not more)
            return i
        star = " ".join({"*" + bank(k) for k in w.split()})
        c = sum(max(64, size(x)) for o, l, x, st in group) * EST["pe"]
        if more or not group[0][3]:
            run("P", f, r, w + " " + star, c)
        else:
            run("P", f, r + " " + star, w, c)

    def acc(out, terms, start=True):
        return [(out, l, x, start and n == 0) for n, (l, x) in enumerate(terms)]

    def lsum(fam, src, lo, hi, n=16):
        return [(fam[:, i, :], src[:, lo + i:hi:n]) for i in range(n)]

    def spread(out, base, w, src, n, start):
        return [(out[:, base + i:base + w:n], T.Dn[:, i, :], src, start) for i in range(n)]

    def m_(k):
        return T.M[:, k, :]

    nxt = T.cores[(rank + 1) % len(T.cores)]
    rid, pid, _se = topo.addr(nxt)
    emask = topo.mask(core, nxt)
    ne = len(topo.engines(core, nxt))

    def send(dst, src, name, t, r, kb):
        s, rs = "n%s%d" % (name, t), "a%s%d" % (name, t)
        run("G", lambda: g.remote_dma(dst, src, T.sem[rs], T.sem[s], pid, rid, emask), r, "l%s%d" % (name, t), 0.1, sem=s, remote=True, n=ne,
            lat=EST["rem"] + kb / 45.0 + (2.0 if t == 0 and name == "T" else 0.0))

    def sm(k):
        return T.sm[:, 16 * k:16 * k + 16]

    def loadv(qn, t):
        dma(qn, T.vvr[0:8, :], T.vv[:, SP * LN * t:SP * LN * (t + 1)], "", "vvr", 100)

    PX, PL = (T.PX0, T.PX1), (T.PL0, T.PL1)

    def K(s, h, b=0):
        return s.replace("@", str(h)).replace("#", str(b))

    def vlist(h, s):
        lo, o, on = LN * s + 1024 * h, PL[h][:, 896 - 512 * (s % 2):1024 - 512 * (s % 2)], K("PL@#.v", h, 1 - s % 2)
        mm(acc(o, [(T.EV[0:8, j, :], T.vvr[0:8, lo + j:lo + 1024:8]) for j in range(8)]), "EV vvr", on)
        act(T.vl[:, 384 * h + 128 * s:384 * h + 128 * s + 128], o, AF.Copy, on, K("vl@#", h, s), scale=0.25)

    loadv("A", 0)
    for k in range(NCH):
        dma("S", T.tk[:, k * CH:(k + 1) * CH], T.tab[:, k * CH:(k + 1) * CH], "", "~S tk%d" % k, 100 + 430 * (k + 1) + (70 if k > 0 else 0))
        if k == 0:
            dma("S", T.cxi[:], T.cx[:, :], "", "~S cxi", 600)
        if k == 3:
            dma("S", T.sfi[:], T.suf[:, :], "", "~S sfi", 2000)
    dma("S", T.lki[:], T.lnk[:, :], "", "~S lki", 2100)

    def iota(out, pat, base, cm, w, small=True):
        c = 0.13 + 2 * size(out) * EST["cy"]
        if small:
            run("G", lambda: g.iota(out, pat, base, cm, allow_small_or_imprecise_dtypes=True), "", w, c)
        else:
            run("G", lambda: g.iota(out, pat, base, cm), "", w, c)

    def select(out, in_, pat, op, x, base, cm, r, w):
        run("G", lambda: g.affine_select(out, in_, pat, op, x, base, cm), r, w, 0.17 + 2 * size(out) * EST["cy"])

    def zero(buf, lo, hi, w, n=1):
        st = (hi - lo) // n
        for k in range(n):
            iota(buf[:, lo + k * st:lo + (k + 1) * st], [[0, st]], 0, 0, w if n == 1 else "%s_%d" % (w, k))
        if n > 1:
            alias[w] = ["%s_%d" % (w, k) for k in range(n)]
    iota(T.ip[:], [[0, 128]], 0, 1, "ip", False)
    iota(T.im[:], [[1, 128]], 0, 0, "im", False)
    zero(T.TC, W0, TW + 16, "TCz")
    zero(T.TS, TW, TW + DU, "TSF0")
    zero(T.TS, W0, TW, "TSz")
    iota(T.mi[:], [[16, 128]], 0, 0, "mi")
    iota(T.krow[:], [[1, 128]], 0, 0, "krow")
    zero(T.MK, 0, 2192, "MK")
    iota(T.TL[:], [[0, 4096]], 1, 0, "TL")
    iota(T.mrow[:], [[1, 512]], 1 - 2048, 0, "mrow")
    zero(T.zz, 0, 128, "zz")
    iota(sm(0), [[0, 16]], -900000, 0, "F")
    iota(T.one[:], [[0, 16]], 1, 0, "one")

    def fam(name, key, n, kn, rows=128, x=1.0):
        for i in range(n):
            ts(T[name][0:rows, i, :], key[0:rows, :], float(i), O.is_equal, kn, "%s_%d" % (name, i), x, O.mult)
        alias[name] = ["%s_%d" % (name, i) for i in range(n)]

    ts(T.pg[:], T.ip[:], 4, O.arith_shift_right, "ip", "pg")
    ts(T.mg[:], T.im[:], 4, O.arith_shift_right, "im", "mg")
    ts(T.pm[:], T.ip[:], 15, O.bitwise_and, "ip", "pm")
    ts(T.mm[:], T.im[:], 15, O.bitwise_and, "im", "mm")
    ts(T.m8[:], T.im[:], 7, O.bitwise_and, "im", "m8")
    tt(m_(BO), T.pg[:], T.mg[:], O.is_equal, "pg mg", "BO")
    tt(T.RS[:], T.pm[:, 0:16], T.mm[:, 0:16], O.is_equal, "pm mm", "RS")
    tt(T.mmV[:], T.mg[:], T.ip[:], O.not_equal, "mg ip", "mmV")
    ts(T.o64[:], m_(BO), -64.0, O.mult, "BO", "o64", 64.0, O.add)
    ts(T.mmV[:], T.mmV[:], 64.0, O.mult, "mmV", "mmV")
    tt(T.m8B[:], T.m8[:], T.o64[:], O.add, "m8 o64", "m8B")
    tt(T.mmV[:], T.mmV[:], T.m8[:], O.add, "mmV m8", "mmV")
    tt(T.mmB[:], T.mm[:], T.o64[:], O.add, "mm o64", "mmB")
    fam("EV", T.mmV, 8, "mmV", 8)
    fill(T.k1[:], 1025.0, "k1")
    act(T.cols[:, 7:8], T.RS[:, 0:1], AF.Copy, "RS", "cl7", scale=64.0 / 63)
    fam("E8", T.m8B, 8, "m8B", x=1.0 / 64)
    fam("ES", T.mmB, 16, "mmB")
    zero(T.H, 0, 1024, "H00 H01")
    for k in (0, 1):
        select(T.Dn[:, 8 * k:8 * k + 8, :], T.H[:, 0:1024], [[-1, 8], [-16, 8], [0, 16]], O.not_equal, 63.0 / 64, -8 * k, 1, "H00 H01", ("Dn8", "Dn9")[k])
    alias["Dn"] = ["Dn8", "Dn9"]
    cu, rt = T.cu, T.rt
    cp(cu[:], T.cxi[:], "cxi", "cu00 cu01 cu10 cu11")
    ts(T.cr[:], T.cxi[:], -CO - R12, O.add, "cxi", "cr00 cr01 cr10 cr11")
    act(rt[:], T.cr[:], AF.Sigmoid, "cr00 cr01 cr10 cr11", "rt00 rt01 rt10 rt11 ~A", bias=256.0 - 512.0 * (CO + R12), scale=-512.0)
    ops[-1]["c"] += 1.3
    ts(T.sff[:], T.sfi[:], -float(CO), O.add, "sfi", "sff")
    dma("S", T.TS[0:128:16, TW:TW + W0], T.sff[:], "sff TSF0", "TSF", 110)
    ts(T.cols[:, 0:1], T.pm[:, 0:1], 0.0, O.add, "pm", "cl0")
    ts(T.t16[:], T.mmB[:], T.cols[:, 0:1], O.subtract, "mmB cl0", "t16")
    ts(m_(ID), T.t16[:], 0.0, O.is_equal, "t16", "ID")
    ts(m_(DL), T.t16[:], 1.0, O.is_equal, "t16", "DL")
    ts(m_(ZT), T.t16[:], 0.5, O.is_gt, "t16", "ZT")
    tt(m_(DX), m_(ID), m_(DL), O.subtract, "ID DL", "DX")
    tt(m_(ZT), m_(ZT), m_(BO), O.mult, "ZT BO", "ZT")
    act(m_(PRE), m_(ZT), AF.Copy, "ZT", "PRE", scale=-1.0 / 64)
    for k, kn, x in ((NI, "NI", -1.0), (NQ, "NQ", -1.0 / 1024), (P4, "P4", 4096.0), (N2, "N2", -2048.0), (IK, "IK", 1.0 / 4096)):
        select(m_(k), T.H[:, 0:128], [[-1, 128]], O.not_equal, x, 0, 1, "H00", kn)
    ts(T.cols[:, 1:2], T.pm[:, 0:1], 7.5, O.is_lt, "pm", "cl1", -4096.0, O.mult)
    ts(T.cols[:, 2:3], T.pm[:, 0:1], 7.5, O.is_gt, "pm", "cl2", -4096.0, O.mult)
    ts(T.cols[:, 3:4], T.pm[:, 0:1], -8.0, O.add, "pm", "cl3")
    ts(m_(RL0), T.m8B[:], T.cols[:, 0:1], O.is_equal, "m8B cl0", "RL0", -512.0, O.mult)
    ts(m_(RL1), T.m8B[:], T.cols[:, 3:4], O.is_equal, "m8B cl3", "RL1", -512.0, O.mult)
    act(m_(SL0), m_(ID), AF.Copy, "ID cl1", "SL0", scale=T.cols[:, 1:2])
    act(m_(SL1), m_(ID), AF.Copy, "ID cl2", "SL1", scale=T.cols[:, 2:3])
    for b in (0, 1):
        ts(m_(SB0 + b), m_(SL0 + b), 16.0, O.mult, "SL%d" % b, "SB%d" % b)
    ts(T.I32[:], T.t16[:], 0.0, O.is_equal, "t16", "I32")
    for h in (0, 1):
        for s in range(SP):
            vlist(h, s)

    NP = W0 // PC
    for k in range(NP):
        sl = slice(k * PC, (k + 1) * PC)
        ti, tn = T.ti[:, PC * (k % 2):PC * (k % 2 + 1)], "ti%d" % (k % 2)
        ts(ti, T.tk[:, sl], 15, O.bitwise_and, "tk%d" % (k // 2), tn)
        ts(T.TC[:, sl], ti, -1.0 / KC, O.add, tn, "TC_%d" % k, -D / KC, O.max)
        act(T.TC[:, sl], T.TC[:, sl], AF.Copy, "TC_%d" % k, "TC_%d" % k + " ~A" * (k == 2), scale=KC)
    for k in range(NP):
        sl = slice(k * PC, (k + 1) * PC)
        b = k % NB4
        o = slice(b * PC, (b + 1) * PC)
        ps, pn = PX[b // 2][:, 512 * (b % 2):512 * (b % 2) + PC], ("PX00", "PX01", "PX10", "PX11")[b]
        ts(T.tr[:, o], T.tk[:, sl], -7.5, O.add, "tk%d" % (k // 2), "tr%d" % b, MAG, O.add)
        act(T.sh[:, o], T.tr[:, o], AF.Identity, "tr%d" % b, "sh%d" % b, bias=-(MAG / 16) - CO, scale=1.0 / 16)
        mm(acc(ps, [(m_(DX), T.sh[:, o])]), "DX sh%d" % b, pn)
        act(T.rb[:, o], ps, AF.Identity, pn, "rb%d" % b, bias=R12)
        mm(acc(ps, [(m_(DX), T.sh[:, o]), (m_(NI), T.rb[:, o])]), "DX NI sh%d rb%d" % (b, b), pn)
        act(T.TS[:, sl], ps, AF.Identity, pn, "TS_%d" % k, bias=R12)

    fill(T.inc[:, 0:16], 0.0, "inc")
    fill(T.nD[:], -D, "nD")
    ts(T.lkj[:], T.lki[:], 6, O.arith_shift_right, "lki", "lkj")
    ts(T.lki[:], T.lki[:], 63, O.bitwise_and, "lki", "lki")
    ts(T.lhf[:], T.lkj[:], 1.0, O.add, "lkj", "lhf", 64.0, O.mult)
    ts(T.llf[:], T.lki[:], 1.0, O.add, "lki", "llf")
    act(T.cols[:, 4:5], T.RS[:, 0:1], AF.Identity, "RS", "cl4", scale=CO + 63.0, bias=1.0)
    for t in range(RO):
        act(T["mk%d" % t][:, CAP:CS], T.RS[:], AF.Identity, "RS cl4", "lz%d" % t, scale=0.0, bias=T.cols[:, 4:5])
    dma("S", T.TL[0:128:16, 0:W0], T.lhf[:], "lhf TL", "TLa", 60)
    dma("S", T.TL[1:128:16, 0:W0], T.llf[:], "llf TL", "TLb", 60)
    act(T.mL[:], T.mi[:], AF.Identity, "mi cl0", "mL", bias=T.cols[:, 0:1])
    act(T.Dm[:], T.mL[:], AF.Identity, "mL", "Dm", bias=float(CS - 2047))
    for x in (0, 1):
        act(T.dum[:, 16 * x:16 * x + 16], T.mL[:, 0:16], AF.Identity, "mL", "dum%d" % x, bias=float(DU - 2048))
    act(T.kL[:, 0:8], T.mL[:, 0:8], AF.Copy, "mL", "kL")
    act(T.dus[:], T.dum[:], AF.Copy, "dum0 dum1", "dus", scale=1.0 / 4096)
    ts(m_(ZT), T.t16[:], -0.5, O.is_lt, "t16 PRE", "ZT", -1.0, O.mult)
    ts(m_(DD), T.t16[:], -1.0, O.is_equal, "t16", "DD")
    act(m_(NB), m_(BO), AF.Copy, "BO", "NB", scale=-1.0)
    tt(m_(DL), m_(ID), m_(DD), O.subtract, "ID DD", "DL")
    for k in range(4):
        act(T.EW[:, 4 * k:4 * k + 4, :], T.ES[:, 4 * k:4 * k + 4, :], AF.Copy, "ES cl0", "EW%d" % k, scale=T.cols[:, 0:1])
    alias["EW"] = ["EW0", "EW1", "EW2", "EW3"]
    select(T.TR[:], T.ES[:], [[1, 16], [16, 8], [0, 16]], O.is_gt, 0.0, 0, -1, "ES", "TR")
    tt(m_(DD), m_(DL), m_(DX), O.add, "DL DX", "DD")
    ts(T.cols[:, 6:7], T.RS[:, 0:1], -1.0, O.mult, "RS", "cl6")
    for t in range(RO - 1):
        act(T.wn[:, B * t:B * t + B], T.mrow[:, 0:256], AF.Identity, "mrow", "wr%d" % t, bias=float(2047 + W0 + B * t - CO))
    iota(T.n128[:], [[0, 1040]], -128, 0, "n128")

    TCR = "TC TCz " + " ".join("TC_%d" % k for k in range(NP))
    TSR = "TS TSz TSF TSF0 " + " ".join("TS_%d" % k for k in range(NP))
    TLR = "TL TLa TLb"
    YBR = "yb " + " ".join("yb%d" % k for k in range(8))

    def HB(h, b):
        return slice(1024 * h + 512 * b, 1024 * h + 512 * b + 512)

    def HC(h):
        return slice(64 * h, 64 * h + 64)

    def OB(h, b):
        return slice(64 * h + 32 * b, 64 * h + 32 * b + 32)

    def marks(t, h, b):
        o = CS + 1024 * h + 512 * b
        return T["mk%d" % (t % 2)][:, o:o + 512]
    MKR = "mk%d00 mk%d01 mk%d10 mk%d11"

    def unit(h, bs):
        return (str(h) + (str(bs[0]) if len(bs) == 1 else ""), lambda x: " ".join(K(k + "@#", h, b) for k in x.split() for b in bs),
                slice(64 * h + 32 * bs[0], 64 * h + 32 * bs[-1] + 32), slice(128 * h + 64 * bs[0], 128 * h + 64 * bs[-1] + 64))
    for x in ("eb", "cf"):
        alias[x] = [x + k for k in ("00", "01", "10", "11")]

    def newc(h, bs, n=None):
        u, N, oc, pr = unit(h, bs)
        label[0] = (n, "u" + u)
        ts(cu[:, oc], T.cr[:, oc], R12 + CO, O.add, N("cr"), N("cu"))
        label[0] = (n, "R" + u)
        act(rt[:, oc], T.cr[:, oc], AF.Relu, N("cr"), N("rt"), bias=1.0 - CO - R12, scale=-1.0)

    def flist(n, s):
        age = T.PL0[:, 320:336]
        mm(acc(age, [(m_(P4), T.one[:])] + [(m_(SB0 + b), T.cd[:, b:32:2]) for b in (0, 1)]), "P4 one SB0 SB1 cd00", "PL00.a")
        if s == SP - 1:
            act(T.r2[:, 0:16], sm(0), AF.Identity, "F", "r2", bias=2 * R12)
            tt(sm(3), age, sm(0), O.subtract, "PL00.a F", "hf")
            tt(sm(2), sm(0), T.r2[:, 0:16], O.subtract, "F r2", "fj")
            for x, key, kn in ((0, sm(2), "fj"), (1, T.cr[:, 0:16], "cr00")):
                o, base = slice(16 * x, 16 * x + 16), (2 - x) * R12 + CO - 2048
                ts(T.dk[:, o], sm(3), base + 61440.0 - 790000.0, O.add, "hf", "dk%d" % x, base, O.max)
                tt(T.dk[:, o], T.dk[:, o], key, O.add, "dk%d %s" % (x, kn), "dk%d" % x)
            tt(T.K[:], T.dk[:], T.dum[:], O.min, "dk0 dk1 dum0 dum1", "K")
        if n < RO * SP - 1:
            label[0] = (n, "f0")
            tt(sm(1), T.cr[:, 0:16], sm(0), O.max, "cr00 F", "val")
            label[0] = (n, "g0")
            tt(sm(0), age, sm(1), O.add, "val PL00.a", "F")

    def ranks(t):
        tot = T.PL1[:, 896:1024]
        mm(acc(tot, [(m_(BO), T.eb[:])]), "BO eb", "PL11.v")
        mm(acc(T.PL1[:, 320:328], [(m_(IK), T.kL[:, 0:8])] + lsum(T.ES, T.eb, 0, 128)), "IK kL ES eb", "PL10.a")
        mm(acc(T.PL1[:, 384:512], [(m_(ZT), T.eb[:]), (m_(N2), T.eb[:])]), "ZT N2 eb", "PL10.v")
        scan(T.inc[:, 1:129], tot, T.zz[:], O.add, "PL11.v zz", "inc")
        mm(acc(T.PL1[:, 832:840], lsum(T.ES, T.inc, 0, 128)), "inc ES", "PL11.a")
        act(T.tot[:, 0:1], T.inc[:, 128:129], AF.Identity, "inc", "tot", bias=-2047.5)
        send(T.lT[:, 8 * t:8 * t + 1], T.tot[:, 0:1], "T", t, "tot", 1)
        ts(T.o8[:, 0:8], T.PL1[:, 832:840], 2048.0, O.add, "PL11.a", "o8a", 2.0 ** -16, O.mult)
        tt(T.X[:], T.inc[:, 1:129], T.PL1[:, 384:512], O.add, "inc PL10.v", "X")
        tt(T.o8[:, 8:16], T.o8[:, 0:8], T.PL1[:, 320:328], O.min, "o8a PL10.a", "o8b")
        ts(T.ofu[:], T.o8[:, 8:16], 4096.0, O.mult, "o8b", "ofu")
        cp(ind(T.MK[:], T.ofu[:]), T.krow[:], "krow ofu", "MK")
        scan(T.kr[:], T.MK[:, 128:640], T.MK[:, 128:640], O.max, "MK", "kr")
        if t < RO - 1:
            zero(T.MK, 0, 640, "MK")

    def keys(last):
        act(T.K16[:], T.K[:], AF.Copy, "K", "K16")
        for x in (0, 1):
            o, on = 768 - 512 * x, "PL0#.c PL0#.a PL0#.v".replace("#", str(1 - x))
            mm(spread(T.PL0, o, 256, T.K16[:, 16 * x:16 * x + 16], 16, True), "K16 Dn", on)
            act(T.R[:, 256 * x:256 * x + 256], T.PL0[:, o:o + 256], AF.Copy, on, "R%d" % x, scale=64.0 / 63)
        oh = T.PX0[:, 0:256]
        mm(acc(oh, [(m_(DL), T.s[:, 0:256])]) + ([] if last else acc(T.PX0[:, 256:512], [(m_(DD), T.s[:, 0:256])])), "DL DD s00", "PX00")
        if last:
            act(T.nb[:], oh, AF.Identity, "PX00", "nu", bias=1.0, scale=-1.0)
            act(T.ob[:], oh, AF.Copy, "PX00", "u1")
        else:
            act(T.nu[:], oh, AF.Identity, "PX00", "nu", bias=1.0, scale=-1.0)
            act(T.u1[:], oh, AF.Copy, "PX00", "u1", scale=KC - 1)
            act(T.dsg[:], T.PX0[:, 256:512], AF.Identity, "PX00 cl6", "dsg", bias=T.cols[:, 6:7])

    def step(h, t, s):
        n, wt = SP * t + s, W0 + B * t
        L = PL[h]

        def lab(x, b=0):
            label[0] = (n, K(x, h, b))
        for b in (0, 1):
            win = ind(T.TC[:, 0:wt], cu[:, OB(h, b)])
            w, wn, pr = L[:, 512 * b:512 * b + 64], K("PL@#.w", h, b), slice(128 * h + 64 * b, 128 * h + 64 * b + 64)
            X, xn = PX[h][:, 512 * b:512 * b + 512], K("PX@#", h, b)
            lab("q@#", b)
            if n == 0:
                cp(T.q[:, HB(h, b)], win, TCR[7:] + K(" cu@#", h, b), K("q@#", h, b))
            else:
                tt(T.q[:, HB(h, b)], win, marks(t, h, b), O.mult, TCR + K(" cu@# mk%d@#" % (t % 2), h, b), K("q@#", h, b))
            lab("W@#", b)
            mm(acc(w, [(m_(ID), T.k1[:])] + lsum(T.E8, T.q, 1024 * h + 512 * b, 1024 * h + 512 * b + 512, 8)), K("ID k1 E8 q@#", h, b), wn)
            lab("p@#", b)
            ts(T.p[:, pr], w, 64.0 / 63, O.mult, wn, K("p@#", h, b), -1025.0 / 63, O.add)
            lab("T@#", b)
            tt(w, T.p[:, pr], w, O.subtract, wn + K(" p@#", h, b), wn)
            lab("x@#", b)
            tt(T.xx[:, pr], w, T.vl[:, 384 * h + 128 * s + 64 * b:384 * h + 128 * s + 64 * b + 64], O.mult, wn + K(" vl@#", h, s), K("xx@#", h, b))
            lab("t@#", b)
            act(T.th[:, pr], T.xx[:, pr], AF.Identity, K("xx@#", h, b), K("th@#", h, b), bias=1024.5015)
            lab("U@#", b)
            mm([(X, m_(PRE), T.q[:, HB(h, b)], True)], K("q@# PRE", h, b), xn, True)
            lab("X@#", b)
            mm(spread(PX[h], 512 * b, 512, T.th[:, pr], 8, False), K("th@# Dn8", h, b), xn)
            lab("s@#", b)
            act(T.s[:, HB(h, b)], X, AF.Sigmoid, xn, K("s@#", h, b), bias=600.0 * (23.5 - 63 * 1025) / 64, scale=600.0)
        for bs in UNITS:
            u, N, oc, pr = unit(h, bs)
            b0, b1, k = 512 * bs[0], 512 * bs[-1], len(bs)
            d, dn, c, cn = L[:, b0 + 64:b0 + 64 + 64 * k], K("PL@#.d", h, bs[0]), L[:, b1 + 256:b1 + 256 + 32 * k], K("PL@#.c", h, bs[-1])
            label[0] = (n, "d" + u)
            mm(acc(d, [(m_(ID), T.th[:, pr]), (m_(NI), T.p[:, pr])]) +
               [(L[:, b0 + 64 + b:b0 + 64 + 64 * k:2], m_(RL0 + b), rt[:, oc], False) for b in (0, 1)], N("th p rt") + " ID NI RL0 RL1", dn)
            label[0] = (n, "e" + u)
            act(T.cd[:, pr], d, AF.Sigmoid, dn, N("cd"), bias=-200.0, scale=-400.0)
            label[0] = (n, "c" + u)
            mm(acc(c, [(T.I32[:], T.cr[:, oc])] + [(m_(SL0 + b), T.cd[:, pr.start + b:pr.stop:2]) for b in (0, 1)]), N("cr cd") + " I32 SL0 SL1", cn)
            ops[-1]["c"] += 192 * EST["pe"]
            label[0] = (n, "o" + u)
            ts(T.cu2[:, oc], c, R12 + TW + CO, O.add, cn, N("cu2"))
            if s == SP - 1:
                ts(T.eb[:, oc], c, -R12 - 2100.0, O.is_gt, cn, N("eb"))
        if h == 0:
            flist(n, s)
        elif s == SP - 1:
            ranks(t)
        for b in (0, 1):
            lab("Y@#", b)
            tt(T.Y[:, HB(h, b)], ind(T.TS[:, 0:TW + wt], T.cu2[:, OB(h, b)]), T.s[:, HB(h, b)], O.mult, TSR + K(" cu2@# s@#", h, b), K("Y@#", h, b))
            if n < RO * SP - 1:
                X, xn = PX[h][:, 512 * b:512 * b + 512], K("PX@#", h, b)
                lab("M@#", b)
                mm([(X, m_(NQ), T.q[:, HB(h, b)], True)] +
                   spread(PX[h], 512 * b, 512, T.cd[:, 128 * h + 64 * b:128 * h + 64 * b + 64], 8, False), K("q@# cd@# NQ Dn8", h, b), xn)
                lab("m@#", b)
                act(marks(t, h, b), X, AF.Sigmoid, xn, K("mk%d@#" % (t % 2), h, b), bias=-200.0, scale=400.0 * 1024 / D)
        for bs in UNITS:
            u, N, oc, pr = unit(h, bs)
            y, yn = L[:, 512 * bs[0] + 192:512 * bs[0] + 192 + 32 * len(bs)], K("PL@#.y", h, bs[0])
            label[0] = (n, "y" + u)
            mm(acc(y, lsum(T.ES, T.Y, 16 * oc.start, 16 * oc.stop)), N("Y") + " ES", yn)
            label[0] = (n, "r" + u)
            act(T.ry[:, oc], y, AF.Identity, yn, N("ry"), bias=R12)
            label[0] = (n, "a" + u)
            tt(T.cr[:, oc], y, T.ry[:, oc], O.subtract, yn + " " + N("ry"), N("cr"))
            if s < SP - 1:
                newc(h, bs, n)
            else:
                act(T.cf[:, oc], T.cr[:, oc], AF.Identity, N("cr"), N("cf"), bias=R12)
        if s == SP - 1 and h == 0 and t < RO - 1:
            ts(cu[:, 0:16], T.cr[:, 0:16], R12 + CO, O.add, "cr00", "cu00")
            act(T.c16[:], T.cr[:, 0:16], AF.Identity, "cr00", "c16", bias=R12)

    def firsts(x):
        E, En = T["EQ%d" % x], " ".join("E%d_%d" % (x, k) for k in range(16))
        for k in range(16):
            ts(E[:, 256 * k:256 * k + 256 - 16 * k], T.R[:, 256 * x + 16 * k:256 * x + 256], T.K[:, 16 * x + k:16 * x + k + 1],
               O.is_equal, "R%d K" % x, "E%d_%d" % (x, k))
        ps, pn = T.PX1[:, 512 * x:512 * x + 512], "PX1%d" % x
        mm([(ps[:, 16 * k + 16:256], m_(BO), E[:, 256 * k + 16:256 * k + 256 - 16 * k], k == 0) for k in range(15)], "BO " + En, pn)
        act(T.du[:, 256 * x + 16:256 * x + 256], ps[:, 16:256], AF.Copy, pn, "du%d" % x)
        mm(acc(ps[:, 256:272], [(m_(IK), T.K16[:, 16 * x:16 * x + 16])] + [(T.TR[:, i, :], E[:, i:4096:256]) for i in range(16)]), "IK K16 TR " + En, pn, True)
        mm(acc(ps[:, 257:272], lsum(T.ES, T.du, 256 * x + 16, 256 * x + 256), False), "ES du%d" % x, pn)
        o = slice(16 * x, 16 * x + 16)
        tt(T.mo[:, o], ps[:, 256:272], T.dus[:, o], O.min, pn + " dus", "mo%d" % x)
        ts(T.ou[:, o], T.mo[:, o], 4096.0, O.mult, "mo%d" % x, "ou%d" % x, 2048.0, O.add)

    for t in range(RO):
        last, wt = t == RO - 1, W0 + B * t
        if last:
            for k in range(8):
                o = slice(520 * k, min(520 * (k + 1), TW + 16))
                act(T.yb[:, o], T.TC[:, o], AF.Identity, TCR, "yb%d" % k, bias=128.0, scale=1.0 / KC)
            for k in range(4):
                n = min(1040, TW + 16 - 1040 * k)
                dma("G", T.yb[:, 1040 * k:1040 * k + n], T.n128[:, 0:n], "n128 yb%d yb%d" % (2 * k, 2 * k + 1), "yc%d" % k, 800, True)
            YBR += " yc0 yc1 yc2 yc3"
        for s in range(SP):
            TAG[0] = "s%d" % (SP * t + s)
            step(0, t, s)
            if s == SP - 1:
                keys(last)
            step(1, t, s)
        TAG[0] = "h%d" % t
        if not last:
            loadv("S", t + 1)
        lane = T.PX0[:, 0:32]
        mm(acc(lane, lsum(T.ES, T.kr, 0, 512)), "kr ES", "PX00")
        ts(T.klu[:], lane, 1.0 / 16, O.mult, "PX00", "klu")
        tt(T.OH[:], ind(T.X[:], T.klu[:]), T.mrow[:], O.is_equal, "X klu mrow", "OH")
        tt(T.CG[:], ind(T.cf[:], T.klu[:]), T.OH[:], O.mult, "cf klu OH", "CG")
        mm(acc(T.PX0[:, 512:544], lsum(T.ES, T.CG, 0, 512)), "CG ES", "PX01")
        if not last:
            mm(acc(lane, lsum(T.ES, T.kr, 0, 512)), "kr ES", "PX00", True)
            mm(acc(lane, lsum(T.EW, T.OH, 0, 512), False), "OH EW", "PX00")
            cp(T.lnu[:], lane, "PX00", "lnu")
            act(T.MS[:], ind(T["mk%d" % t][:, CS:], T.lnu[:]), AF.Identity, MKR % ((t,) * 4) + " lnu", "MS", bias=-1.0, scale=2.0)
        ts(T.cmu[:], T.PX0[:, 512:544], float(CO), O.add, "PX01", "cmu")
        if last:
            cp(T.Lg[:], ind(T.TL[:, 0:wt], T.cmu[:]), TLR + " cmu", "Lg")
        else:
            tt(T.Lg[:], ind(T.TL[:, 0:wt], T.cmu[:]), T.MS[:], O.mult, TLR + " cmu MS", "Lg")
        send(T["mk%d" % t][:, 0:CAP], T.Lg[:], "L", t, "Lg", 128)
        firsts(0)
        firsts(1)
        wb = slice(wt, wt + B)
        of, od = T.ou[:, 0:16], T.ou[:, 16:32]
        act(sm(5), T.mo[:, 0:16], AF.Relu, "mo0", "nf", scale=2.0 ** 26, bias=-(DU - 2048.5) * 2.0 ** 14)
        tt(sm(5), sm(5), T.cf[:, 0:16], O.add, "nf cf00", "nf")
        ts(T.su[:], sm(5), float(CO), O.add, "nf", "su", float(TW), O.min)
        if last:
            act(T.Cc[:], ind(T.yb[:], T.su[:]), AF.Identity, YBR + " su", "Cc", bias=128.25, scale=0.5)
            tt(T.ab[:], ind(T.yb[:], of), T.nb[:], O.mult, YBR + " ou0 nu", "ab")
            tt(ind(T.yb[:], of), T.ab[:], T.ob[:], O.add, "ab u1 ou0", "yb")
            tt(T.ab[:], ind(T.yb[:], od), T.ob[:], O.add, YBR + " ou1 u1", "ab")
            ts(T.ab[:], T.ab[:], 15.0, O.min, "ab", "ab")
            cp(ind(T.yb[:], od), T.ab[:], "ab ou1", "yb")
            ts(T.yb[:, wb], T.Cc[:], -128.0, O.add, "Cc", "yb")
            for k in range(2):
                o = slice(2048 * k, 2048 * k + 2048)
                dma("SA"[k], T.yn[:, o], T.yb[:, o], YBR, "yn%d" % k, 512 * (k + 1))
        else:
            act(T.TS[:, wb], ind(T.TS[:, 0:wt], cu[:, 0:16]), AF.Copy, TSR + " cu00", "TS")
            act(T.TL[:, wb], ind(T.TL[:, 0:wt], cu[:, 0:16]), AF.Copy, TLR + " cu00", "TL")
            mm(spread(T.PL0, 768, 256, T.c16[:], 16, True), "c16 Dn", "PL01.c PL01.a PL01.v")
            act(T.TS[:, TW + wt:TW + wt + B], T.PL0[:, 768:1024], AF.Copy, "PL01.c PL01.a PL01.v cl7", "TSF", scale=T.cols[:, 7:8])
            act(T.PL1[:, 256:512], T.nu[:], AF.Identity, "nu", "PL10.c PL10.a PL10.v", bias=-127.0 - 1.0 / KC, scale=-1.0)
            act(T.Cc[:], ind(T.TC[:], T.su[:]), AF.Identity, TCR + " su", "Cc", bias=128.26, scale=0.5 / KC)
            tt(T.aC[:], ind(T.TC[:], of), T.nu[:], O.mult, TCR + " ou0 nu", "aC")
            tt(ind(T.TC[:], of), T.aC[:], T.u1[:], O.add, "aC u1 ou0", "TC")
            act(T.Cb[:], ind(T.TC[:], od), AF.Identity, TCR + " ou1", "Cb", bias=128.0, scale=1.0 / KC)
            act(T.aF[:], T.Cc[:], AF.Relu, "Cc", "aF", bias=D - 1.0 - 128.0 * KC, scale=KC)
            act(T.TC[:, wb], T.aF[:], AF.Identity, "aF", "TC", bias=-D)
            tt(T.aC[:], T.Cb[:], T.PL1[:, 256:512], O.add, "Cb PL10.c PL10.a PL10.v", "aC")
            ts(T.aC[:], T.aC[:], 15.0 - 1.0 / KC, O.min, "aC", "aC", KC, O.mult)
            tt(ind(T.TC[:], od), T.aC[:], T.nD[:], O.max, "aC nD ou1", "TC")
            tt(T.Yf[:], ind(T.TS[:, 0:TW], of), T.s[:, 0:256], O.mult, TSR + " ou0 s00", "Yf")
            mm(acc(T.PL0[:, 256:512], [(m_(ID), T.wn[:, B * t:B * t + B]), (m_(NB), T.Yf[:])]), "ID NB Yf wr%d" % t, "PL00.c PL00.a PL00.v")
            act(T.aD[:], ind(T.TS[:, 0:TW], of), AF.Copy, TSR + " ou0", "aD")
            tt(T.PL0[:, 256:512], T.PL0[:, 256:512], T.dsg[:], O.mult, "PL00.c PL00.a PL00.v dsg", "PL00.c PL00.a PL00.v")
            tt(T.aE[:], T.aD[:], T.PL0[:, 256:512], O.add, "PL00.c PL00.a PL00.v aD", "aE")
            act(T.r2[:], T.aE[:], AF.Identity, "aE", "r2", bias=R12)
            act(T.aD[:], T.r2[:], AF.Identity, "r2", "aD", bias=-R12)
            tt(ind(T.TS[:, 0:TW], of), T.aE[:], T.aD[:], O.subtract, "aE aD ou0", "TS")
            for h in (0, 1):
                for s in range(SP):
                    vlist(h, s)
        tt(T.tot[:, 1:2], T.tot[:, 0:1], T.lT[:, 8 * t:8 * t + 1], O.min, "tot lT%d" % t, "tm1")
        ts(T.tot[:, 2:3], T.tot[:, 1:2], CAP - 2047.5, O.min, "tm1", "tm2", -400.0, O.mult)
        act(T.nmv[:], T.X[:], AF.Sigmoid, "X tm2", "nmv", bias=T.tot[:, 2:3], scale=400.0)
        act(T.X16[:], T.X[:], AF.Copy, "X", "X16")
        slot = T.PX0[:, 640:768]
        mm(acc(slot, [(m_(ID), T.X16[:]), (m_(P4), T.nmv[:])]), "ID P4 X16 nmv", "PX01")
        ts(T.hu[:], slot, 2047.0, O.add, "PX01", "hu", float(CAP), O.min)
        tt(T.cm[:], T.cf[:], T.nmv[:], O.mult, "cf nmv", "cm")
        if not last:
            tt(T.so[:], slot, T.Dm[:], O.min, "PX01 Dm", "so")
            ts(T.mu[:], T.so[:], 2047.0, O.add, "so", "mu")
            act(sm(1), T.nmv[:, 0:16], AF.Identity, "nmv", "val", scale=65536.0, bias=-65536.0)
            tt(sm(0), sm(0), sm(1), O.add, "F val", "F")
        for h in (0, 1):
            for b in (0, 1):
                win = ind(T["mk%d" % t][:, 0:CS], T.hu[:, OB(h, b)])
                if last and b:
                    cp(T.H[:, HB(h, b)], win, "hu lz%d lL%d" % (t, t), K("H@#", h, b))
                else:
                    act(T.H[:, HB(h, b)], win, AF.Abs, "hu lz%d lL%d" % (t, t), K("H@#", h, b))
            for bs in UNITS:
                u, N, oc, pr = unit(h, bs)
                y, yn = PL[h][:, 512 * bs[0] + 192:512 * bs[0] + 192 + 32 * len(bs)], K("PL@#.y", h, bs[0])
                mm(acc(y, [(m_(ID), T.cm[:, oc])] + lsum(T.ES, T.H, 16 * oc.start, 16 * oc.stop)), "ID cm ES " + N("H"), yn)
                if last:
                    ts(T.cf[:, oc], y, -79.0, O.add, yn, N("cf"))
                else:
                    ts(T.cr[:, oc], y, -79.0 - CO - R12, O.add, yn, N("cr"))
                    newc(h, bs)
            if not last:
                for b in (0, 1):
                    win, r, w = ind(T["mk%d" % t][:], T.mu[:, OB(h, b)]), MKR % ((t,) * 4) + " mu lz%d lL%d" % (t, t), K("mk%d@#" % ((t + 1) % 2), h, b)
                    if (h, b) in MKV:
                        ts(marks(t + 1, h, b), win, 0.5, O.is_gt, r, w)
                    else:
                        act(marks(t + 1, h, b), win, AF.Sigmoid, r, w, bias=-200.0, scale=400.0)
        if last:
            dma("A", T.yc[:, :], T.cf[:], "cf", "yc", 64)
    issue()
